import numpy as np
import ml_dtypes


def mxq(x, axis, fmt="e4m3"):
    dtype, down = {"e4m3": (ml_dtypes.float8_e4m3fn, 7), "e5m2": (ml_dtypes.float8_e5m2, 14)}[fmt]
    v = np.moveaxis(np.asarray(x, np.float32).astype(ml_dtypes.bfloat16).astype(np.float64), axis, -1)
    blocks = v.reshape(v.shape[:-1] + (-1, 32))
    amax = np.abs(blocks).max(-1, keepdims=True)
    byte = np.maximum(np.where(amax > 0, np.frexp(amax)[1] - 1 + 127, 0) - down, 1)
    scale = np.exp2(byte - 127.0)
    codes = (blocks / scale).astype(np.float32).astype(dtype).astype(np.float64)
    return np.moveaxis((codes * scale).reshape(v.shape), -1, axis)


WIDE = False


def mx_kscale(k):
    if not WIDE:
        return np.ones(k)
    levels = np.array([18, -18])
    if k % 512:
        return np.exp2(np.random.permutation(np.resize(levels, k // 32))).repeat(32)
    a = np.empty((k // 512, 16))
    for p in range(k // 512):
        a[p, :8] = np.random.permutation(np.resize(levels, 8))
        for g in range(8):
            far = levels[np.abs(levels - a[p, g]) >= 10]
            a[p, g + 8] = far[np.random.randint(len(far))]
    return np.exp2(a.ravel()).repeat(32)


def f64(x):
    return np.asarray(x).astype(np.float64)


def striped(idx):
    return np.tile(np.asarray(idx).reshape(-1, 16).T, (8, 1)).astype(np.uint16)


def unstriped(offs):
    return offs[:16].T.reshape(-1).astype(np.int64)


E2M1 = np.array([0.0, 0.5, 1.0, 1.5, 2.0, 3.0, 4.0, 6.0, -0.0, -0.5, -1.0, -1.5, -2.0, -3.0, -4.0, -6.0])


def pack_weight(w, fmt):
    k, n = w.shape
    w = f64(np.asarray(w, np.float32).astype(ml_dtypes.bfloat16)).reshape(k // 32, 32, n)
    amax = np.abs(w).max(1)
    if fmt == "e4m3":
        byte = np.frexp(amax)[1] - 1 + 127 - 7
    else:
        mant, ex = np.frexp(amax / 6.0)
        byte = np.where(mant > 0.5, ex, ex - 1) + 127
    byte = np.clip(np.where(amax > 0, byte, 1), 1, 254)
    scaled = (w * np.exp2(127.0 - byte)[:, None, :]).reshape(k, n).astype(np.float32)
    by_word = np.ascontiguousarray(scaled.reshape(k // 512, 128, 4, n).transpose(0, 1, 3, 2))
    if fmt == "e4m3":
        words = by_word.astype(ml_dtypes.float8_e4m3fn).view(np.uint8)
    else:
        c = by_word.astype(ml_dtypes.float4_e2m1fn).view(np.uint8) & 0xF
        words = (c[..., 0::2] | (c[..., 1::2] << 4)).reshape(k // 512, 128, 2 * n)
    return np.ascontiguousarray(words), np.ascontiguousarray(byte.astype(np.uint8).reshape(k // 512, 16, n))


def unpack_weight(words, scales, fmt):
    g, _, n = scales.shape
    words = np.ascontiguousarray(words).reshape(g, 128, n, -1)
    if fmt == "e4m3":
        vals = words.view(ml_dtypes.float8_e4m3fn).astype(np.float64)
    else:
        nib = np.empty((g, 128, n, 4), np.uint8)
        nib[..., 0::2] = words & 0xF
        nib[..., 1::2] = words >> 4
        vals = E2M1[nib]
    vals = vals * np.repeat(np.exp2(scales.astype(np.float64) - 127.0), 8, axis=1)[..., None]
    return vals.transpose(0, 1, 3, 2).reshape(g * 512, n)


B, N, T, D, R = 1, 512, 2048, 1024, 512


def setup_inputs():
    n = np.random.standard_normal
    idx = np.random.permutation(T)[:B * N]
    s = mx_kscale(D)[:, None]
    z = mx_kscale(R)[:, None]
    x = n((B, D, R))
    teach = np.exp(n((B, R, N)))
    teach = teach / teach.sum(-1, keepdims=True)
    wp = pack_weight(n((D, T)) * (0.50 / np.sqrt(D)) / s, "e2m1")
    return {
        "xT": (x * s).astype(np.float32),
        "w_words": np.ascontiguousarray(wp[0].reshape(1, 2, 128, T, 2).transpose(0, 2, 3, 1, 4)).reshape(1, 128, T, 4),
        "w_scales": wp[1],
        "y": teach.astype(np.float32),
        "lse": (np.log(N) + 0.12 + 0.1 * n((B, R, 1))).astype(np.float32),
        "wt": (np.random.uniform(0.5, 1.5, (B, R, 1)) * N / np.sqrt(R) * z).astype(np.float32),
        "xm": (x.transpose(0, 2, 1) / z).astype(np.float32),
        "offs": striped(idx),
    }


def reference(xT, w_words, w_scales, y, lse, wt, xm, offs):
    idx = unstriped(offs)
    w = unpack_weight(w_words.reshape(1, 128, T, 2, 2).transpose(0, 3, 1, 2, 4).reshape(2, 128, 2 * T), w_scales, "e2m1")
    pick = lambda x: x[:, idx].reshape(x.shape[0], B, N).transpose(1, 0, 2)
    a = mxq(f64(xT), 1, "e4m3").transpose(0, 2, 1) @ pick(w)
    g = f64(wt) * (np.exp(a - f64(lse)) - f64(y))
    dw = mxq(f64(xm), 1, "e4m3").transpose(0, 2, 1) @ mxq(g, 1, "e5m2")
    gw = np.zeros((D, T))
    gw[:, idx] = dw.transpose(1, 0, 2).reshape(D, B * N)
    return gw

@@ -1,0 +1,192 @@
+from contextlib import ExitStack
+
+import concourse.mybir as mybir
+
+N, T, D, R = 512, 2048, 1024, 512
+P = 128
+PACK = 4
+PASSES = D // (P * PACK)
+BLOCKS = D // P
+HALF = N // 2
+FLOPS = 2 * 2 * R * D * N
+
+F32 = mybir.dt.float32
+BF16 = mybir.dt.bfloat16
+I32 = mybir.dt.int32
+U32 = mybir.dt.uint32
+U16 = mybir.dt.uint16
+U8 = mybir.dt.uint8
+E4M3 = mybir.dt.float8_e4m3fn_x4
+E5M2 = mybir.dt.float8_e5m2_x4
+E2M1 = mybir.dt.float4_e2m1fn_x4
+ACT = mybir.ActivationFunctionType
+ALU = mybir.AluOpType
+
+VECTOR_SHARE = (24, 68)
+XM_CHUNKS = ((0, 1, "xT0"), (1, 4, "xT1"), (4, 8, "word_window"))
+
+
+def tile_attend_glse_w_kernel(tc, xT, w_words, w_scales, y, lse, wt, xm, offs, out):
+    nc = tc.nc
+    with ExitStack() as ctx:
+        keep = ctx.enter_context(tc.tile_pool(name="keep", bufs=1))
+        ring = ctx.enter_context(tc.tile_pool(name="ring", bufs=3))
+        psum = ctx.enter_context(tc.psum_pool(name="psum", bufs=1))
+
+        offsets = keep.tile([P, N // 16], U16, name="offsets")
+        nc.sync.dma_start(offsets[:], offs)
+        word_window = keep.tile([P, T], U32, name="word_window", tag="word_window")
+        nc.sync.dma_start(word_window[:].bitcast(I32), w_words[0].rearrange("p n b -> p (n b)").bitcast(I32))
+        scale_window = keep.tile([P, PASSES * T], U8, name="scale_window", tag="scale_window")
+        nc.vector.memset(scale_window[:].bitcast(I32), 0)
+        for q in range(4):
+            nc.scalar.dma_start(
+                scale_window[32 * q : 32 * q + 4, :].bitcast(I32).rearrange("f (o t) -> f o t", o=PASSES),
+                w_scales[:, 4 * q : 4 * q + 4, :].rearrange("o f t -> f o t").bitcast(I32),
+            )
+        windows = []
+        for i in range(2):
+            win = keep.tile([P, T], F32, name=f"out_window{i}")
+            nc.vector.memset(win[:], 0.0)
+            windows.append(win)
+        warm = keep.tile([P, PACK], F32, name="warm", tag="xT1")
+        nc.scalar.activation(warm[:], windows[0][:, :PACK], ACT.Exp)
+        x_raw = []
+        for o in range(PASSES):
+            raw = keep.tile([P, PACK, R], F32, name=f"x_raw{o}", tag=f"xT{o}")
+            nc.sync.dma_start(raw[:], xT[0, o * 512 : (o + 1) * 512, :].rearrange("(p j) r -> p j r", j=PACK))
+            x_raw.append(raw)
+        lse_sb = keep.tile([P, PACK], F32, name="lse_sb")
+        wt_sb = keep.tile([P, PACK], F32, name="wt_sb")
+        nc.gpsimd.dma_start(lse_sb[:], lse[0].rearrange("(p j) o -> p (j o)", j=PACK))
+        nc.gpsimd.dma_start(wt_sb[:], wt[0].rearrange("(p j) o -> p (j o)", j=PACK))
+        neg_lse = keep.tile([P, PACK], F32, name="neg_lse")
+        nc.gpsimd.tensor_scalar(neg_lse[:], lse_sb[:], -1.0, 0.0, ALU.mult, ALU.add)
+
+        w_pairs = keep.tile([P, N], U32, name="w_pairs", tag="w_pairs")
+        nc.vector.tensor_copy(w_pairs[:], word_window[:].indirect(offsets[:]))
+        w_codes = keep.tile([P, PASSES, N], U16, name="w_codes", align_bytes=64)
+        nc.vector.tensor_copy(w_codes[:], w_pairs[:].bitcast(U16).rearrange("p (s o) -> p o s", o=PASSES))
+        w_planes = []
+        for o in range(PASSES):
+            plane = keep.tile([P, N], U8, name=f"w_plane{o}", align_bytes=64)
+            nc.vector.tensor_copy(plane[:], scale_window[:, o * T : (o + 1) * T].indirect(offsets[:]))
+            w_planes.append(plane)
+
+        y_rows = y[0].rearrange("(p j) s -> p j s", j=PACK)
+        y_sb = []
+        for u, tag in enumerate(("word_window", "w_pairs")):
+            y_pair = keep.tile([P, 2, N], F32, name=f"y_pair{u}", tag=tag)
+            nc.sync.dma_start(y_pair[:], y_rows[:, 2 * u : 2 * u + 2, :])
+            y_sb.append(y_pair)
+
+        x_codes, x_planes = [], []
+        for o in range(PASSES):
+            grouped = keep.tile([P, R * PACK], BF16, name=f"x_grouped{o}", align_bytes=64)
+            dst = grouped[:].rearrange("p (t m j) -> p m j t", t=PACK, j=PACK)
+            src = x_raw[o][:].rearrange("p j (m t) -> p m j t", t=PACK)
+            share = VECTOR_SHARE[o]
+            nc.vector.tensor_copy(dst[:, :share], src[:, :share])
+            nc.scalar.copy(dst[:, share:], src[:, share:])
+            codes = keep.tile([P, R], U32, name=f"x_codes{o}", align_bytes=64)
+            plane = keep.tile([P, R], U8, name=f"x_plane{o}", align_bytes=64)
+            width = R if o == 0 else P
+            for c in range(0, R, width):
+                nc.vector.quantize_mx(
+                    out=codes[:, c : c + width].bitcast(E4M3),
+                    scales=plane[:, c : c + width],
+                    in_=grouped[:, PACK * c : PACK * (c + width)],
+                )
+            x_codes.append(codes)
+            x_planes.append(plane)
+
+        scores = [psum.tile([P, N], F32, name=f"scores{t}") for t in range(PACK)]
+        for o in range(PASSES):
+            for t in range(PACK):
+                rows = slice(t * P, (t + 1) * P)
+                nc.tensor.matmul_mx(
+                    out=scores[t][:],
+                    lhsT=x_codes[o][:, rows].bitcast(E4M3),
+                    lhsT_scale=x_planes[o][:, rows],
+                    rhs=w_codes[:, o, :].bitcast(E2M1),
+                    rhs_scale=w_planes[o][:],
+                    start=(o == 0),
+                    stop=(o == PASSES - 1),
+                )
+
+        y_wt = keep.tile([P, PACK, N], F32, name="y_wt")
+        nc.scalar.activation(y_wt[:, 0, :], y_sb[0][:, 0, :], ACT.Copy, scale=wt_sb[:, 0:1])
+        for t in range(1, PACK):
+            nc.vector.tensor_scalar(y_wt[:, t, :], y_sb[t // 2][:, t % 2, :], wt_sb[:, t : t + 1], None, ALU.mult)
+
+        probs = keep.tile([P, PACK, N], F32, name="probs")
+        for t, h in ((0, 0), (0, 1), (1, 0), (1, 1), (2, 0), (3, 0), (2, 1), (3, 1)):
+            cols = slice(h * HALF, (h + 1) * HALF)
+            nc.scalar.activation(probs[:, t, cols], scores[t][:, cols], ACT.Exp, bias=neg_lse[:, t : t + 1])
+
+        g_codes = keep.tile([P, N], U32, name="g_codes", align_bytes=64)
+        g_plane = keep.tile([P, N], U8, name="g_plane", align_bytes=64)
+        g_rows = [keep.tile([P, PACK, HALF], BF16, name=f"g_rows{h}") for h in range(2)]
+        for h in range(2):
+            cols = slice(h * HALF, (h + 1) * HALF)
+            for t in range(PACK):
+                nc.vector.scalar_tensor_tensor(
+                    g_rows[h][:, t, :], probs[:, t, cols], wt_sb[:, t : t + 1], y_wt[:, t, cols], ALU.mult, ALU.subtract
+                )
+        g_grouped = []
+        for h, copy in enumerate((nc.scalar.copy, nc.vector.tensor_copy)):
+            grouped = keep.tile([P, HALF * PACK], BF16, name=f"g_grouped{h}", tag=f"g_grouped{h}", align_bytes=64)
+            copy(
+                grouped[:].rearrange("p (c i t) -> p c t i", i=4, t=PACK),
+                g_rows[h][:].rearrange("p t (c i) -> p c t i", i=4),
+            )
+            g_grouped.append(grouped)
+        for h in (1, 0):
+            cols = slice(h * HALF, (h + 1) * HALF)
+            nc.vector.quantize_mx(out=g_codes[:, cols].bitcast(E5M2), scales=g_plane[:, cols], in_=g_grouped[h][:])
+
+        xm_rows = xm[0].rearrange("(p j) d -> p j d", j=PACK)
+        xm_codes = keep.tile([P, D], U32, name="xm_codes", align_bytes=64)
+        xm_plane = keep.tile([P, D], U8, name="xm_plane", align_bytes=64)
+        xm_grouped = keep.tile([P, D * PACK], BF16, name="xm_grouped", align_bytes=64)
+
+        def load_xm(first, last, tag):
+            raw = keep.tile([P, PACK, (last - first) * P], F32, name=f"xm_raw{first}", tag=tag)
+            nc.sync.dma_start(raw[:], xm_rows[:, :, first * P : last * P])
+            return raw
+
+        def quantise_xm(raw, first, b):
+            nc.scalar.copy(
+                xm_grouped[:, b * P * PACK : (b + 1) * P * PACK].rearrange("p (c i j) -> p c j i", i=4, j=PACK),
+                raw[:, :, (b - first) * P : (b - first + 1) * P].rearrange("p j (c i) -> p c j i", i=4),
+            )
+            nc.vector.quantize_mx(
+                out=xm_codes[:, b * P : (b + 1) * P].bitcast(E4M3),
+                scales=xm_plane[:, b * P : (b + 1) * P],
+                in_=xm_grouped[:, b * P * PACK : (b + 1) * P * PACK],
+            )
+
+        for first, last, tag in XM_CHUNKS:
+            raw = load_xm(first, last, tag)
+            for b in range(first, last):
+                quantise_xm(raw, first, b)
+                if b == 0:
+                    win = keep.tile([P, T], F32, name="out_window2", tag="g_grouped0", align_bytes=64)
+                    nc.vector.memset(win[:], 0.0)
+                    windows.append(win)
+                cols = slice(b * P, (b + 1) * P)
+                grad = psum.tile([P, N], F32, name="grad", bufs=4)
+                nc.tensor.matmul_mx(
+                    out=grad[:],
+                    lhsT=xm_codes[:, cols].bitcast(E4M3),
+                    lhsT_scale=xm_plane[:, cols],
+                    rhs=g_codes[:].bitcast(E5M2),
+                    rhs_scale=g_plane[:],
+                    start=True,
+                    stop=True,
+                )
+                dense = ring.tile([P, N], F32, name="dense")
+                nc.scalar.copy(dense[:], grad[:])
+                win = windows[b % len(windows)]
+                nc.vector.tensor_copy(win[:].indirect(offsets[:]), dense[:])
+                nc.sync.dma_start(out[cols, :], win[:])

@@ -22,8 +22,8 @@ E2M1 = mybir.dt.float4_e2m1fn_x4
 ACT = mybir.ActivationFunctionType
 ALU = mybir.AluOpType
 
-VECTOR_SHARE = (24, 68)
-XM_CHUNKS = ((0, 1, "xT0"), (1, 4, "xT1"), (4, 8, "word_window"))
+VECTOR_SHARE = (64, 84)
+XM_CHUNKS = ((0, 2, "word_window"), (2, 4, "xT0"), (4, 8, "xT1"))
 
 
 def tile_attend_glse_w_kernel(tc, xT, w_words, w_scales, y, lse, wt, xm, offs, out):
@@ -37,20 +37,19 @@ def tile_attend_glse_w_kernel(tc, xT, w_words, w_scales, y, lse, wt, xm, offs, o
         nc.sync.dma_start(offsets[:], offs)
         word_window = keep.tile([P, T], U32, name="word_window", tag="word_window")
         nc.sync.dma_start(word_window[:].bitcast(I32), w_words[0].rearrange("p n b -> p (n b)").bitcast(I32))
-        scale_window = keep.tile([P, PASSES * T], U8, name="scale_window", tag="scale_window")
+        scale_window = keep.tile([P, T], U8, name="scale_window", tag="scale_window")
         nc.vector.memset(scale_window[:].bitcast(I32), 0)
         for q in range(4):
-            nc.scalar.dma_start(
-                scale_window[32 * q : 32 * q + 4, :].bitcast(I32).rearrange("f (o t) -> f o t", o=PASSES),
-                w_scales[:, 4 * q : 4 * q + 4, :].rearrange("o f t -> f o t").bitcast(I32),
+            nc.sync.dma_start(
+                scale_window[32 * q : 32 * q + 8, :].bitcast(I32),
+                w_scales[:, 4 * q : 4 * q + 4, :].bitcast(I32),
             )
-        windows = []
-        for i in range(2):
-            win = keep.tile([P, T], F32, name=f"out_window{i}")
-            nc.vector.memset(win[:], 0.0)
-            windows.append(win)
-        warm = keep.tile([P, PACK], F32, name="warm", tag="xT1")
-        nc.scalar.activation(warm[:], windows[0][:, :PACK], ACT.Exp)
+        windows = [keep.tile([P, T], F32, name="out_window0")]
+        nc.vector.memset(windows[0][:].bitcast(I32), 0)
+        warm_in = keep.tile([P, PACK], F32, name="warm_in", tag="xT1")
+        nc.gpsimd.memset(warm_in[:], 0.0)
+        warm = keep.tile([P, PACK], F32, name="warm", tag="xT0")
+        nc.scalar.activation(warm[:], warm_in[:], ACT.Exp)
         x_raw = []
         for o in range(PASSES):
             raw = keep.tile([P, PACK, R], F32, name=f"x_raw{o}", tag=f"xT{o}")
@@ -60,25 +59,27 @@ def tile_attend_glse_w_kernel(tc, xT, w_words, w_scales, y, lse, wt, xm, offs, o
         wt_sb = keep.tile([P, PACK], F32, name="wt_sb")
         nc.gpsimd.dma_start(lse_sb[:], lse[0].rearrange("(p j) o -> p (j o)", j=PACK))
         nc.gpsimd.dma_start(wt_sb[:], wt[0].rearrange("(p j) o -> p (j o)", j=PACK))
-        neg_lse = keep.tile([P, PACK], F32, name="neg_lse")
+        neg_lse = keep.tile([P, PACK], F32, name="neg_lse", tag="neg_lse", align_bytes=64)
         nc.gpsimd.tensor_scalar(neg_lse[:], lse_sb[:], -1.0, 0.0, ALU.mult, ALU.add)
 
+        both_planes = keep.tile([P, N], U8, name="both_planes", align_bytes=64)
+        nc.vector.tensor_copy(both_planes[:], scale_window[:].indirect(offsets[:]))
+        second_plane = keep.tile([P, N], U8, name="second_plane", align_bytes=64)
+        for q in range(4):
+            nc.sync.dma_start(
+                second_plane[32 * q : 32 * q + 4, :].bitcast(I32),
+                both_planes[32 * q + 4 : 32 * q + 8, :].bitcast(I32),
+            )
+        w_planes = [both_planes, second_plane]
         w_pairs = keep.tile([P, N], U32, name="w_pairs", tag="w_pairs")
         nc.vector.tensor_copy(w_pairs[:], word_window[:].indirect(offsets[:]))
         w_codes = keep.tile([P, PASSES, N], U16, name="w_codes", align_bytes=64)
         nc.vector.tensor_copy(w_codes[:], w_pairs[:].bitcast(U16).rearrange("p (s o) -> p o s", o=PASSES))
-        w_planes = []
-        for o in range(PASSES):
-            plane = keep.tile([P, N], U8, name=f"w_plane{o}", align_bytes=64)
-            nc.vector.tensor_copy(plane[:], scale_window[:, o * T : (o + 1) * T].indirect(offsets[:]))
-            w_planes.append(plane)
 
         y_rows = y[0].rearrange("(p j) s -> p j s", j=PACK)
-        y_sb = []
-        for u, tag in enumerate(("word_window", "w_pairs")):
-            y_pair = keep.tile([P, 2, N], F32, name=f"y_pair{u}", tag=tag)
-            nc.sync.dma_start(y_pair[:], y_rows[:, 2 * u : 2 * u + 2, :])
-            y_sb.append(y_pair)
+        y_sb = keep.tile([P, PACK, N], F32, name="y_sb", tag="scale_window")
+        for u in range(2):
+            nc.sync.dma_start(y_sb[:, 2 * u : 2 * u + 2, :], y_rows[:, 2 * u : 2 * u + 2, :])
 
         x_codes, x_planes = [], []
         for o in range(PASSES):
@@ -90,7 +91,7 @@ def tile_attend_glse_w_kernel(tc, xT, w_words, w_scales, y, lse, wt, xm, offs, o
             nc.scalar.copy(dst[:, share:], src[:, share:])
             codes = keep.tile([P, R], U32, name=f"x_codes{o}", align_bytes=64)
             plane = keep.tile([P, R], U8, name=f"x_plane{o}", align_bytes=64)
-            width = R if o == 0 else P
+            width = P
             for c in range(0, R, width):
                 nc.vector.quantize_mx(
                     out=codes[:, c : c + width].bitcast(E4M3),
@@ -115,30 +116,26 @@ def tile_attend_glse_w_kernel(tc, xT, w_words, w_scales, y, lse, wt, xm, offs, o
                 )
 
         y_wt = keep.tile([P, PACK, N], F32, name="y_wt")
-        nc.scalar.activation(y_wt[:, 0, :], y_sb[0][:, 0, :], ACT.Copy, scale=wt_sb[:, 0:1])
+        nc.scalar.activation(y_wt[:, 0, :], y_sb[:, 0, :], ACT.Copy, scale=wt_sb[:, 0:1])
         for t in range(1, PACK):
-            nc.vector.tensor_scalar(y_wt[:, t, :], y_sb[t // 2][:, t % 2, :], wt_sb[:, t : t + 1], None, ALU.mult)
+            nc.vector.tensor_scalar(y_wt[:, t, :], y_sb[:, t, :], wt_sb[:, t : t + 1], None, ALU.mult)
 
         probs = keep.tile([P, PACK, N], F32, name="probs")
-        for t, h in ((0, 0), (0, 1), (1, 0), (1, 1), (2, 0), (3, 0), (2, 1), (3, 1)):
-            cols = slice(h * HALF, (h + 1) * HALF)
+        g_rows = keep.tile([P, PACK, N], BF16, name="g_rows")
+        pieces = [(t, slice(0, N)) for t in range(PACK - 1)] + [(PACK - 1, slice(0, HALF)), (PACK - 1, slice(HALF, N))]
+        for t, cols in pieces:
             nc.scalar.activation(probs[:, t, cols], scores[t][:, cols], ACT.Exp, bias=neg_lse[:, t : t + 1])
-
+            nc.vector.scalar_tensor_tensor(
+                g_rows[:, t, cols], probs[:, t, cols], wt_sb[:, t : t + 1], y_wt[:, t, cols], ALU.mult, ALU.subtract
+            )
         g_codes = keep.tile([P, N], U32, name="g_codes", align_bytes=64)
         g_plane = keep.tile([P, N], U8, name="g_plane", align_bytes=64)
-        g_rows = [keep.tile([P, PACK, HALF], BF16, name=f"g_rows{h}") for h in range(2)]
-        for h in range(2):
-            cols = slice(h * HALF, (h + 1) * HALF)
-            for t in range(PACK):
-                nc.vector.scalar_tensor_tensor(
-                    g_rows[h][:, t, :], probs[:, t, cols], wt_sb[:, t : t + 1], y_wt[:, t, cols], ALU.mult, ALU.subtract
-                )
         g_grouped = []
         for h, copy in enumerate((nc.scalar.copy, nc.vector.tensor_copy)):
             grouped = keep.tile([P, HALF * PACK], BF16, name=f"g_grouped{h}", tag=f"g_grouped{h}", align_bytes=64)
             copy(
                 grouped[:].rearrange("p (c i t) -> p c t i", i=4, t=PACK),
-                g_rows[h][:].rearrange("p t (c i) -> p c t i", i=4),
+                g_rows[:, :, h * HALF : (h + 1) * HALF].rearrange("p t (c i) -> p c t i", i=4),
             )
             g_grouped.append(grouped)
         for h in (1, 0):
@@ -148,45 +145,60 @@ def tile_attend_glse_w_kernel(tc, xT, w_words, w_scales, y, lse, wt, xm, offs, o
         xm_rows = xm[0].rearrange("(p j) d -> p j d", j=PACK)
         xm_codes = keep.tile([P, D], U32, name="xm_codes", align_bytes=64)
         xm_plane = keep.tile([P, D], U8, name="xm_plane", align_bytes=64)
-        xm_grouped = keep.tile([P, D * PACK], BF16, name="xm_grouped", align_bytes=64)
+        xm_grouped = keep.tile([P, D * PACK], BF16, name="xm_grouped", tag="neg_lse", align_bytes=64)
 
         def load_xm(first, last, tag):
             raw = keep.tile([P, PACK, (last - first) * P], F32, name=f"xm_raw{first}", tag=tag)
             nc.sync.dma_start(raw[:], xm_rows[:, :, first * P : last * P])
             return raw
 
-        def quantise_xm(raw, first, b):
+        def cast_xm(raw, first, b):
             nc.scalar.copy(
                 xm_grouped[:, b * P * PACK : (b + 1) * P * PACK].rearrange("p (c i j) -> p c j i", i=4, j=PACK),
                 raw[:, :, (b - first) * P : (b - first + 1) * P].rearrange("p j (c i) -> p c j i", i=4),
             )
+
+        def quantise_xm(first, last):
             nc.vector.quantize_mx(
-                out=xm_codes[:, b * P : (b + 1) * P].bitcast(E4M3),
-                scales=xm_plane[:, b * P : (b + 1) * P],
-                in_=xm_grouped[:, b * P * PACK : (b + 1) * P * PACK],
+                out=xm_codes[:, first * P : last * P].bitcast(E4M3),
+                scales=xm_plane[:, first * P : last * P],
+                in_=xm_grouped[:, first * P * PACK : last * P * PACK],
             )
 
+        second = keep.tile([P, T], F32, name="out_window1", tag="g_grouped0", align_bytes=64)
+        nc.vector.memset(second[:].bitcast(I32), 0)
+        windows.append(second)
+        xm_raw = {}
         for first, last, tag in XM_CHUNKS:
             raw = load_xm(first, last, tag)
             for b in range(first, last):
-                quantise_xm(raw, first, b)
-                if b == 0:
-                    win = keep.tile([P, T], F32, name="out_window2", tag="g_grouped0", align_bytes=64)
-                    nc.vector.memset(win[:], 0.0)
-                    windows.append(win)
-                cols = slice(b * P, (b + 1) * P)
-                grad = psum.tile([P, N], F32, name="grad", bufs=4)
-                nc.tensor.matmul_mx(
-                    out=grad[:],
-                    lhsT=xm_codes[:, cols].bitcast(E4M3),
-                    lhsT_scale=xm_plane[:, cols],
-                    rhs=g_codes[:].bitcast(E5M2),
-                    rhs_scale=g_plane[:],
-                    start=True,
-                    stop=True,
-                )
+                xm_raw[b] = (raw, first)
+        quantise_before = {0: ((0, 1), (1, 2)), 1: ((2, 4),), 2: ((4, 8),)}
+        for b in range(BLOCKS):
+            for first, last in quantise_before.get(b, ()):
+                for c in range(first, last):
+                    cast_xm(*xm_raw[c], c)
+                quantise_xm(first, last)
+            cols = slice(b * P, (b + 1) * P)
+            grad = psum.tile([P, N], F32, name="grad", bufs=4)
+            nc.tensor.matmul_mx(
+                out=grad[:],
+                lhsT=xm_codes[:, cols].bitcast(E4M3),
+                lhsT_scale=xm_plane[:, cols],
+                rhs=g_codes[:].bitcast(E5M2),
+                rhs_scale=g_plane[:],
+                start=True,
+                stop=True,
+            )
+            if b == 0:
+                dense = keep.tile([P, N], F32, name="first_dense", tag="first_dense")
+            else:
                 dense = ring.tile([P, N], F32, name="dense")
-                nc.scalar.copy(dense[:], grad[:])
-                win = windows[b % len(windows)]
-                nc.vector.tensor_copy(win[:].indirect(offsets[:]), dense[:])
-                nc.sync.dma_start(out[cols, :], win[:])
+            nc.scalar.copy(dense[:], grad[:])
+            win = windows[b % 3]
+            nc.vector.tensor_copy(win[:].indirect(offsets[:]), dense[:])
+            nc.sync.dma_start(out[cols, :], win[:])
+            if b == 0:
+                third = keep.tile([P, T], F32, name="out_window2", tag="first_dense")
+                nc.gpsimd.memset(third[:], 0.0)
+                windows.append(third)

@@ -23,7 +23,7 @@ ACT = mybir.ActivationFunctionType
 ALU = mybir.AluOpType
 
 VECTOR_SHARE = (64, 84)
-XM_CHUNKS = ((0, 2, "word_window"), (2, 4, "xT0"), (4, 8, "xT1"))
+XM_CHUNKS = ((0, 1, "word_window"), (1, 4, "xT0"), (4, 8, "xT1"))
 
 
 def tile_attend_glse_w_kernel(tc, xT, w_words, w_scales, y, lse, wt, xm, offs, out):
@@ -38,17 +38,24 @@ def tile_attend_glse_w_kernel(tc, xT, w_words, w_scales, y, lse, wt, xm, offs, o
         word_window = keep.tile([P, T], U32, name="word_window", tag="word_window")
         nc.sync.dma_start(word_window[:].bitcast(I32), w_words[0].rearrange("p n b -> p (n b)").bitcast(I32))
         scale_window = keep.tile([P, T], U8, name="scale_window", tag="scale_window")
-        nc.vector.memset(scale_window[:].bitcast(I32), 0)
+        nc.gpsimd.memset(scale_window[:].bitcast(I32), 0)
         for q in range(4):
             nc.sync.dma_start(
                 scale_window[32 * q : 32 * q + 8, :].bitcast(I32),
                 w_scales[:, 4 * q : 4 * q + 4, :].bitcast(I32),
             )
-        windows = [keep.tile([P, T], F32, name="out_window0")]
-        nc.vector.memset(windows[0][:].bitcast(I32), 0)
-        warm_in = keep.tile([P, PACK], F32, name="warm_in", tag="xT1")
+        windows = []
+        for i in range(2):
+            win = keep.tile([P, T], F32, name=f"out_window{i}")
+            nc.vector.memset(win[:].bitcast(I32), 0)
+            windows.append(win)
+        g_codes = keep.tile([P, N], U32, name="g_codes", align_bytes=64)
+        g_plane = keep.tile([P, N], U8, name="g_plane", align_bytes=64)
+        nc.gpsimd.memset(g_codes[:, HALF:].bitcast(I32), 0)
+        nc.gpsimd.memset(g_plane[:, HALF:].bitcast(I32), 0)
+        warm_in = keep.tile([P, PACK], F32, name="warm_in")
         nc.gpsimd.memset(warm_in[:], 0.0)
-        warm = keep.tile([P, PACK], F32, name="warm", tag="xT0")
+        warm = keep.tile([P, PACK], F32, name="warm")
         nc.scalar.activation(warm[:], warm_in[:], ACT.Exp)
         x_raw = []
         for o in range(PASSES):
@@ -59,7 +66,7 @@ def tile_attend_glse_w_kernel(tc, xT, w_words, w_scales, y, lse, wt, xm, offs, o
         wt_sb = keep.tile([P, PACK], F32, name="wt_sb")
         nc.gpsimd.dma_start(lse_sb[:], lse[0].rearrange("(p j) o -> p (j o)", j=PACK))
         nc.gpsimd.dma_start(wt_sb[:], wt[0].rearrange("(p j) o -> p (j o)", j=PACK))
-        neg_lse = keep.tile([P, PACK], F32, name="neg_lse", tag="neg_lse", align_bytes=64)
+        neg_lse = keep.tile([P, PACK], F32, name="neg_lse")
         nc.gpsimd.tensor_scalar(neg_lse[:], lse_sb[:], -1.0, 0.0, ALU.mult, ALU.add)
 
         both_planes = keep.tile([P, N], U8, name="both_planes", align_bytes=64)
@@ -78,8 +85,8 @@ def tile_attend_glse_w_kernel(tc, xT, w_words, w_scales, y, lse, wt, xm, offs, o
 
         y_rows = y[0].rearrange("(p j) s -> p j s", j=PACK)
         y_sb = keep.tile([P, PACK, N], F32, name="y_sb", tag="scale_window")
-        for u in range(2):
-            nc.sync.dma_start(y_sb[:, 2 * u : 2 * u + 2, :], y_rows[:, 2 * u : 2 * u + 2, :])
+        for planes in (slice(0, 2), slice(2, 3), slice(3, 4)):
+            nc.sync.dma_start(y_sb[:, planes, :], y_rows[:, planes, :])
 
         x_codes, x_planes = [], []
         for o in range(PASSES):
@@ -120,65 +127,62 @@ def tile_attend_glse_w_kernel(tc, xT, w_words, w_scales, y, lse, wt, xm, offs, o
         for t in range(1, PACK):
             nc.vector.tensor_scalar(y_wt[:, t, :], y_sb[:, t, :], wt_sb[:, t : t + 1], None, ALU.mult)
 
-        probs = keep.tile([P, PACK, N], F32, name="probs")
-        g_rows = keep.tile([P, PACK, N], BF16, name="g_rows")
-        pieces = [(t, slice(0, N)) for t in range(PACK - 1)] + [(PACK - 1, slice(0, HALF)), (PACK - 1, slice(HALF, N))]
-        for t, cols in pieces:
-            nc.scalar.activation(probs[:, t, cols], scores[t][:, cols], ACT.Exp, bias=neg_lse[:, t : t + 1])
-            nc.vector.scalar_tensor_tensor(
-                g_rows[:, t, cols], probs[:, t, cols], wt_sb[:, t : t + 1], y_wt[:, t, cols], ALU.mult, ALU.subtract
-            )
-        g_codes = keep.tile([P, N], U32, name="g_codes", align_bytes=64)
-        g_plane = keep.tile([P, N], U8, name="g_plane", align_bytes=64)
-        g_grouped = []
-        for h, copy in enumerate((nc.scalar.copy, nc.vector.tensor_copy)):
-            grouped = keep.tile([P, HALF * PACK], BF16, name=f"g_grouped{h}", tag=f"g_grouped{h}", align_bytes=64)
-            copy(
-                grouped[:].rearrange("p (c i t) -> p c t i", i=4, t=PACK),
-                g_rows[:, :, h * HALF : (h + 1) * HALF].rearrange("p t (c i) -> p c t i", i=4),
-            )
-            g_grouped.append(grouped)
-        for h in (1, 0):
-            cols = slice(h * HALF, (h + 1) * HALF)
-            nc.vector.quantize_mx(out=g_codes[:, cols].bitcast(E5M2), scales=g_plane[:, cols], in_=g_grouped[h][:])
-
         xm_rows = xm[0].rearrange("(p j) d -> p j d", j=PACK)
-        xm_codes = keep.tile([P, D], U32, name="xm_codes", align_bytes=64)
-        xm_plane = keep.tile([P, D], U8, name="xm_plane", align_bytes=64)
-        xm_grouped = keep.tile([P, D * PACK], BF16, name="xm_grouped", tag="neg_lse", align_bytes=64)
-
-        def load_xm(first, last, tag):
+        xm_raw = {}
+        for first, last, tag in XM_CHUNKS:
             raw = keep.tile([P, PACK, (last - first) * P], F32, name=f"xm_raw{first}", tag=tag)
             nc.sync.dma_start(raw[:], xm_rows[:, :, first * P : last * P])
-            return raw
+            for b in range(first, last):
+                xm_raw[b] = raw[:, :, (b - first) * P : (b - first + 1) * P]
 
-        def cast_xm(raw, first, b):
-            nc.scalar.copy(
-                xm_grouped[:, b * P * PACK : (b + 1) * P * PACK].rearrange("p (c i j) -> p c j i", i=4, j=PACK),
-                raw[:, :, (b - first) * P : (b - first + 1) * P].rearrange("p j (c i) -> p c j i", i=4),
+        halves = [slice(h * HALF, (h + 1) * HALF) for h in range(2)]
+        probs = keep.tile([P, PACK, N], F32, name="probs")
+        g_rows = [keep.tile([P, PACK, HALF], BF16, name=f"g_rows{h}", tag=f"g_rows{h}") for h in range(2)]
+        xm_codes = keep.tile([P, D], U32, name="xm_codes", align_bytes=64)
+        xm_plane = keep.tile([P, D], U8, name="xm_plane", align_bytes=64)
+        xm_grouped = keep.tile([P, D * PACK], BF16, name="xm_grouped", align_bytes=64)
+
+        def exponentiate(h):
+            for t in range(PACK):
+                nc.scalar.activation(
+                    probs[:, t, halves[h]], scores[t][:, halves[h]], ACT.Exp, bias=neg_lse[:, t : t + 1]
+                )
+
+        def form_g(h):
+            for t in range(PACK):
+                nc.vector.scalar_tensor_tensor(
+                    g_rows[h][:, t, :],
+                    probs[:, t, halves[h]],
+                    wt_sb[:, t : t + 1],
+                    y_wt[:, t, halves[h]],
+                    ALU.mult,
+                    ALU.subtract,
+                )
+
+        def interleave_g(h, copy):
+            grouped = keep.tile([P, HALF * PACK], BF16, name=f"g_grouped{h}", align_bytes=64)
+            copy(
+                grouped[:].rearrange("p (c i t) -> p c t i", i=4, t=PACK),
+                g_rows[h][:].rearrange("p t (c i) -> p c t i", i=4),
             )
+            return grouped
+
+        def quantise_g(h, grouped):
+            nc.vector.quantize_mx(out=g_codes[:, halves[h]].bitcast(E5M2), scales=g_plane[:, halves[h]], in_=grouped[:])
 
         def quantise_xm(first, last):
+            for b in range(first, last):
+                nc.scalar.copy(
+                    xm_grouped[:, b * P * PACK : (b + 1) * P * PACK].rearrange("p (c i j) -> p c j i", i=4, j=PACK),
+                    xm_raw[b].rearrange("p j (c i) -> p c j i", i=4),
+                )
             nc.vector.quantize_mx(
                 out=xm_codes[:, first * P : last * P].bitcast(E4M3),
                 scales=xm_plane[:, first * P : last * P],
                 in_=xm_grouped[:, first * P * PACK : last * P * PACK],
             )
 
-        second = keep.tile([P, T], F32, name="out_window1", tag="g_grouped0", align_bytes=64)
-        nc.vector.memset(second[:].bitcast(I32), 0)
-        windows.append(second)
-        xm_raw = {}
-        for first, last, tag in XM_CHUNKS:
-            raw = load_xm(first, last, tag)
-            for b in range(first, last):
-                xm_raw[b] = (raw, first)
-        quantise_before = {0: ((0, 1), (1, 2)), 1: ((2, 4),), 2: ((4, 8),)}
-        for b in range(BLOCKS):
-            for first, last in quantise_before.get(b, ()):
-                for c in range(first, last):
-                    cast_xm(*xm_raw[c], c)
-                quantise_xm(first, last)
+        def multiply(b):
             cols = slice(b * P, (b + 1) * P)
             grad = psum.tile([P, N], F32, name="grad", bufs=4)
             nc.tensor.matmul_mx(
@@ -190,15 +194,36 @@ def tile_attend_glse_w_kernel(tc, xT, w_words, w_scales, y, lse, wt, xm, offs, o
                 start=True,
                 stop=True,
             )
-            if b == 0:
-                dense = keep.tile([P, N], F32, name="first_dense", tag="first_dense")
-            else:
-                dense = ring.tile([P, N], F32, name="dense")
-            nc.scalar.copy(dense[:], grad[:])
-            win = windows[b % 3]
-            nc.vector.tensor_copy(win[:].indirect(offsets[:]), dense[:])
-            nc.sync.dma_start(out[cols, :], win[:])
-            if b == 0:
-                third = keep.tile([P, T], F32, name="out_window2", tag="first_dense")
-                nc.gpsimd.memset(third[:], 0.0)
-                windows.append(third)
+            return grad
+
+        def scatter(b, grad, slots, dense):
+            nc.scalar.copy(dense[:], grad[:, slots])
+            entries = offsets[:, slots.start // 16 : slots.stop // 16]
+            nc.vector.tensor_copy(windows[b % 3][:].indirect(entries), dense[:])
+
+        def store(b):
+            nc.sync.dma_start(out[b * P : (b + 1) * P, :], windows[b % 3][:])
+
+        exponentiate(0)
+        form_g(0)
+        quantise_g(0, interleave_g(0, nc.vector.tensor_copy))
+        quantise_xm(0, 1)
+        early = [multiply(0)]
+        exponentiate(1)
+        quantise_xm(1, 2)
+        early.append(multiply(1))
+        form_g(1)
+        scatter(0, early[0], halves[0], keep.tile([P, HALF], F32, name="dense_first"))
+        quantise_g(1, interleave_g(1, nc.scalar.copy))
+        scatter(1, early[1], halves[0], keep.tile([P, HALF], F32, name="dense_second", tag="g_rows1"))
+        third = keep.tile([P, T], F32, name="out_window2", tag="g_rows1")
+        nc.gpsimd.memset(third[:].bitcast(I32), 0)
+        windows.append(third)
+        quantise_xm(2, 4)
+        for b in range(2):
+            scatter(b, multiply(b), halves[1], ring.tile([P, HALF], F32, name="dense_half"))
+            store(b)
+        quantise_xm(4, BLOCKS)
+        for b in range(2, BLOCKS):
+            scatter(b, multiply(b), slice(0, N), ring.tile([P, N], F32, name="dense"))
+            store(b)

@@ -23,7 +23,7 @@ ACT = mybir.ActivationFunctionType
 ALU = mybir.AluOpType
 
 VECTOR_SHARE = (64, 84)
-XM_CHUNKS = ((0, 1, "word_window"), (1, 4, "xT0"), (4, 8, "xT1"))
+XM_CHUNKS = ((0, 2, "word_window"), (2, 4, "xT0"), (4, 8, "xT1"))
 
 
 def tile_attend_glse_w_kernel(tc, xT, w_words, w_scales, y, lse, wt, xm, offs, out):
@@ -35,51 +35,52 @@ def tile_attend_glse_w_kernel(tc, xT, w_words, w_scales, y, lse, wt, xm, offs, o
 
         offsets = keep.tile([P, N // 16], U16, name="offsets")
         nc.sync.dma_start(offsets[:], offs)
+        lse_sb = keep.tile([P, PACK], F32, name="lse_sb")
+        wt_sb = keep.tile([P, PACK], F32, name="wt_sb")
+        nc.scalar.dma_start(lse_sb[:], lse[0].rearrange("(p j) o -> p (j o)", j=PACK))
+        nc.scalar.dma_start(wt_sb[:], wt[0].rearrange("(p j) o -> p (j o)", j=PACK))
         word_window = keep.tile([P, T], U32, name="word_window", tag="word_window")
         nc.sync.dma_start(word_window[:].bitcast(I32), w_words[0].rearrange("p n b -> p (n b)").bitcast(I32))
         scale_window = keep.tile([P, T], U8, name="scale_window", tag="scale_window")
-        nc.gpsimd.memset(scale_window[:].bitcast(I32), 0)
+        nc.vector.memset(scale_window[:].bitcast(I32), 0)
+        warm_in = keep.tile([P, PACK], F32, name="warm_in", tag="xT1")
+        nc.vector.memset(warm_in[:], 0.0)
+        warm = keep.tile([P, PACK], F32, name="warm", tag="xT0")
+        nc.scalar.activation(warm[:], warm_in[:], ACT.Exp)
         for q in range(4):
             nc.sync.dma_start(
-                scale_window[32 * q : 32 * q + 8, :].bitcast(I32),
-                w_scales[:, 4 * q : 4 * q + 4, :].bitcast(I32),
+                scale_window[32 * q : 32 * q + 4, :].bitcast(I32),
+                w_scales[0, 4 * q : 4 * q + 4, :].bitcast(I32),
             )
+        nc.sync.dma_start(scale_window[4:20, :].bitcast(I32), w_scales[1].bitcast(I32))
         windows = []
-        for i in range(2):
+        for i in range(3):
             win = keep.tile([P, T], F32, name=f"out_window{i}")
             nc.vector.memset(win[:].bitcast(I32), 0)
             windows.append(win)
         g_codes = keep.tile([P, N], U32, name="g_codes", align_bytes=64)
         g_plane = keep.tile([P, N], U8, name="g_plane", align_bytes=64)
-        nc.gpsimd.memset(g_codes[:, HALF:].bitcast(I32), 0)
-        nc.gpsimd.memset(g_plane[:, HALF:].bitcast(I32), 0)
-        warm_in = keep.tile([P, PACK], F32, name="warm_in")
-        nc.gpsimd.memset(warm_in[:], 0.0)
-        warm = keep.tile([P, PACK], F32, name="warm")
-        nc.scalar.activation(warm[:], warm_in[:], ACT.Exp)
+        nc.vector.memset(g_codes[:, HALF:].bitcast(I32), 0)
+        nc.vector.memset(g_plane[:, HALF:].bitcast(I32), 0)
+        neg_lse = keep.tile([P, PACK], F32, name="neg_lse")
+        nc.scalar.activation(neg_lse[:], lse_sb[:], ACT.Copy, scale=-1.0)
         x_raw = []
         for o in range(PASSES):
             raw = keep.tile([P, PACK, R], F32, name=f"x_raw{o}", tag=f"xT{o}")
             nc.sync.dma_start(raw[:], xT[0, o * 512 : (o + 1) * 512, :].rearrange("(p j) r -> p j r", j=PACK))
             x_raw.append(raw)
-        lse_sb = keep.tile([P, PACK], F32, name="lse_sb")
-        wt_sb = keep.tile([P, PACK], F32, name="wt_sb")
-        nc.gpsimd.dma_start(lse_sb[:], lse[0].rearrange("(p j) o -> p (j o)", j=PACK))
-        nc.gpsimd.dma_start(wt_sb[:], wt[0].rearrange("(p j) o -> p (j o)", j=PACK))
-        neg_lse = keep.tile([P, PACK], F32, name="neg_lse")
-        nc.gpsimd.tensor_scalar(neg_lse[:], lse_sb[:], -1.0, 0.0, ALU.mult, ALU.add)
 
+        w_pairs = keep.tile([P, N], U32, name="w_pairs", tag="w_pairs")
+        nc.vector.tensor_copy(w_pairs[:], word_window[:].indirect(offsets[:]))
         both_planes = keep.tile([P, N], U8, name="both_planes", align_bytes=64)
         nc.vector.tensor_copy(both_planes[:], scale_window[:].indirect(offsets[:]))
         second_plane = keep.tile([P, N], U8, name="second_plane", align_bytes=64)
         for q in range(4):
             nc.sync.dma_start(
                 second_plane[32 * q : 32 * q + 4, :].bitcast(I32),
-                both_planes[32 * q + 4 : 32 * q + 8, :].bitcast(I32),
+                both_planes[4 * q + 4 : 4 * q + 8, :].bitcast(I32),
             )
         w_planes = [both_planes, second_plane]
-        w_pairs = keep.tile([P, N], U32, name="w_pairs", tag="w_pairs")
-        nc.vector.tensor_copy(w_pairs[:], word_window[:].indirect(offsets[:]))
         w_codes = keep.tile([P, PASSES, N], U16, name="w_codes", align_bytes=64)
         nc.vector.tensor_copy(w_codes[:], w_pairs[:].bitcast(U16).rearrange("p (s o) -> p o s", o=PASSES))
 
@@ -90,7 +91,7 @@ def tile_attend_glse_w_kernel(tc, xT, w_words, w_scales, y, lse, wt, xm, offs, o
 
         x_codes, x_planes = [], []
         for o in range(PASSES):
-            grouped = keep.tile([P, R * PACK], BF16, name=f"x_grouped{o}", align_bytes=64)
+            grouped = keep.tile([P, R * PACK], BF16, name=f"x_grouped{o}", tag="x_grouped", align_bytes=64)
             dst = grouped[:].rearrange("p (t m j) -> p m j t", t=PACK, j=PACK)
             src = x_raw[o][:].rearrange("p j (m t) -> p m j t", t=PACK)
             share = VECTOR_SHARE[o]
@@ -98,7 +99,7 @@ def tile_attend_glse_w_kernel(tc, xT, w_words, w_scales, y, lse, wt, xm, offs, o
             nc.scalar.copy(dst[:, share:], src[:, share:])
             codes = keep.tile([P, R], U32, name=f"x_codes{o}", align_bytes=64)
             plane = keep.tile([P, R], U8, name=f"x_plane{o}", align_bytes=64)
-            width = P
+            width = R if o == 0 else P
             for c in range(0, R, width):
                 nc.vector.quantize_mx(
                     out=codes[:, c : c + width].bitcast(E4M3),
@@ -122,10 +123,12 @@ def tile_attend_glse_w_kernel(tc, xT, w_words, w_scales, y, lse, wt, xm, offs, o
                     stop=(o == PASSES - 1),
                 )
 
-        y_wt = keep.tile([P, PACK, N], F32, name="y_wt")
-        nc.scalar.activation(y_wt[:, 0, :], y_sb[:, 0, :], ACT.Copy, scale=wt_sb[:, 0:1])
+        y_wt_first = keep.tile([P, N], F32, name="y_wt_first")
+        nc.scalar.activation(y_wt_first[:], y_sb[:, 0, :], ACT.Copy, scale=wt_sb[:, 0:1])
+        y_wt_rest = keep.tile([P, PACK - 1, N], F32, name="y_wt_rest", tag="x_grouped", align_bytes=64)
+        y_wt = [y_wt_first[:]] + [y_wt_rest[:, t - 1, :] for t in range(1, PACK)]
         for t in range(1, PACK):
-            nc.vector.tensor_scalar(y_wt[:, t, :], y_sb[:, t, :], wt_sb[:, t : t + 1], None, ALU.mult)
+            nc.vector.tensor_scalar(y_wt[t], y_sb[:, t, :], wt_sb[:, t : t + 1], None, ALU.mult)
 
         xm_rows = xm[0].rearrange("(p j) d -> p j d", j=PACK)
         xm_raw = {}
@@ -137,10 +140,9 @@ def tile_attend_glse_w_kernel(tc, xT, w_words, w_scales, y, lse, wt, xm, offs, o
 
         halves = [slice(h * HALF, (h + 1) * HALF) for h in range(2)]
         probs = keep.tile([P, PACK, N], F32, name="probs")
-        g_rows = [keep.tile([P, PACK, HALF], BF16, name=f"g_rows{h}", tag=f"g_rows{h}") for h in range(2)]
+        g_rows = [keep.tile([P, PACK, HALF], BF16, name=f"g_rows{h}", tag=f"g_rows{h}", align_bytes=64) for h in range(1)]
         xm_codes = keep.tile([P, D], U32, name="xm_codes", align_bytes=64)
         xm_plane = keep.tile([P, D], U8, name="xm_plane", align_bytes=64)
-        xm_grouped = keep.tile([P, D * PACK], BF16, name="xm_grouped", align_bytes=64)
 
         def exponentiate(h):
             for t in range(PACK):
@@ -154,7 +156,7 @@ def tile_attend_glse_w_kernel(tc, xT, w_words, w_scales, y, lse, wt, xm, offs, o
                     g_rows[h][:, t, :],
                     probs[:, t, halves[h]],
                     wt_sb[:, t : t + 1],
-                    y_wt[:, t, halves[h]],
+                    y_wt[t][:, halves[h]],
                     ALU.mult,
                     ALU.subtract,
                 )
@@ -170,16 +172,20 @@ def tile_attend_glse_w_kernel(tc, xT, w_words, w_scales, y, lse, wt, xm, offs, o
         def quantise_g(h, grouped):
             nc.vector.quantize_mx(out=g_codes[:, halves[h]].bitcast(E5M2), scales=g_plane[:, halves[h]], in_=grouped[:])
 
-        def quantise_xm(first, last):
+        def cast_xm(first, last, tag):
+            grouped = keep.tile([P, (last - first) * P * PACK], BF16, name=f"xm_grouped{first}", tag=tag, align_bytes=64)
             for b in range(first, last):
                 nc.scalar.copy(
-                    xm_grouped[:, b * P * PACK : (b + 1) * P * PACK].rearrange("p (c i j) -> p c j i", i=4, j=PACK),
+                    grouped[:, (b - first) * P * PACK : (b - first + 1) * P * PACK].rearrange("p (c i j) -> p c j i", i=4, j=PACK),
                     xm_raw[b].rearrange("p j (c i) -> p c j i", i=4),
                 )
+            return grouped
+
+        def quantise_xm(first, last, grouped):
             nc.vector.quantize_mx(
                 out=xm_codes[:, first * P : last * P].bitcast(E4M3),
                 scales=xm_plane[:, first * P : last * P],
-                in_=xm_grouped[:, first * P * PACK : last * P * PACK],
+                in_=grouped[:],
             )
 
         def multiply(b):
@@ -206,24 +212,24 @@ def tile_attend_glse_w_kernel(tc, xT, w_words, w_scales, y, lse, wt, xm, offs, o
 
         exponentiate(0)
         form_g(0)
-        quantise_g(0, interleave_g(0, nc.vector.tensor_copy))
-        quantise_xm(0, 1)
+        first_g = interleave_g(0, nc.vector.tensor_copy)
+        quantise_xm(0, 1, cast_xm(0, 1, "g_rows1"))
+        quantise_g(0, first_g)
         early = [multiply(0)]
         exponentiate(1)
-        quantise_xm(1, 2)
-        early.append(multiply(1))
+        second_xm = cast_xm(1, 2, "xm_grouped1")
+        g_rows.append(keep.tile([P, PACK, HALF], BF16, name="g_rows1", tag="g_rows1", align_bytes=64))
         form_g(1)
+        quantise_xm(1, 2, second_xm)
+        early.append(multiply(1))
         scatter(0, early[0], halves[0], keep.tile([P, HALF], F32, name="dense_first"))
         quantise_g(1, interleave_g(1, nc.scalar.copy))
-        scatter(1, early[1], halves[0], keep.tile([P, HALF], F32, name="dense_second", tag="g_rows1"))
-        third = keep.tile([P, T], F32, name="out_window2", tag="g_rows1")
-        nc.gpsimd.memset(third[:].bitcast(I32), 0)
-        windows.append(third)
-        quantise_xm(2, 4)
+        scatter(1, early[1], halves[0], keep.tile([P, HALF], F32, name="dense_second", tag="g_rows1", align_bytes=64))
+        quantise_xm(2, 4, cast_xm(2, 4, "xm_grouped2"))
         for b in range(2):
             scatter(b, multiply(b), halves[1], ring.tile([P, HALF], F32, name="dense_half"))
             store(b)
-        quantise_xm(4, BLOCKS)
+        quantise_xm(4, BLOCKS, cast_xm(4, BLOCKS, "xm_grouped4"))
         for b in range(2, BLOCKS):
             scatter(b, multiply(b), slice(0, N), ring.tile([P, N], F32, name="dense"))
             store(b)

@@ -92,14 +92,14 @@ def tile_attend_glse_w_kernel(tc, xT, w_words, w_scales, y, lse, wt, xm, offs, o
         x_codes, x_planes = [], []
         for o in range(PASSES):
             grouped = keep.tile([P, R * PACK], BF16, name=f"x_grouped{o}", tag="x_grouped", align_bytes=64)
-            dst = grouped[:].rearrange("p (t m j) -> p m j t", t=PACK, j=PACK)
-            src = x_raw[o][:].rearrange("p j (m t) -> p m j t", t=PACK)
+            dst = grouped[:].rearrange("p (t m j) -> p m t j", t=PACK, j=PACK)
+            src = x_raw[o][:].rearrange("p j (m t) -> p m t j", t=PACK)
             share = VECTOR_SHARE[o]
             nc.vector.tensor_copy(dst[:, :share], src[:, :share])
             nc.scalar.copy(dst[:, share:], src[:, share:])
             codes = keep.tile([P, R], U32, name=f"x_codes{o}", align_bytes=64)
             plane = keep.tile([P, R], U8, name=f"x_plane{o}", align_bytes=64)
-            width = R if o == 0 else P
+            width = P
             for c in range(0, R, width):
                 nc.vector.quantize_mx(
                     out=codes[:, c : c + width].bitcast(E4M3),

@@ -22,8 +22,9 @@ E2M1 = mybir.dt.float4_e2m1fn_x4
 ACT = mybir.ActivationFunctionType
 ALU = mybir.AluOpType
 
-VECTOR_SHARE = (64, 84)
-XM_CHUNKS = ((0, 2, "word_window"), (2, 4, "xT0"), (4, 8, "xT1"))
+VECTOR_SHARE = 84
+SCALE_ROWS = 16 * PASSES
+XM_CHUNKS = ((0, 1, "scale_rows"), (1, 4, "x_raw0"), (4, 8, "scale_window"))
 
 
 def tile_attend_glse_w_kernel(tc, xT, w_words, w_scales, y, lse, wt, xm, offs, out):
@@ -32,79 +33,76 @@ def tile_attend_glse_w_kernel(tc, xT, w_words, w_scales, y, lse, wt, xm, offs, o
         keep = ctx.enter_context(tc.tile_pool(name="keep", bufs=1))
         ring = ctx.enter_context(tc.tile_pool(name="ring", bufs=3))
         psum = ctx.enter_context(tc.psum_pool(name="psum", bufs=1))
+        halves = [slice(h * HALF, (h + 1) * HALF) for h in range(2)]
 
         offsets = keep.tile([P, N // 16], U16, name="offsets")
         nc.sync.dma_start(offsets[:], offs)
+        scale_tile = keep.tile([P, T + 4], U8, name="scale_tile", tag="scale_window")
+        nc.scalar.dma_start(
+            scale_tile[:SCALE_ROWS, :T].bitcast(I32), w_scales.rearrange("o f t -> f o t").bitcast(I32)
+        )
+        word_window = keep.tile([P, T], U32, name="word_window", tag="word_window")
+        nc.sync.dma_start(word_window[:].bitcast(I32), w_words[0].rearrange("p n b -> p (n b)").bitcast(I32))
         lse_sb = keep.tile([P, PACK], F32, name="lse_sb")
         wt_sb = keep.tile([P, PACK], F32, name="wt_sb")
         nc.scalar.dma_start(lse_sb[:], lse[0].rearrange("(p j) o -> p (j o)", j=PACK))
         nc.scalar.dma_start(wt_sb[:], wt[0].rearrange("(p j) o -> p (j o)", j=PACK))
-        word_window = keep.tile([P, T], U32, name="word_window", tag="word_window")
-        nc.sync.dma_start(word_window[:].bitcast(I32), w_words[0].rearrange("p n b -> p (n b)").bitcast(I32))
-        scale_window = keep.tile([P, T], U8, name="scale_window", tag="scale_window")
-        nc.vector.memset(scale_window[:].bitcast(I32), 0)
-        warm_in = keep.tile([P, PACK], F32, name="warm_in", tag="xT1")
-        nc.vector.memset(warm_in[:], 0.0)
-        warm = keep.tile([P, PACK], F32, name="warm", tag="xT0")
-        nc.scalar.activation(warm[:], warm_in[:], ACT.Exp)
-        for q in range(4):
-            nc.sync.dma_start(
-                scale_window[32 * q : 32 * q + 4, :].bitcast(I32),
-                w_scales[0, 4 * q : 4 * q + 4, :].bitcast(I32),
-            )
-        nc.sync.dma_start(scale_window[4:20, :].bitcast(I32), w_scales[1].bitcast(I32))
-        windows = []
-        for i in range(3):
-            win = keep.tile([P, T], F32, name=f"out_window{i}")
-            nc.vector.memset(win[:].bitcast(I32), 0)
-            windows.append(win)
+
+        def load_x(o, tag):
+            raw = keep.tile([P, PACK, R], F32, name=f"x_raw{o}", tag=tag)
+            nc.sync.dma_start(raw[:], xT[0, o * 512 : (o + 1) * 512, :].rearrange("(p j) r -> p j r", j=PACK))
+            return raw
+
+        x_raw = [load_x(0, "x_raw0")]
+
+        for rows in (slice(32, 64), slice(64, P)):
+            nc.vector.memset(scale_tile[rows, :].bitcast(I32), 0)
         g_codes = keep.tile([P, N], U32, name="g_codes", align_bytes=64)
         g_plane = keep.tile([P, N], U8, name="g_plane", align_bytes=64)
-        nc.vector.memset(g_codes[:, HALF:].bitcast(I32), 0)
-        nc.vector.memset(g_plane[:, HALF:].bitcast(I32), 0)
+        nc.gpsimd.memset(g_codes[:, HALF:].bitcast(I32), 0)
+        nc.gpsimd.memset(g_plane[:, HALF:].bitcast(I32), 0)
+        windows = [keep.tile([P, T], F32, name=f"out_window{i}") for i in range(3)]
+        for cols in (slice(0, T // 2 - 1), slice(T // 2 - 1, T)):
+            nc.vector.memset(windows[0][:, cols].bitcast(I32), 0)
+        for win in windows[1:]:
+            nc.gpsimd.memset(win[:].bitcast(I32), 0)
         neg_lse = keep.tile([P, PACK], F32, name="neg_lse")
         nc.scalar.activation(neg_lse[:], lse_sb[:], ACT.Copy, scale=-1.0)
-        x_raw = []
-        for o in range(PASSES):
-            raw = keep.tile([P, PACK, R], F32, name=f"x_raw{o}", tag=f"xT{o}")
-            nc.sync.dma_start(raw[:], xT[0, o * 512 : (o + 1) * 512, :].rearrange("(p j) r -> p j r", j=PACK))
-            x_raw.append(raw)
 
-        w_pairs = keep.tile([P, N], U32, name="w_pairs", tag="w_pairs")
-        nc.vector.tensor_copy(w_pairs[:], word_window[:].indirect(offsets[:]))
-        both_planes = keep.tile([P, N], U8, name="both_planes", align_bytes=64)
-        nc.vector.tensor_copy(both_planes[:], scale_window[:].indirect(offsets[:]))
-        second_plane = keep.tile([P, N], U8, name="second_plane", align_bytes=64)
+        scale_rows = keep.tile([P, N], U8, name="scale_rows", tag="scale_rows")
+        nc.vector.tensor_copy(scale_rows[:], scale_tile[:, :T].indirect(offsets[:]))
+        w_planes = keep.tile([P, PASSES, N], U8, name="w_planes", align_bytes=64)
         for q in range(4):
             nc.sync.dma_start(
-                second_plane[32 * q : 32 * q + 4, :].bitcast(I32),
-                both_planes[4 * q + 4 : 4 * q + 8, :].bitcast(I32),
+                w_planes[32 * q : 32 * q + 4].rearrange("p o s -> p (o s)").bitcast(I32),
+                scale_rows[8 * q : 8 * q + 8, :].bitcast(I32),
             )
-        w_planes = [both_planes, second_plane]
+        x_raw.append(load_x(1, "scale_window"))
+        w_pairs = keep.tile([P, N], U32, name="w_pairs", tag="w_pairs")
+        nc.vector.tensor_copy(w_pairs[:], word_window[:].indirect(offsets[:]))
         w_codes = keep.tile([P, PASSES, N], U16, name="w_codes", align_bytes=64)
         nc.vector.tensor_copy(w_codes[:], w_pairs[:].bitcast(U16).rearrange("p (s o) -> p o s", o=PASSES))
 
         y_rows = y[0].rearrange("(p j) s -> p j s", j=PACK)
-        y_sb = keep.tile([P, PACK, N], F32, name="y_sb", tag="scale_window")
-        for planes in (slice(0, 2), slice(2, 3), slice(3, 4)):
-            nc.sync.dma_start(y_sb[:, planes, :], y_rows[:, planes, :])
+        y_sb = []
+        for h, tag in enumerate(("word_window", "w_pairs")):
+            y_sb.append(keep.tile([P, PACK, HALF], F32, name=f"y_sb{h}", tag=tag))
+            nc.sync.dma_start(y_sb[h][:], y_rows[:, :, halves[h]])
 
         x_codes, x_planes = [], []
         for o in range(PASSES):
-            grouped = keep.tile([P, R * PACK], BF16, name=f"x_grouped{o}", tag="x_grouped", align_bytes=64)
+            grouped = keep.tile([P, R * PACK], BF16, name=f"x_grouped{o}", align_bytes=64)
             dst = grouped[:].rearrange("p (t m j) -> p m t j", t=PACK, j=PACK)
             src = x_raw[o][:].rearrange("p j (m t) -> p m t j", t=PACK)
-            share = VECTOR_SHARE[o]
-            nc.vector.tensor_copy(dst[:, :share], src[:, :share])
-            nc.scalar.copy(dst[:, share:], src[:, share:])
-            codes = keep.tile([P, R], U32, name=f"x_codes{o}", align_bytes=64)
+            nc.vector.tensor_copy(dst[:, :VECTOR_SHARE], src[:, :VECTOR_SHARE])
+            nc.scalar.copy(dst[:, VECTOR_SHARE:], src[:, VECTOR_SHARE:])
+            codes = keep.tile([P, R], U32, name=f"x_codes{o}", tag=f"x_codes{o}", align_bytes=64)
             plane = keep.tile([P, R], U8, name=f"x_plane{o}", align_bytes=64)
-            width = P
-            for c in range(0, R, width):
+            for c in range(0, R, P):
                 nc.vector.quantize_mx(
-                    out=codes[:, c : c + width].bitcast(E4M3),
-                    scales=plane[:, c : c + width],
-                    in_=grouped[:, PACK * c : PACK * (c + width)],
+                    out=codes[:, c : c + P].bitcast(E4M3),
+                    scales=plane[:, c : c + P],
+                    in_=grouped[:, PACK * c : PACK * (c + P)],
                 )
             x_codes.append(codes)
             x_planes.append(plane)
@@ -118,17 +116,10 @@ def tile_attend_glse_w_kernel(tc, xT, w_words, w_scales, y, lse, wt, xm, offs, o
                     lhsT=x_codes[o][:, rows].bitcast(E4M3),
                     lhsT_scale=x_planes[o][:, rows],
                     rhs=w_codes[:, o, :].bitcast(E2M1),
-                    rhs_scale=w_planes[o][:],
+                    rhs_scale=w_planes[:, o, :],
                     start=(o == 0),
                     stop=(o == PASSES - 1),
                 )
-
-        y_wt_first = keep.tile([P, N], F32, name="y_wt_first")
-        nc.scalar.activation(y_wt_first[:], y_sb[:, 0, :], ACT.Copy, scale=wt_sb[:, 0:1])
-        y_wt_rest = keep.tile([P, PACK - 1, N], F32, name="y_wt_rest", tag="x_grouped", align_bytes=64)
-        y_wt = [y_wt_first[:]] + [y_wt_rest[:, t - 1, :] for t in range(1, PACK)]
-        for t in range(1, PACK):
-            nc.vector.tensor_scalar(y_wt[t], y_sb[:, t, :], wt_sb[:, t : t + 1], None, ALU.mult)
 
         xm_rows = xm[0].rearrange("(p j) d -> p j d", j=PACK)
         xm_raw = {}
@@ -138,25 +129,28 @@ def tile_attend_glse_w_kernel(tc, xT, w_words, w_scales, y, lse, wt, xm, offs, o
             for b in range(first, last):
                 xm_raw[b] = raw[:, :, (b - first) * P : (b - first + 1) * P]
 
-        halves = [slice(h * HALF, (h + 1) * HALF) for h in range(2)]
-        probs = keep.tile([P, PACK, N], F32, name="probs")
-        g_rows = [keep.tile([P, PACK, HALF], BF16, name=f"g_rows{h}", tag=f"g_rows{h}", align_bytes=64) for h in range(1)]
+        probs = [keep.tile([P, PACK, HALF], F32, name=f"probs{h}") for h in range(2)]
+        y_wt, g_rows = {}, {}
         xm_codes = keep.tile([P, D], U32, name="xm_codes", align_bytes=64)
         xm_plane = keep.tile([P, D], U8, name="xm_plane", align_bytes=64)
 
-        def exponentiate(h):
+        def exponentiate(h, places):
+            for t in places:
+                nc.scalar.activation(probs[h][:, t, :], scores[t][:, halves[h]], ACT.Exp, bias=neg_lse[:, t : t + 1])
+
+        def weigh_targets(h, tag):
+            y_wt[h] = keep.tile([P, PACK, HALF], F32, name=f"y_wt{h}", tag=tag)
             for t in range(PACK):
-                nc.scalar.activation(
-                    probs[:, t, halves[h]], scores[t][:, halves[h]], ACT.Exp, bias=neg_lse[:, t : t + 1]
-                )
+                nc.vector.tensor_scalar(y_wt[h][:, t, :], y_sb[h][:, t, :], wt_sb[:, t : t + 1], None, ALU.mult)
 
         def form_g(h):
+            g_rows[h] = keep.tile([P, PACK, HALF], BF16, name=f"g_rows{h}", tag=f"g_rows{h}")
             for t in range(PACK):
                 nc.vector.scalar_tensor_tensor(
                     g_rows[h][:, t, :],
-                    probs[:, t, halves[h]],
+                    probs[h][:, t, :],
                     wt_sb[:, t : t + 1],
-                    y_wt[t][:, halves[h]],
+                    y_wt[h][:, t, :],
                     ALU.mult,
                     ALU.subtract,
                 )
@@ -210,21 +204,23 @@ def tile_attend_glse_w_kernel(tc, xT, w_words, w_scales, y, lse, wt, xm, offs, o
         def store(b):
             nc.sync.dma_start(out[b * P : (b + 1) * P, :], windows[b % 3][:])
 
-        exponentiate(0)
+
+        exponentiate(0, range(PACK))
+        weigh_targets(0, "y_wt0")
         form_g(0)
         first_g = interleave_g(0, nc.vector.tensor_copy)
-        quantise_xm(0, 1, cast_xm(0, 1, "g_rows1"))
+        exponentiate(1, range(2))
+        quantise_xm(0, 1, cast_xm(0, 1, "x_codes1"))
         quantise_g(0, first_g)
         early = [multiply(0)]
-        exponentiate(1)
-        second_xm = cast_xm(1, 2, "xm_grouped1")
-        g_rows.append(keep.tile([P, PACK, HALF], BF16, name="g_rows1", tag="g_rows1", align_bytes=64))
+        exponentiate(1, range(2, PACK))
+        weigh_targets(1, "g_rows0")
         form_g(1)
-        quantise_xm(1, 2, second_xm)
-        early.append(multiply(1))
         scatter(0, early[0], halves[0], keep.tile([P, HALF], F32, name="dense_first"))
+        quantise_xm(1, 2, cast_xm(1, 2, "xm_grouped1"))
+        early.append(multiply(1))
         quantise_g(1, interleave_g(1, nc.scalar.copy))
-        scatter(1, early[1], halves[0], keep.tile([P, HALF], F32, name="dense_second", tag="g_rows1", align_bytes=64))
+        scatter(1, early[1], halves[0], keep.tile([P, HALF], F32, name="dense_second"))
         quantise_xm(2, 4, cast_xm(2, 4, "xm_grouped2"))
         for b in range(2):
             scatter(b, multiply(b), halves[1], ring.tile([P, HALF], F32, name="dense_half"))

@@ -22,8 +22,8 @@ E2M1 = mybir.dt.float4_e2m1fn_x4
 ACT = mybir.ActivationFunctionType
 ALU = mybir.AluOpType
 
-VECTOR_SHARE = 84
-SCALE_ROWS = 16 * PASSES
+VECTOR_SHARE = (40, 84)
+SCALE_FIRST = P - 16 * PASSES
 XM_CHUNKS = ((0, 1, "scale_rows"), (1, 4, "x_raw0"), (4, 8, "scale_window"))
 
 
@@ -37,9 +37,9 @@ def tile_attend_glse_w_kernel(tc, xT, w_words, w_scales, y, lse, wt, xm, offs, o
 
         offsets = keep.tile([P, N // 16], U16, name="offsets")
         nc.sync.dma_start(offsets[:], offs)
-        scale_tile = keep.tile([P, T + 4], U8, name="scale_tile", tag="scale_window")
+        scale_window = keep.tile([P, T], U8, name="scale_window", tag="scale_window")
         nc.scalar.dma_start(
-            scale_tile[:SCALE_ROWS, :T].bitcast(I32), w_scales.rearrange("o f t -> f o t").bitcast(I32)
+            scale_window[SCALE_FIRST:, :].bitcast(I32), w_scales.rearrange("o f t -> f o t").bitcast(I32)
         )
         word_window = keep.tile([P, T], U32, name="word_window", tag="word_window")
         nc.sync.dma_start(word_window[:].bitcast(I32), w_words[0].rearrange("p n b -> p (n b)").bitcast(I32))
@@ -55,29 +55,27 @@ def tile_attend_glse_w_kernel(tc, xT, w_words, w_scales, y, lse, wt, xm, offs, o
 
         x_raw = [load_x(0, "x_raw0")]
 
-        for rows in (slice(32, 64), slice(64, P)):
-            nc.vector.memset(scale_tile[rows, :].bitcast(I32), 0)
-        g_codes = keep.tile([P, N], U32, name="g_codes", align_bytes=64)
-        g_plane = keep.tile([P, N], U8, name="g_plane", align_bytes=64)
-        nc.gpsimd.memset(g_codes[:, HALF:].bitcast(I32), 0)
-        nc.gpsimd.memset(g_plane[:, HALF:].bitcast(I32), 0)
+        nc.vector.memset(scale_window[:SCALE_FIRST, :].bitcast(I32), 0)
         windows = [keep.tile([P, T], F32, name=f"out_window{i}") for i in range(3)]
-        for cols in (slice(0, T // 2 - 1), slice(T // 2 - 1, T)):
-            nc.vector.memset(windows[0][:, cols].bitcast(I32), 0)
-        for win in windows[1:]:
-            nc.gpsimd.memset(win[:].bitcast(I32), 0)
+        for win in windows[:2]:
+            nc.vector.memset(win[:].bitcast(I32), 0)
         neg_lse = keep.tile([P, PACK], F32, name="neg_lse")
         nc.scalar.activation(neg_lse[:], lse_sb[:], ACT.Copy, scale=-1.0)
 
         scale_rows = keep.tile([P, N], U8, name="scale_rows", tag="scale_rows")
-        nc.vector.tensor_copy(scale_rows[:], scale_tile[:, :T].indirect(offsets[:]))
+        nc.vector.tensor_copy(scale_rows[:], scale_window[:].indirect(offsets[:]))
         w_planes = keep.tile([P, PASSES, N], U8, name="w_planes", align_bytes=64)
         for q in range(4):
             nc.sync.dma_start(
                 w_planes[32 * q : 32 * q + 4].rearrange("p o s -> p (o s)").bitcast(I32),
-                scale_rows[8 * q : 8 * q + 8, :].bitcast(I32),
+                scale_rows[SCALE_FIRST + 8 * q : SCALE_FIRST + 8 * q + 8, :].bitcast(I32),
             )
         x_raw.append(load_x(1, "scale_window"))
+        nc.vector.memset(windows[2][:].bitcast(I32), 0)
+        g_codes = keep.tile([P, N], U32, name="g_codes", align_bytes=64)
+        g_plane = keep.tile([P, N], U8, name="g_plane", align_bytes=64)
+        nc.vector.memset(g_codes[:, HALF:].bitcast(I32), 0)
+        nc.vector.memset(g_plane[:, HALF:].bitcast(I32), 0)
         w_pairs = keep.tile([P, N], U32, name="w_pairs", tag="w_pairs")
         nc.vector.tensor_copy(w_pairs[:], word_window[:].indirect(offsets[:]))
         w_codes = keep.tile([P, PASSES, N], U16, name="w_codes", align_bytes=64)
@@ -94,8 +92,9 @@ def tile_attend_glse_w_kernel(tc, xT, w_words, w_scales, y, lse, wt, xm, offs, o
             grouped = keep.tile([P, R * PACK], BF16, name=f"x_grouped{o}", align_bytes=64)
             dst = grouped[:].rearrange("p (t m j) -> p m t j", t=PACK, j=PACK)
             src = x_raw[o][:].rearrange("p j (m t) -> p m t j", t=PACK)
-            nc.vector.tensor_copy(dst[:, :VECTOR_SHARE], src[:, :VECTOR_SHARE])
-            nc.scalar.copy(dst[:, VECTOR_SHARE:], src[:, VECTOR_SHARE:])
+            share = VECTOR_SHARE[o]
+            nc.vector.tensor_copy(dst[:, :share], src[:, :share])
+            nc.scalar.copy(dst[:, share:], src[:, share:])
             codes = keep.tile([P, R], U32, name=f"x_codes{o}", tag=f"x_codes{o}", align_bytes=64)
             plane = keep.tile([P, R], U8, name=f"x_plane{o}", align_bytes=64)
             for c in range(0, R, P):
@@ -129,7 +128,7 @@ def tile_attend_glse_w_kernel(tc, xT, w_words, w_scales, y, lse, wt, xm, offs, o
             for b in range(first, last):
                 xm_raw[b] = raw[:, :, (b - first) * P : (b - first + 1) * P]
 
-        probs = [keep.tile([P, PACK, HALF], F32, name=f"probs{h}") for h in range(2)]
+        probs = [keep.tile([P, PACK, HALF], F32, name=f"probs{h}", tag=f"probs{h}", align_bytes=64) for h in range(2)]
         y_wt, g_rows = {}, {}
         xm_codes = keep.tile([P, D], U32, name="xm_codes", align_bytes=64)
         xm_plane = keep.tile([P, D], U8, name="xm_plane", align_bytes=64)
@@ -156,7 +155,7 @@ def tile_attend_glse_w_kernel(tc, xT, w_words, w_scales, y, lse, wt, xm, offs, o
                 )
 
         def interleave_g(h, copy):
-            grouped = keep.tile([P, HALF * PACK], BF16, name=f"g_grouped{h}", align_bytes=64)
+            grouped = keep.tile([P, HALF * PACK], BF16, name=f"g_grouped{h}", tag=f"g_grouped{h}", align_bytes=64)
             copy(
                 grouped[:].rearrange("p (c i t) -> p c t i", i=4, t=PACK),
                 g_rows[h][:].rearrange("p t (c i) -> p c t i", i=4),
@@ -217,15 +216,19 @@ def tile_attend_glse_w_kernel(tc, xT, w_words, w_scales, y, lse, wt, xm, offs, o
         weigh_targets(1, "g_rows0")
         form_g(1)
         scatter(0, early[0], halves[0], keep.tile([P, HALF], F32, name="dense_first"))
-        quantise_xm(1, 2, cast_xm(1, 2, "xm_grouped1"))
+        quantise_xm(1, 2, cast_xm(1, 2, "g_grouped0"))
         early.append(multiply(1))
         quantise_g(1, interleave_g(1, nc.scalar.copy))
-        scatter(1, early[1], halves[0], keep.tile([P, HALF], F32, name="dense_second"))
-        quantise_xm(2, 4, cast_xm(2, 4, "xm_grouped2"))
-        for b in range(2):
-            scatter(b, multiply(b), halves[1], ring.tile([P, HALF], F32, name="dense_half"))
+        scatter(1, early[1], halves[0], keep.tile([P, HALF], F32, name="dense_second", tag="g_rows1"))
+        quantise_xm(2, 4, cast_xm(2, 4, "probs1"))
+        for b, tag in enumerate(("dense_third", "probs1")):
+            scatter(b, multiply(b), halves[1], keep.tile([P, HALF], F32, name=f"dense_late{b}", tag=tag, align_bytes=64))
             store(b)
-        quantise_xm(4, BLOCKS, cast_xm(4, BLOCKS, "xm_grouped4"))
+        quantise_xm(4, BLOCKS, cast_xm(4, BLOCKS, "g_grouped1"))
         for b in range(2, BLOCKS):
-            scatter(b, multiply(b), slice(0, N), ring.tile([P, N], F32, name="dense"))
+            if b == 3:
+                dense = keep.tile([P, N], F32, name="dense_held", tag="g_grouped1", align_bytes=64)
+            else:
+                dense = ring.tile([P, N], F32, name="dense")
+            scatter(b, multiply(b), slice(0, N), dense)
             store(b)

@@ -22,9 +22,10 @@ E2M1 = mybir.dt.float4_e2m1fn_x4
 ACT = mybir.ActivationFunctionType
 ALU = mybir.AluOpType
 
-VECTOR_SHARE = (40, 84)
+VECTOR_SHARE = 84
 SCALE_FIRST = P - 16 * PASSES
-XM_CHUNKS = ((0, 1, "scale_rows"), (1, 4, "x_raw0"), (4, 8, "scale_window"))
+WINDOWS = 4
+EARLY = 3
 
 
 def tile_attend_glse_w_kernel(tc, xT, w_words, w_scales, y, lse, wt, xm, offs, out):
@@ -37,9 +38,9 @@ def tile_attend_glse_w_kernel(tc, xT, w_words, w_scales, y, lse, wt, xm, offs, o
 
         offsets = keep.tile([P, N // 16], U16, name="offsets")
         nc.sync.dma_start(offsets[:], offs)
-        scale_window = keep.tile([P, T], U8, name="scale_window", tag="scale_window")
+        scale_tile = keep.tile([P, T + 4], U8, name="scale_tile", tag="scale_window")
         nc.scalar.dma_start(
-            scale_window[SCALE_FIRST:, :].bitcast(I32), w_scales.rearrange("o f t -> f o t").bitcast(I32)
+            scale_tile[SCALE_FIRST:, :T].bitcast(I32), w_scales.rearrange("o f t -> f o t").bitcast(I32)
         )
         word_window = keep.tile([P, T], U32, name="word_window", tag="word_window")
         nc.sync.dma_start(word_window[:].bitcast(I32), w_words[0].rearrange("p n b -> p (n b)").bitcast(I32))
@@ -55,15 +56,21 @@ def tile_attend_glse_w_kernel(tc, xT, w_words, w_scales, y, lse, wt, xm, offs, o
 
         x_raw = [load_x(0, "x_raw0")]
 
-        nc.vector.memset(scale_window[:SCALE_FIRST, :].bitcast(I32), 0)
-        windows = [keep.tile([P, T], F32, name=f"out_window{i}") for i in range(3)]
-        for win in windows[:2]:
-            nc.vector.memset(win[:].bitcast(I32), 0)
+        nc.vector.memset(scale_tile[:SCALE_FIRST, :].bitcast(I32), 0)
+        g_codes = keep.tile([P, N], U32, name="g_codes", align_bytes=64)
+        g_plane = keep.tile([P, N], U8, name="g_plane", align_bytes=64)
+        nc.gpsimd.memset(g_codes[:, HALF:].bitcast(I32), 0)
+        nc.gpsimd.memset(g_plane[:, HALF:].bitcast(I32), 0)
+        windows = [keep.tile([P, T], F32, name=f"out_window{i}") for i in range(WINDOWS)]
+        for cols in (slice(0, T // 2 - 1), slice(T // 2 - 1, T)):
+            nc.vector.memset(windows[0][:, cols].bitcast(I32), 0)
+        for win in windows[1:]:
+            nc.gpsimd.memset(win[:].bitcast(I32), 0)
         neg_lse = keep.tile([P, PACK], F32, name="neg_lse")
         nc.scalar.activation(neg_lse[:], lse_sb[:], ACT.Copy, scale=-1.0)
 
         scale_rows = keep.tile([P, N], U8, name="scale_rows", tag="scale_rows")
-        nc.vector.tensor_copy(scale_rows[:], scale_window[:].indirect(offsets[:]))
+        nc.vector.tensor_copy(scale_rows[:], scale_tile[:, :T].indirect(offsets[:]))
         w_planes = keep.tile([P, PASSES, N], U8, name="w_planes", align_bytes=64)
         for q in range(4):
             nc.sync.dma_start(
@@ -71,30 +78,36 @@ def tile_attend_glse_w_kernel(tc, xT, w_words, w_scales, y, lse, wt, xm, offs, o
                 scale_rows[SCALE_FIRST + 8 * q : SCALE_FIRST + 8 * q + 8, :].bitcast(I32),
             )
         x_raw.append(load_x(1, "scale_window"))
-        nc.vector.memset(windows[2][:].bitcast(I32), 0)
-        g_codes = keep.tile([P, N], U32, name="g_codes", align_bytes=64)
-        g_plane = keep.tile([P, N], U8, name="g_plane", align_bytes=64)
-        nc.vector.memset(g_codes[:, HALF:].bitcast(I32), 0)
-        nc.vector.memset(g_plane[:, HALF:].bitcast(I32), 0)
         w_pairs = keep.tile([P, N], U32, name="w_pairs", tag="w_pairs")
         nc.vector.tensor_copy(w_pairs[:], word_window[:].indirect(offsets[:]))
         w_codes = keep.tile([P, PASSES, N], U16, name="w_codes", align_bytes=64)
         nc.vector.tensor_copy(w_codes[:], w_pairs[:].bitcast(U16).rearrange("p (s o) -> p o s", o=PASSES))
 
         y_rows = y[0].rearrange("(p j) s -> p j s", j=PACK)
-        y_sb = []
-        for h, tag in enumerate(("word_window", "w_pairs")):
-            y_sb.append(keep.tile([P, PACK, HALF], F32, name=f"y_sb{h}", tag=tag))
+        xm_rows = xm[0].rearrange("(p j) d -> p j d", j=PACK)
+        y_sb, xm_raw = {}, {}
+
+        def load_y(h, tag):
+            y_sb[h] = keep.tile([P, PACK, HALF], F32, name=f"y_sb{h}", tag=tag)
             nc.sync.dma_start(y_sb[h][:], y_rows[:, :, halves[h]])
+
+        def load_xm(first, last, tag):
+            raw = keep.tile([P, PACK, (last - first) * P], F32, name=f"xm_raw{first}", tag=tag)
+            nc.sync.dma_start(raw[:], xm_rows[:, :, first * P : last * P])
+            for b in range(first, last):
+                xm_raw[b] = raw[:, :, (b - first) * P : (b - first + 1) * P]
+
+        load_y(0, "word_window")
+        load_xm(0, 2, "w_pairs")
+        load_y(1, "scale_rows")
 
         x_codes, x_planes = [], []
         for o in range(PASSES):
             grouped = keep.tile([P, R * PACK], BF16, name=f"x_grouped{o}", align_bytes=64)
             dst = grouped[:].rearrange("p (t m j) -> p m t j", t=PACK, j=PACK)
             src = x_raw[o][:].rearrange("p j (m t) -> p m t j", t=PACK)
-            share = VECTOR_SHARE[o]
-            nc.vector.tensor_copy(dst[:, :share], src[:, :share])
-            nc.scalar.copy(dst[:, share:], src[:, share:])
+            nc.vector.tensor_copy(dst[:, :VECTOR_SHARE], src[:, :VECTOR_SHARE])
+            nc.scalar.copy(dst[:, VECTOR_SHARE:], src[:, VECTOR_SHARE:])
             codes = keep.tile([P, R], U32, name=f"x_codes{o}", tag=f"x_codes{o}", align_bytes=64)
             plane = keep.tile([P, R], U8, name=f"x_plane{o}", align_bytes=64)
             for c in range(0, R, P):
@@ -106,53 +119,57 @@ def tile_attend_glse_w_kernel(tc, xT, w_words, w_scales, y, lse, wt, xm, offs, o
             x_codes.append(codes)
             x_planes.append(plane)
 
-        scores = [psum.tile([P, N], F32, name=f"scores{t}") for t in range(PACK)]
+        scores = [[psum.tile([P, HALF], F32, name=f"scores{h}{t}", tag=f"bank{h}{t}") for t in range(PACK)] for h in range(2)]
         for o in range(PASSES):
-            for t in range(PACK):
-                rows = slice(t * P, (t + 1) * P)
-                nc.tensor.matmul_mx(
-                    out=scores[t][:],
-                    lhsT=x_codes[o][:, rows].bitcast(E4M3),
-                    lhsT_scale=x_planes[o][:, rows],
-                    rhs=w_codes[:, o, :].bitcast(E2M1),
-                    rhs_scale=w_planes[:, o, :],
-                    start=(o == 0),
-                    stop=(o == PASSES - 1),
-                )
+            for h in range(2):
+                for t in range(PACK):
+                    rows = slice(t * P, (t + 1) * P)
+                    for c in range(0, HALF, P):
+                        slots = slice(h * HALF + c, h * HALF + c + P)
+                        nc.tensor.matmul_mx(
+                            out=scores[h][t][:, c : c + P],
+                            lhsT=x_codes[o][:, rows].bitcast(E4M3),
+                            lhsT_scale=x_planes[o][:, rows],
+                            rhs=w_codes[:, o, slots].bitcast(E2M1),
+                            rhs_scale=w_planes[:, o, slots],
+                            start=(o == 0 and c == 0),
+                            stop=(o == PASSES - 1 and c == HALF - P),
+                        )
 
-        xm_rows = xm[0].rearrange("(p j) d -> p j d", j=PACK)
-        xm_raw = {}
-        for first, last, tag in XM_CHUNKS:
-            raw = keep.tile([P, PACK, (last - first) * P], F32, name=f"xm_raw{first}", tag=tag)
-            nc.sync.dma_start(raw[:], xm_rows[:, :, first * P : last * P])
-            for b in range(first, last):
-                xm_raw[b] = raw[:, :, (b - first) * P : (b - first + 1) * P]
+        load_xm(2, 4, "x_raw0")
+        load_xm(4, BLOCKS, "scale_window")
 
         probs = [keep.tile([P, PACK, HALF], F32, name=f"probs{h}", tag=f"probs{h}", align_bytes=64) for h in range(2)]
-        y_wt, g_rows = {}, {}
+        g_rows = [keep.tile([P, PACK, HALF], BF16, name=f"g_rows{h}", tag=f"g_rows{h}") for h in range(2)]
+        y_wt = keep.tile([P, PACK, HALF], F32, name="y_wt")
+        excess = keep.tile([P, PACK, HALF], F32, name="excess", tag="excess", align_bytes=64)
         xm_codes = keep.tile([P, D], U32, name="xm_codes", align_bytes=64)
         xm_plane = keep.tile([P, D], U8, name="xm_plane", align_bytes=64)
 
         def exponentiate(h, places):
             for t in places:
-                nc.scalar.activation(probs[h][:, t, :], scores[t][:, halves[h]], ACT.Exp, bias=neg_lse[:, t : t + 1])
+                nc.scalar.activation(probs[h][:, t, :], scores[h][t][:], ACT.Exp, bias=neg_lse[:, t : t + 1])
 
-        def weigh_targets(h, tag):
-            y_wt[h] = keep.tile([P, PACK, HALF], F32, name=f"y_wt{h}", tag=tag)
-            for t in range(PACK):
-                nc.vector.tensor_scalar(y_wt[h][:, t, :], y_sb[h][:, t, :], wt_sb[:, t : t + 1], None, ALU.mult)
-
-        def form_g(h):
-            g_rows[h] = keep.tile([P, PACK, HALF], BF16, name=f"g_rows{h}", tag=f"g_rows{h}")
+        def form_first_g():
+            for t in range(2, PACK):
+                nc.vector.tensor_scalar(y_wt[:, t, :], y_sb[0][:, t, :], wt_sb[:, t : t + 1], None, ALU.mult)
             for t in range(PACK):
                 nc.vector.scalar_tensor_tensor(
-                    g_rows[h][:, t, :],
-                    probs[h][:, t, :],
+                    g_rows[0][:, t, :],
+                    probs[0][:, t, :],
                     wt_sb[:, t : t + 1],
-                    y_wt[h][:, t, :],
+                    y_wt[:, t, :],
                     ALU.mult,
                     ALU.subtract,
                 )
+
+        def subtract_targets(places):
+            for t in places:
+                nc.vector.tensor_tensor(excess[:, t, :], probs[1][:, t, :], y_sb[1][:, t, :], ALU.subtract)
+
+        def weigh_excess(places):
+            for t in places:
+                nc.scalar.activation(g_rows[1][:, t, :], excess[:, t, :], ACT.Copy, scale=wt_sb[:, t : t + 1])
 
         def interleave_g(h, copy):
             grouped = keep.tile([P, HALF * PACK], BF16, name=f"g_grouped{h}", tag=f"g_grouped{h}", align_bytes=64)
@@ -181,9 +198,12 @@ def tile_attend_glse_w_kernel(tc, xT, w_words, w_scales, y, lse, wt, xm, offs, o
                 in_=grouped[:],
             )
 
+        products = []
+
         def multiply(b):
             cols = slice(b * P, (b + 1) * P)
-            grad = psum.tile([P, N], F32, name="grad", bufs=4)
+            grad = psum.tile([P, N], F32, name="grad", tag=f"bank0{len(products) % PACK}")
+            products.append(grad)
             nc.tensor.matmul_mx(
                 out=grad[:],
                 lhsT=xm_codes[:, cols].bitcast(E4M3),
@@ -198,37 +218,43 @@ def tile_attend_glse_w_kernel(tc, xT, w_words, w_scales, y, lse, wt, xm, offs, o
         def scatter(b, grad, slots, dense):
             nc.scalar.copy(dense[:], grad[:, slots])
             entries = offsets[:, slots.start // 16 : slots.stop // 16]
-            nc.vector.tensor_copy(windows[b % 3][:].indirect(entries), dense[:])
+            nc.vector.tensor_copy(windows[b % WINDOWS][:].indirect(entries), dense[:])
 
         def store(b):
-            nc.sync.dma_start(out[b * P : (b + 1) * P, :], windows[b % 3][:])
+            nc.sync.dma_start(out[b * P : (b + 1) * P, :], windows[b % WINDOWS][:])
 
 
+        def dense_tile(name, width, tag):
+            return keep.tile([P, width], F32, name=name, tag=tag, align_bytes=64)
+
+        for t in range(2):
+            nc.scalar.activation(y_wt[:, t, :], y_sb[0][:, t, :], ACT.Copy, scale=wt_sb[:, t : t + 1])
         exponentiate(0, range(PACK))
-        weigh_targets(0, "y_wt0")
-        form_g(0)
+        form_first_g()
         first_g = interleave_g(0, nc.vector.tensor_copy)
-        exponentiate(1, range(2))
         quantise_xm(0, 1, cast_xm(0, 1, "x_codes1"))
         quantise_g(0, first_g)
         early = [multiply(0)]
-        exponentiate(1, range(2, PACK))
-        weigh_targets(1, "g_rows0")
-        form_g(1)
-        scatter(0, early[0], halves[0], keep.tile([P, HALF], F32, name="dense_first"))
-        quantise_xm(1, 2, cast_xm(1, 2, "g_grouped0"))
+        exponentiate(1, range(2))
+        subtract_targets(range(2))
+        quantise_xm(1, 2, cast_xm(1, 2, "x_codes0"))
         early.append(multiply(1))
+        scatter(0, early[0], halves[0], dense_tile("dense_early0", HALF, "dense_early0"))
+        exponentiate(1, range(2, PACK))
+        subtract_targets(range(2, PACK))
+        weigh_excess(range(2))
+        quantise_xm(2, 3, cast_xm(2, 3, "g_grouped0"))
+        early.append(multiply(2))
+        scatter(1, early[1], halves[0], dense_tile("dense_early1", HALF, "dense_early1"))
+        weigh_excess(range(2, PACK))
         quantise_g(1, interleave_g(1, nc.scalar.copy))
-        scatter(1, early[1], halves[0], keep.tile([P, HALF], F32, name="dense_second", tag="g_rows1"))
-        quantise_xm(2, 4, cast_xm(2, 4, "probs1"))
-        for b, tag in enumerate(("dense_third", "probs1")):
-            scatter(b, multiply(b), halves[1], keep.tile([P, HALF], F32, name=f"dense_late{b}", tag=tag, align_bytes=64))
+        scatter(2, early[2], halves[0], keep.tile([P, HALF], F32, name="dense_early2", tag="g_rows1"))
+        quantise_xm(3, 4, cast_xm(3, 4, "excess"))
+        for b, tag in enumerate(("dense_early0", "dense_early1", "excess")):
+            scatter(b, multiply(b), halves[1], dense_tile(f"dense_late{b}", HALF, tag))
             store(b)
         quantise_xm(4, BLOCKS, cast_xm(4, BLOCKS, "g_grouped1"))
-        for b in range(2, BLOCKS):
-            if b == 3:
-                dense = keep.tile([P, N], F32, name="dense_held", tag="g_grouped1", align_bytes=64)
-            else:
-                dense = ring.tile([P, N], F32, name="dense")
+        for b in range(EARLY, BLOCKS):
+            dense = dense_tile("dense_held", N, "g_grouped1") if b == EARLY else ring.tile([P, N], F32, name="dense")
             scatter(b, multiply(b), slice(0, N), dense)
             store(b)

@@ -24,8 +24,9 @@ ALU = mybir.AluOpType
 
 VECTOR_SHARE = 84
 SCALE_FIRST = P - 16 * PASSES
+ODD_CUTS = (0, 511, 1024, 1535, T)
 WINDOWS = 4
-EARLY = 3
+EARLY = 4
 
 
 def tile_attend_glse_w_kernel(tc, xT, w_words, w_scales, y, lse, wt, xm, offs, out):
@@ -38,7 +39,7 @@ def tile_attend_glse_w_kernel(tc, xT, w_words, w_scales, y, lse, wt, xm, offs, o
 
         offsets = keep.tile([P, N // 16], U16, name="offsets")
         nc.sync.dma_start(offsets[:], offs)
-        scale_tile = keep.tile([P, T + 4], U8, name="scale_tile", tag="scale_window")
+        scale_tile = keep.tile([P, T + 4], U8, name="scale_tile", tag="scale_window", align_bytes=64)
         nc.scalar.dma_start(
             scale_tile[SCALE_FIRST:, :T].bitcast(I32), w_scales.rearrange("o f t -> f o t").bitcast(I32)
         )
@@ -50,7 +51,7 @@ def tile_attend_glse_w_kernel(tc, xT, w_words, w_scales, y, lse, wt, xm, offs, o
         nc.scalar.dma_start(wt_sb[:], wt[0].rearrange("(p j) o -> p (j o)", j=PACK))
 
         def load_x(o, tag):
-            raw = keep.tile([P, PACK, R], F32, name=f"x_raw{o}", tag=tag)
+            raw = keep.tile([P, PACK, R], F32, name=f"x_raw{o}", tag=tag, align_bytes=64)
             nc.sync.dma_start(raw[:], xT[0, o * 512 : (o + 1) * 512, :].rearrange("(p j) r -> p j r", j=PACK))
             return raw
 
@@ -62,8 +63,6 @@ def tile_attend_glse_w_kernel(tc, xT, w_words, w_scales, y, lse, wt, xm, offs, o
         nc.gpsimd.memset(g_codes[:, HALF:].bitcast(I32), 0)
         nc.gpsimd.memset(g_plane[:, HALF:].bitcast(I32), 0)
         windows = [keep.tile([P, T], F32, name=f"out_window{i}") for i in range(WINDOWS)]
-        for cols in (slice(0, T // 2 - 1), slice(T // 2 - 1, T)):
-            nc.vector.memset(windows[0][:, cols].bitcast(I32), 0)
         for win in windows[1:]:
             nc.gpsimd.memset(win[:].bitcast(I32), 0)
         neg_lse = keep.tile([P, PACK], F32, name="neg_lse")
@@ -78,10 +77,13 @@ def tile_attend_glse_w_kernel(tc, xT, w_words, w_scales, y, lse, wt, xm, offs, o
                 scale_rows[SCALE_FIRST + 8 * q : SCALE_FIRST + 8 * q + 8, :].bitcast(I32),
             )
         x_raw.append(load_x(1, "scale_window"))
-        w_pairs = keep.tile([P, N], U32, name="w_pairs", tag="w_pairs")
+        w_pairs = keep.tile([P, N], U32, name="w_pairs", tag="w_pairs", align_bytes=64)
         nc.vector.tensor_copy(w_pairs[:], word_window[:].indirect(offsets[:]))
         w_codes = keep.tile([P, PASSES, N], U16, name="w_codes", align_bytes=64)
         nc.vector.tensor_copy(w_codes[:], w_pairs[:].bitcast(U16).rearrange("p (s o) -> p o s", o=PASSES))
+
+        for first, last in zip(ODD_CUTS, ODD_CUTS[1:]):
+            nc.vector.memset(windows[0][:, first:last].bitcast(I32), 0)
 
         y_rows = y[0].rearrange("(p j) s -> p j s", j=PACK)
         xm_rows = xm[0].rearrange("(p j) d -> p j d", j=PACK)
@@ -92,7 +94,7 @@ def tile_attend_glse_w_kernel(tc, xT, w_words, w_scales, y, lse, wt, xm, offs, o
             nc.sync.dma_start(y_sb[h][:], y_rows[:, :, halves[h]])
 
         def load_xm(first, last, tag):
-            raw = keep.tile([P, PACK, (last - first) * P], F32, name=f"xm_raw{first}", tag=tag)
+            raw = keep.tile([P, PACK, (last - first) * P], F32, name=f"xm_raw{first}", tag=tag, align_bytes=64)
             nc.sync.dma_start(raw[:], xm_rows[:, :, first * P : last * P])
             for b in range(first, last):
                 xm_raw[b] = raw[:, :, (b - first) * P : (b - first + 1) * P]
@@ -103,7 +105,7 @@ def tile_attend_glse_w_kernel(tc, xT, w_words, w_scales, y, lse, wt, xm, offs, o
 
         x_codes, x_planes = [], []
         for o in range(PASSES):
-            grouped = keep.tile([P, R * PACK], BF16, name=f"x_grouped{o}", align_bytes=64)
+            grouped = keep.tile([P, R * PACK], BF16, name=f"x_grouped{o}", tag=f"x_grouped{o}", align_bytes=64)
             dst = grouped[:].rearrange("p (t m j) -> p m t j", t=PACK, j=PACK)
             src = x_raw[o][:].rearrange("p j (m t) -> p m t j", t=PACK)
             nc.vector.tensor_copy(dst[:, :VECTOR_SHARE], src[:, :VECTOR_SHARE])
@@ -119,36 +121,41 @@ def tile_attend_glse_w_kernel(tc, xT, w_words, w_scales, y, lse, wt, xm, offs, o
             x_codes.append(codes)
             x_planes.append(plane)
 
-        scores = [[psum.tile([P, HALF], F32, name=f"scores{h}{t}", tag=f"bank{h}{t}") for t in range(PACK)] for h in range(2)]
+        scores = {}
+
+        def score(h, o, t):
+            if o == 0:
+                scores[h, t] = psum.tile([P, HALF], F32, name=f"scores{h}{t}", tag=f"score_bank{t}")
+            rows = slice(t * P, (t + 1) * P)
+            for c in range(0, HALF, P):
+                slots = slice(h * HALF + c, h * HALF + c + P)
+                nc.tensor.matmul_mx(
+                    out=scores[h, t][:, c : c + P],
+                    lhsT=x_codes[o][:, rows].bitcast(E4M3),
+                    lhsT_scale=x_planes[o][:, rows],
+                    rhs=w_codes[:, o, slots].bitcast(E2M1),
+                    rhs_scale=w_planes[:, o, slots],
+                    start=(o == 0 and c == 0),
+                    stop=(o == PASSES - 1 and c == HALF - P),
+                )
+
         for o in range(PASSES):
-            for h in range(2):
-                for t in range(PACK):
-                    rows = slice(t * P, (t + 1) * P)
-                    for c in range(0, HALF, P):
-                        slots = slice(h * HALF + c, h * HALF + c + P)
-                        nc.tensor.matmul_mx(
-                            out=scores[h][t][:, c : c + P],
-                            lhsT=x_codes[o][:, rows].bitcast(E4M3),
-                            lhsT_scale=x_planes[o][:, rows],
-                            rhs=w_codes[:, o, slots].bitcast(E2M1),
-                            rhs_scale=w_planes[:, o, slots],
-                            start=(o == 0 and c == 0),
-                            stop=(o == PASSES - 1 and c == HALF - P),
-                        )
+            for t in range(PACK):
+                score(0, o, t)
 
         load_xm(2, 4, "x_raw0")
         load_xm(4, BLOCKS, "scale_window")
 
         probs = [keep.tile([P, PACK, HALF], F32, name=f"probs{h}", tag=f"probs{h}", align_bytes=64) for h in range(2)]
         g_rows = [keep.tile([P, PACK, HALF], BF16, name=f"g_rows{h}", tag=f"g_rows{h}") for h in range(2)]
-        y_wt = keep.tile([P, PACK, HALF], F32, name="y_wt")
+        y_wt = keep.tile([P, PACK, HALF], F32, name="y_wt", tag="y_wt", align_bytes=64)
         excess = keep.tile([P, PACK, HALF], F32, name="excess", tag="excess", align_bytes=64)
         xm_codes = keep.tile([P, D], U32, name="xm_codes", align_bytes=64)
         xm_plane = keep.tile([P, D], U8, name="xm_plane", align_bytes=64)
 
         def exponentiate(h, places):
             for t in places:
-                nc.scalar.activation(probs[h][:, t, :], scores[h][t][:], ACT.Exp, bias=neg_lse[:, t : t + 1])
+                nc.scalar.activation(probs[h][:, t, :], scores[h, t][:], ACT.Exp, bias=neg_lse[:, t : t + 1])
 
         def form_first_g():
             for t in range(2, PACK):
@@ -198,12 +205,9 @@ def tile_attend_glse_w_kernel(tc, xT, w_words, w_scales, y, lse, wt, xm, offs, o
                 in_=grouped[:],
             )
 
-        products = []
-
         def multiply(b):
             cols = slice(b * P, (b + 1) * P)
-            grad = psum.tile([P, N], F32, name="grad", tag=f"bank0{len(products) % PACK}")
-            products.append(grad)
+            grad = psum.tile([P, N], F32, name="grad", bufs=4)
             nc.tensor.matmul_mx(
                 out=grad[:],
                 lhsT=xm_codes[:, cols].bitcast(E4M3),
@@ -221,7 +225,12 @@ def tile_attend_glse_w_kernel(tc, xT, w_words, w_scales, y, lse, wt, xm, offs, o
             nc.vector.tensor_copy(windows[b % WINDOWS][:].indirect(entries), dense[:])
 
         def store(b):
-            nc.sync.dma_start(out[b * P : (b + 1) * P, :], windows[b % WINDOWS][:])
+            rows = slice(b * P, (b + 1) * P)
+            if b < BLOCKS - 1:
+                nc.sync.dma_start(out[rows, :], windows[b % WINDOWS][:])
+            else:
+                nc.sync.dma_start(out[rows, : T // 2], windows[b % WINDOWS][:, : T // 2])
+                nc.scalar.dma_start(out[rows, T // 2 :], windows[b % WINDOWS][:, T // 2 :])
 
 
         def dense_tile(name, width, tag):
@@ -230,14 +239,17 @@ def tile_attend_glse_w_kernel(tc, xT, w_words, w_scales, y, lse, wt, xm, offs, o
         for t in range(2):
             nc.scalar.activation(y_wt[:, t, :], y_sb[0][:, t, :], ACT.Copy, scale=wt_sb[:, t : t + 1])
         exponentiate(0, range(PACK))
+        for t in range(PACK):
+            for o in range(PASSES):
+                score(1, o, t)
         form_first_g()
         first_g = interleave_g(0, nc.vector.tensor_copy)
-        quantise_xm(0, 1, cast_xm(0, 1, "x_codes1"))
+        quantise_xm(0, 1, cast_xm(0, 1, "x_grouped1"))
         quantise_g(0, first_g)
         early = [multiply(0)]
         exponentiate(1, range(2))
         subtract_targets(range(2))
-        quantise_xm(1, 2, cast_xm(1, 2, "x_codes0"))
+        quantise_xm(1, 2, cast_xm(1, 2, "y_wt"))
         early.append(multiply(1))
         scatter(0, early[0], halves[0], dense_tile("dense_early0", HALF, "dense_early0"))
         exponentiate(1, range(2, PACK))
@@ -246,15 +258,16 @@ def tile_attend_glse_w_kernel(tc, xT, w_words, w_scales, y, lse, wt, xm, offs, o
         quantise_xm(2, 3, cast_xm(2, 3, "g_grouped0"))
         early.append(multiply(2))
         scatter(1, early[1], halves[0], dense_tile("dense_early1", HALF, "dense_early1"))
+        quantise_xm(3, 4, cast_xm(3, 4, "g_grouped0"))
+        early.append(multiply(3))
+        scatter(2, early[2], halves[0], dense_tile("dense_early2", HALF, "x_raw0"))
         weigh_excess(range(2, PACK))
         quantise_g(1, interleave_g(1, nc.scalar.copy))
-        scatter(2, early[2], halves[0], keep.tile([P, HALF], F32, name="dense_early2", tag="g_rows1"))
-        quantise_xm(3, 4, cast_xm(3, 4, "excess"))
-        for b, tag in enumerate(("dense_early0", "dense_early1", "excess")):
+        scatter(3, early[3], halves[0], keep.tile([P, HALF], F32, name="dense_early3", tag="g_rows1"))
+        quantise_xm(EARLY, BLOCKS, cast_xm(EARLY, BLOCKS, "g_grouped1"))
+        for b, tag in enumerate(("dense_early0", "dense_early1", "scale_window", "x_raw0")):
             scatter(b, multiply(b), halves[1], dense_tile(f"dense_late{b}", HALF, tag))
             store(b)
-        quantise_xm(4, BLOCKS, cast_xm(4, BLOCKS, "g_grouped1"))
         for b in range(EARLY, BLOCKS):
-            dense = dense_tile("dense_held", N, "g_grouped1") if b == EARLY else ring.tile([P, N], F32, name="dense")
-            scatter(b, multiply(b), slice(0, N), dense)
+            scatter(b, multiply(b), slice(0, N), ring.tile([P, N], F32, name="dense"))
             store(b)

@@ -25,6 +25,8 @@ ALU = mybir.AluOpType
 VECTOR_SHARE = 84
 SCALE_FIRST = P - 16 * PASSES
 ODD_CUTS = (0, 511, 1024, 1535, T)
+LAST_CUTS = (0, 223, 448)
+QUANTISE_WIDTH = (R, P)
 WINDOWS = 4
 EARLY = 4
 
@@ -60,11 +62,10 @@ def tile_attend_glse_w_kernel(tc, xT, w_words, w_scales, y, lse, wt, xm, offs, o
         nc.vector.memset(scale_tile[:SCALE_FIRST, :].bitcast(I32), 0)
         g_codes = keep.tile([P, N], U32, name="g_codes", align_bytes=64)
         g_plane = keep.tile([P, N], U8, name="g_plane", align_bytes=64)
-        nc.gpsimd.memset(g_codes[:, HALF:].bitcast(I32), 0)
-        nc.gpsimd.memset(g_plane[:, HALF:].bitcast(I32), 0)
         windows = [keep.tile([P, T], F32, name=f"out_window{i}") for i in range(WINDOWS)]
-        for win in windows[1:]:
+        for win in windows[1:-1]:
             nc.gpsimd.memset(win[:].bitcast(I32), 0)
+        nc.gpsimd.memset(windows[-1][:, LAST_CUTS[-1] :].bitcast(I32), 0)
         neg_lse = keep.tile([P, PACK], F32, name="neg_lse")
         nc.scalar.activation(neg_lse[:], lse_sb[:], ACT.Copy, scale=-1.0)
 
@@ -84,6 +85,10 @@ def tile_attend_glse_w_kernel(tc, xT, w_words, w_scales, y, lse, wt, xm, offs, o
 
         for first, last in zip(ODD_CUTS, ODD_CUTS[1:]):
             nc.vector.memset(windows[0][:, first:last].bitcast(I32), 0)
+        for first, last in zip(LAST_CUTS, LAST_CUTS[1:]):
+            nc.vector.memset(windows[-1][:, first:last].bitcast(I32), 0)
+        nc.vector.memset(g_codes[:, HALF - 1 :].bitcast(I32), 0)
+        nc.vector.memset(g_plane[:, HALF - 4 :].bitcast(I32), 0)
 
         y_rows = y[0].rearrange("(p j) s -> p j s", j=PACK)
         xm_rows = xm[0].rearrange("(p j) d -> p j d", j=PACK)
@@ -112,11 +117,12 @@ def tile_attend_glse_w_kernel(tc, xT, w_words, w_scales, y, lse, wt, xm, offs, o
             nc.scalar.copy(dst[:, VECTOR_SHARE:], src[:, VECTOR_SHARE:])
             codes = keep.tile([P, R], U32, name=f"x_codes{o}", tag=f"x_codes{o}", align_bytes=64)
             plane = keep.tile([P, R], U8, name=f"x_plane{o}", align_bytes=64)
-            for c in range(0, R, P):
+            width = QUANTISE_WIDTH[o]
+            for c in range(0, R, width):
                 nc.vector.quantize_mx(
-                    out=codes[:, c : c + P].bitcast(E4M3),
-                    scales=plane[:, c : c + P],
-                    in_=grouped[:, PACK * c : PACK * (c + P)],
+                    out=codes[:, c : c + width].bitcast(E4M3),
+                    scales=plane[:, c : c + width],
+                    in_=grouped[:, PACK * c : PACK * (c + width)],
                 )
             x_codes.append(codes)
             x_planes.append(plane)
@@ -264,8 +270,9 @@ def tile_attend_glse_w_kernel(tc, xT, w_words, w_scales, y, lse, wt, xm, offs, o
         weigh_excess(range(2, PACK))
         quantise_g(1, interleave_g(1, nc.scalar.copy))
         scatter(3, early[3], halves[0], keep.tile([P, HALF], F32, name="dense_early3", tag="g_rows1"))
-        quantise_xm(EARLY, BLOCKS, cast_xm(EARLY, BLOCKS, "g_grouped1"))
-        for b, tag in enumerate(("dense_early0", "dense_early1", "scale_window", "x_raw0")):
+        for b, tag in enumerate(("dense_early0", "dense_early1", "x_raw0", "scale_window")):
+            if b == EARLY - 1:
+                quantise_xm(EARLY, BLOCKS, cast_xm(EARLY, BLOCKS, "g_grouped1"))
             scatter(b, multiply(b), halves[1], dense_tile(f"dense_late{b}", HALF, tag))
             store(b)
         for b in range(EARLY, BLOCKS):

@@ -24,8 +24,7 @@ ALU = mybir.AluOpType
 
 VECTOR_SHARE = 84
 SCALE_FIRST = P - 16 * PASSES
-ODD_CUTS = (0, 511, 1024, 1535, T)
-LAST_CUTS = (0, 223, 448)
+VECTOR_ZEROES = 384
 QUANTISE_WIDTH = (R, P)
 WINDOWS = 4
 EARLY = 4
@@ -41,9 +40,9 @@ def tile_attend_glse_w_kernel(tc, xT, w_words, w_scales, y, lse, wt, xm, offs, o
 
         offsets = keep.tile([P, N // 16], U16, name="offsets")
         nc.sync.dma_start(offsets[:], offs)
-        scale_tile = keep.tile([P, T + 4], U8, name="scale_tile", tag="scale_window", align_bytes=64)
+        scale_window = keep.tile([P, T], U8, name="scale_window", tag="scale_window", align_bytes=64)
         nc.scalar.dma_start(
-            scale_tile[SCALE_FIRST:, :T].bitcast(I32), w_scales.rearrange("o f t -> f o t").bitcast(I32)
+            scale_window[SCALE_FIRST:, :].bitcast(I32), w_scales.rearrange("o f t -> f o t").bitcast(I32)
         )
         word_window = keep.tile([P, T], U32, name="word_window", tag="word_window")
         nc.sync.dma_start(word_window[:].bitcast(I32), w_words[0].rearrange("p n b -> p (n b)").bitcast(I32))
@@ -59,18 +58,23 @@ def tile_attend_glse_w_kernel(tc, xT, w_words, w_scales, y, lse, wt, xm, offs, o
 
         x_raw = [load_x(0, "x_raw0")]
 
-        nc.vector.memset(scale_tile[:SCALE_FIRST, :].bitcast(I32), 0)
+        def zero_in_odd_pieces(words):
+            middle = words.shape[1] // 2 - 1
+            nc.vector.memset(words[:, :middle], 0)
+            nc.vector.memset(words[:, middle:], 0)
+
+        zero_in_odd_pieces(scale_window[:SCALE_FIRST, :].bitcast(I32))
         g_codes = keep.tile([P, N], U32, name="g_codes", align_bytes=64)
         g_plane = keep.tile([P, N], U8, name="g_plane", align_bytes=64)
         windows = [keep.tile([P, T], F32, name=f"out_window{i}") for i in range(WINDOWS)]
         for win in windows[1:-1]:
             nc.gpsimd.memset(win[:].bitcast(I32), 0)
-        nc.gpsimd.memset(windows[-1][:, LAST_CUTS[-1] :].bitcast(I32), 0)
+        nc.gpsimd.memset(windows[-1][:, VECTOR_ZEROES:].bitcast(I32), 0)
         neg_lse = keep.tile([P, PACK], F32, name="neg_lse")
         nc.scalar.activation(neg_lse[:], lse_sb[:], ACT.Copy, scale=-1.0)
 
         scale_rows = keep.tile([P, N], U8, name="scale_rows", tag="scale_rows")
-        nc.vector.tensor_copy(scale_rows[:], scale_tile[:, :T].indirect(offsets[:]))
+        nc.vector.tensor_copy(scale_rows[:], scale_window[:].indirect(offsets[:]))
         w_planes = keep.tile([P, PASSES, N], U8, name="w_planes", align_bytes=64)
         for q in range(4):
             nc.sync.dma_start(
@@ -83,20 +87,20 @@ def tile_attend_glse_w_kernel(tc, xT, w_words, w_scales, y, lse, wt, xm, offs, o
         w_codes = keep.tile([P, PASSES, N], U16, name="w_codes", align_bytes=64)
         nc.vector.tensor_copy(w_codes[:], w_pairs[:].bitcast(U16).rearrange("p (s o) -> p o s", o=PASSES))
 
-        for first, last in zip(ODD_CUTS, ODD_CUTS[1:]):
-            nc.vector.memset(windows[0][:, first:last].bitcast(I32), 0)
-        for first, last in zip(LAST_CUTS, LAST_CUTS[1:]):
-            nc.vector.memset(windows[-1][:, first:last].bitcast(I32), 0)
-        nc.vector.memset(g_codes[:, HALF - 1 :].bitcast(I32), 0)
-        nc.vector.memset(g_plane[:, HALF - 4 :].bitcast(I32), 0)
+        for cols in (slice(0, T // 2), slice(T // 2, T)):
+            zero_in_odd_pieces(windows[0][:, cols].bitcast(I32))
+        zero_in_odd_pieces(windows[-1][:, :VECTOR_ZEROES].bitcast(I32))
+        zero_in_odd_pieces(g_codes[:, HALF:].bitcast(I32))
+        zero_in_odd_pieces(g_plane[:, HALF:].bitcast(I32))
 
         y_rows = y[0].rearrange("(p j) s -> p j s", j=PACK)
         xm_rows = xm[0].rearrange("(p j) d -> p j d", j=PACK)
         y_sb, xm_raw = {}, {}
 
-        def load_y(h, tag):
+        def load_y(h, tag, places):
             y_sb[h] = keep.tile([P, PACK, HALF], F32, name=f"y_sb{h}", tag=tag)
-            nc.sync.dma_start(y_sb[h][:], y_rows[:, :, halves[h]])
+            for first in range(0, PACK, places):
+                nc.sync.dma_start(y_sb[h][:, first : first + places, :], y_rows[:, first : first + places, halves[h]])
 
         def load_xm(first, last, tag):
             raw = keep.tile([P, PACK, (last - first) * P], F32, name=f"xm_raw{first}", tag=tag, align_bytes=64)
@@ -104,9 +108,9 @@ def tile_attend_glse_w_kernel(tc, xT, w_words, w_scales, y, lse, wt, xm, offs, o
             for b in range(first, last):
                 xm_raw[b] = raw[:, :, (b - first) * P : (b - first + 1) * P]
 
-        load_y(0, "word_window")
+        load_y(0, "word_window", 2)
         load_xm(0, 2, "w_pairs")
-        load_y(1, "scale_rows")
+        load_y(1, "scale_rows", PACK)
 
         x_codes, x_planes = [], []
         for o in range(PASSES):

@@ -44,7 +44,7 @@ def tile_attend_glse_w_kernel(tc, xT, w_words, w_scales, y, lse, wt, xm, offs, o
         nc.scalar.dma_start(
             scale_window[SCALE_FIRST:, :].bitcast(I32), w_scales.rearrange("o f t -> f o t").bitcast(I32)
         )
-        word_window = keep.tile([P, T], U32, name="word_window", tag="word_window")
+        word_window = keep.tile([P, T], U32, name="word_window", tag="word_window", align_bytes=64)
         nc.sync.dma_start(word_window[:].bitcast(I32), w_words[0].rearrange("p n b -> p (n b)").bitcast(I32))
         lse_sb = keep.tile([P, PACK], F32, name="lse_sb")
         wt_sb = keep.tile([P, PACK], F32, name="wt_sb")
@@ -73,7 +73,7 @@ def tile_attend_glse_w_kernel(tc, xT, w_words, w_scales, y, lse, wt, xm, offs, o
         neg_lse = keep.tile([P, PACK], F32, name="neg_lse")
         nc.scalar.activation(neg_lse[:], lse_sb[:], ACT.Copy, scale=-1.0)
 
-        scale_rows = keep.tile([P, N], U8, name="scale_rows", tag="scale_rows")
+        scale_rows = keep.tile([P, N], U8, name="scale_rows", tag="scale_rows", align_bytes=64)
         nc.vector.tensor_copy(scale_rows[:], scale_window[:].indirect(offsets[:]))
         w_planes = keep.tile([P, PASSES, N], U8, name="w_planes", align_bytes=64)
         for q in range(4):
@@ -98,7 +98,7 @@ def tile_attend_glse_w_kernel(tc, xT, w_words, w_scales, y, lse, wt, xm, offs, o
         y_sb, xm_raw = {}, {}
 
         def load_y(h, tag, places):
-            y_sb[h] = keep.tile([P, PACK, HALF], F32, name=f"y_sb{h}", tag=tag)
+            y_sb[h] = keep.tile([P, PACK, HALF], F32, name=f"y_sb{h}", tag=tag, align_bytes=64)
             for first in range(0, PACK, places):
                 nc.sync.dma_start(y_sb[h][:, first : first + places, :], y_rows[:, first : first + places, halves[h]])
 
@@ -110,7 +110,7 @@ def tile_attend_glse_w_kernel(tc, xT, w_words, w_scales, y, lse, wt, xm, offs, o
 
         load_y(0, "word_window", 2)
         load_xm(0, 2, "w_pairs")
-        load_y(1, "scale_rows", PACK)
+        load_xm(2, 4, "scale_rows")
 
         x_codes, x_planes = [], []
         for o in range(PASSES):
@@ -153,13 +153,12 @@ def tile_attend_glse_w_kernel(tc, xT, w_words, w_scales, y, lse, wt, xm, offs, o
             for t in range(PACK):
                 score(0, o, t)
 
-        load_xm(2, 4, "x_raw0")
+        load_y(1, "x_raw0", PACK)
         load_xm(4, BLOCKS, "scale_window")
 
         probs = [keep.tile([P, PACK, HALF], F32, name=f"probs{h}", tag=f"probs{h}", align_bytes=64) for h in range(2)]
-        g_rows = [keep.tile([P, PACK, HALF], BF16, name=f"g_rows{h}", tag=f"g_rows{h}") for h in range(2)]
+        g_rows = [keep.tile([P, PACK, HALF], BF16, name=f"g_rows{h}", tag=f"g_rows{h}", align_bytes=64) for h in range(2)]
         y_wt = keep.tile([P, PACK, HALF], F32, name="y_wt", tag="y_wt", align_bytes=64)
-        excess = keep.tile([P, PACK, HALF], F32, name="excess", tag="excess", align_bytes=64)
         xm_codes = keep.tile([P, D], U32, name="xm_codes", align_bytes=64)
         xm_plane = keep.tile([P, D], U8, name="xm_plane", align_bytes=64)
 
@@ -180,29 +179,34 @@ def tile_attend_glse_w_kernel(tc, xT, w_words, w_scales, y, lse, wt, xm, offs, o
                     ALU.subtract,
                 )
 
-        def subtract_targets(places):
-            for t in places:
-                nc.vector.tensor_tensor(excess[:, t, :], probs[1][:, t, :], y_sb[1][:, t, :], ALU.subtract)
+        g_grouped = [
+            keep.tile([P, HALF * PACK], BF16, name=f"g_grouped{h}", tag=f"g_grouped{h}", align_bytes=64) for h in range(2)
+        ]
 
-        def weigh_excess(places):
-            for t in places:
-                nc.scalar.activation(g_rows[1][:, t, :], excess[:, t, :], ACT.Copy, scale=wt_sb[:, t : t + 1])
-
-        def interleave_g(h, copy):
-            grouped = keep.tile([P, HALF * PACK], BF16, name=f"g_grouped{h}", tag=f"g_grouped{h}", align_bytes=64)
+        def interleave_g(h, cols, copy):
             copy(
-                grouped[:].rearrange("p (c i t) -> p c t i", i=4, t=PACK),
-                g_rows[h][:].rearrange("p t (c i) -> p c t i", i=4),
+                g_grouped[h][:, PACK * cols.start : PACK * cols.stop].rearrange("p (c i t) -> p c t i", i=4, t=PACK),
+                g_rows[h][:, :, cols].rearrange("p t (c i) -> p c t i", i=4),
             )
-            return grouped
 
-        def quantise_g(h, grouped):
-            nc.vector.quantize_mx(out=g_codes[:, halves[h]].bitcast(E5M2), scales=g_plane[:, halves[h]], in_=grouped[:])
+        def form_second_g(excess):
+            for cols in (slice(0, HALF // 2), slice(HALF // 2, HALF)):
+                nc.gpsimd.tensor_tensor(excess[:, :, cols], probs[1][:, :, cols], y_sb[1][:, :, cols], ALU.subtract)
+                for t in range(PACK):
+                    nc.scalar.activation(
+                        g_rows[1][:, t, cols], excess[:, t, cols], ACT.Copy, scale=wt_sb[:, t : t + 1]
+                    )
+                interleave_g(1, cols, nc.scalar.copy)
 
-        def cast_xm(first, last, tag):
+        def quantise_g(h):
+            nc.vector.quantize_mx(
+                out=g_codes[:, halves[h]].bitcast(E5M2), scales=g_plane[:, halves[h]], in_=g_grouped[h][:]
+            )
+
+        def cast_xm(first, last, tag, copy):
             grouped = keep.tile([P, (last - first) * P * PACK], BF16, name=f"xm_grouped{first}", tag=tag, align_bytes=64)
             for b in range(first, last):
-                nc.scalar.copy(
+                copy(
                     grouped[:, (b - first) * P * PACK : (b - first + 1) * P * PACK].rearrange("p (c i j) -> p c j i", i=4, j=PACK),
                     xm_raw[b].rearrange("p j (c i) -> p c j i", i=4),
                 )
@@ -253,30 +257,26 @@ def tile_attend_glse_w_kernel(tc, xT, w_words, w_scales, y, lse, wt, xm, offs, o
             for o in range(PASSES):
                 score(1, o, t)
         form_first_g()
-        first_g = interleave_g(0, nc.vector.tensor_copy)
-        quantise_xm(0, 1, cast_xm(0, 1, "x_grouped1"))
-        quantise_g(0, first_g)
+        interleave_g(0, slice(0, HALF), nc.vector.tensor_copy)
+        quantise_xm(0, 1, cast_xm(0, 1, "x_grouped1", nc.scalar.copy))
+        second_xm = cast_xm(1, 2, "x_grouped0", nc.scalar.copy)
+        quantise_g(0)
         early = [multiply(0)]
-        exponentiate(1, range(2))
-        subtract_targets(range(2))
-        quantise_xm(1, 2, cast_xm(1, 2, "y_wt"))
+        exponentiate(1, range(PACK))
+        later_xm = cast_xm(2, EARLY, "g_rows0", nc.vector.tensor_copy)
+        quantise_xm(1, 2, second_xm)
         early.append(multiply(1))
-        scatter(0, early[0], halves[0], dense_tile("dense_early0", HALF, "dense_early0"))
-        exponentiate(1, range(2, PACK))
-        subtract_targets(range(2, PACK))
-        weigh_excess(range(2))
-        quantise_xm(2, 3, cast_xm(2, 3, "g_grouped0"))
-        early.append(multiply(2))
-        scatter(1, early[1], halves[0], dense_tile("dense_early1", HALF, "dense_early1"))
-        quantise_xm(3, 4, cast_xm(3, 4, "g_grouped0"))
-        early.append(multiply(3))
-        scatter(2, early[2], halves[0], dense_tile("dense_early2", HALF, "x_raw0"))
-        weigh_excess(range(2, PACK))
-        quantise_g(1, interleave_g(1, nc.scalar.copy))
-        scatter(3, early[3], halves[0], keep.tile([P, HALF], F32, name="dense_early3", tag="g_rows1"))
-        for b, tag in enumerate(("dense_early0", "dense_early1", "x_raw0", "scale_window")):
-            if b == EARLY - 1:
-                quantise_xm(EARLY, BLOCKS, cast_xm(EARLY, BLOCKS, "g_grouped1"))
+        quantise_xm(2, EARLY, later_xm)
+        early.extend(multiply(b) for b in range(2, EARLY))
+        excess = keep.tile([P, PACK, HALF], F32, name="excess", tag="g_rows0", align_bytes=64)
+        for b in range(EARLY - 1):
+            scatter(b, early[b], halves[0], dense_tile(f"dense_early{b}", HALF, f"dense_early{b}"))
+        form_second_g(excess)
+        quantise_g(1)
+        scatter(3, early[3], halves[0], dense_tile("dense_early3", HALF, "g_rows1"))
+        for b, tag in enumerate(("dense_early0", "dense_early1", "scale_window", "dense_early2")):
+            if b == EARLY - 2:
+                quantise_xm(EARLY, BLOCKS, cast_xm(EARLY, BLOCKS, "g_grouped1", nc.scalar.copy))
             scatter(b, multiply(b), halves[1], dense_tile(f"dense_late{b}", HALF, tag))
             store(b)
         for b in range(EARLY, BLOCKS):

@@ -25,7 +25,7 @@ ALU = mybir.AluOpType
 VECTOR_SHARE = 84
 SCALE_FIRST = P - 16 * PASSES
 VECTOR_ZEROES = 384
-QUANTISE_WIDTH = (R, P)
+VECTOR_PAIR_SHARE = 24
 WINDOWS = 4
 EARLY = 4
 
@@ -112,24 +112,30 @@ def tile_attend_glse_w_kernel(tc, xT, w_words, w_scales, y, lse, wt, xm, offs, o
         load_xm(0, 2, "w_pairs")
         load_xm(2, 4, "scale_rows")
 
-        x_codes, x_planes = [], []
-        for o in range(PASSES):
-            grouped = keep.tile([P, R * PACK], BF16, name=f"x_grouped{o}", tag=f"x_grouped{o}", align_bytes=64)
-            dst = grouped[:].rearrange("p (t m j) -> p m t j", t=PACK, j=PACK)
-            src = x_raw[o][:].rearrange("p j (m t) -> p m t j", t=PACK)
-            nc.vector.tensor_copy(dst[:, :VECTOR_SHARE], src[:, :VECTOR_SHARE])
-            nc.scalar.copy(dst[:, VECTOR_SHARE:], src[:, VECTOR_SHARE:])
-            codes = keep.tile([P, R], U32, name=f"x_codes{o}", tag=f"x_codes{o}", align_bytes=64)
-            plane = keep.tile([P, R], U8, name=f"x_plane{o}", align_bytes=64)
-            width = QUANTISE_WIDTH[o]
-            for c in range(0, R, width):
-                nc.vector.quantize_mx(
-                    out=codes[:, c : c + width].bitcast(E4M3),
-                    scales=plane[:, c : c + width],
-                    in_=grouped[:, PACK * c : PACK * (c + width)],
-                )
-            x_codes.append(codes)
-            x_planes.append(plane)
+        x_codes = [keep.tile([P, R], U32, name=f"x_codes{o}", align_bytes=64) for o in range(PASSES)]
+        x_planes = [keep.tile([P, R], U8, name=f"x_plane{o}", align_bytes=64) for o in range(PASSES)]
+
+        def quantise_x(o, first, last, grouped):
+            cols = slice(first * P, last * P)
+            nc.vector.quantize_mx(out=x_codes[o][:, cols].bitcast(E4M3), scales=x_planes[o][:, cols], in_=grouped)
+
+        grouped = keep.tile([P, R * PACK], BF16, name="x_grouped0", tag="x_grouped0", align_bytes=64)
+        dst = grouped[:].rearrange("p (t m j) -> p m t j", t=PACK, j=PACK)
+        src = x_raw[0][:].rearrange("p j (m t) -> p m t j", t=PACK)
+        nc.vector.tensor_copy(dst[:, :VECTOR_SHARE], src[:, :VECTOR_SHARE])
+        nc.scalar.copy(dst[:, VECTOR_SHARE:], src[:, VECTOR_SHARE:])
+        quantise_x(0, 0, PACK, grouped[:])
+
+        pairs = [
+            keep.tile([P, 2 * P * PACK], BF16, name=f"x_pair{u}", tag=f"x_pair{u}", align_bytes=64) for u in range(2)
+        ]
+        dst = [pair[:].rearrange("p (t m j) -> p m j t", t=2, j=PACK) for pair in pairs]
+        src = x_raw[1][:].rearrange("p j (m u t) -> p u m j t", u=2, t=2)
+        nc.vector.tensor_copy(dst[0], src[:, 0])
+        nc.scalar.copy(dst[1][:, VECTOR_PAIR_SHARE:], src[:, 1, VECTOR_PAIR_SHARE:])
+        nc.vector.tensor_copy(dst[1][:, :VECTOR_PAIR_SHARE], src[:, 1, :VECTOR_PAIR_SHARE])
+        for t in range(PACK):
+            quantise_x(1, t, t + 1, pairs[t // 2][:, (t % 2) * P * PACK : (t % 2 + 1) * P * PACK])
 
         scores = {}
 
@@ -162,19 +168,19 @@ def tile_attend_glse_w_kernel(tc, xT, w_words, w_scales, y, lse, wt, xm, offs, o
         xm_codes = keep.tile([P, D], U32, name="xm_codes", align_bytes=64)
         xm_plane = keep.tile([P, D], U8, name="xm_plane", align_bytes=64)
 
-        def exponentiate(h, places):
-            for t in places:
-                nc.scalar.activation(probs[h][:, t, :], scores[h, t][:], ACT.Exp, bias=neg_lse[:, t : t + 1])
+        pieces = [slice(0, HALF // 2), slice(HALF // 2, HALF)]
 
-        def form_first_g():
-            for t in range(2, PACK):
-                nc.vector.tensor_scalar(y_wt[:, t, :], y_sb[0][:, t, :], wt_sb[:, t : t + 1], None, ALU.mult)
+        def exponentiate(h, cols):
+            for t in range(PACK):
+                nc.scalar.activation(probs[h][:, t, cols], scores[h, t][:, cols], ACT.Exp, bias=neg_lse[:, t : t + 1])
+
+        def form_first_g(cols):
             for t in range(PACK):
                 nc.vector.scalar_tensor_tensor(
-                    g_rows[0][:, t, :],
-                    probs[0][:, t, :],
+                    g_rows[0][:, t, cols],
+                    probs[0][:, t, cols],
                     wt_sb[:, t : t + 1],
-                    y_wt[:, t, :],
+                    y_wt[:, t, cols],
                     ALU.mult,
                     ALU.subtract,
                 )
@@ -190,17 +196,30 @@ def tile_attend_glse_w_kernel(tc, xT, w_words, w_scales, y, lse, wt, xm, offs, o
             )
 
         def form_second_g(excess):
-            for cols in (slice(0, HALF // 2), slice(HALF // 2, HALF)):
+            second_pieces = (slice(0, 64), slice(64, 192), slice(192, HALF))
+            for cols in second_pieces:
                 nc.gpsimd.tensor_tensor(excess[:, :, cols], probs[1][:, :, cols], y_sb[1][:, :, cols], ALU.subtract)
+            for cols in second_pieces[:-1]:
                 for t in range(PACK):
                     nc.scalar.activation(
                         g_rows[1][:, t, cols], excess[:, t, cols], ACT.Copy, scale=wt_sb[:, t : t + 1]
                     )
                 interleave_g(1, cols, nc.scalar.copy)
+            cols = second_pieces[-1]
+            groups = (cols.stop - cols.start) // 4
+            nc.gpsimd.tensor_tensor(
+                g_grouped[1][:, PACK * cols.start : PACK * cols.stop].rearrange("p (c i t) -> p c t i", i=4, t=PACK),
+                excess[:, :, cols].rearrange("p t (c i) -> p c t i", i=4),
+                wt_sb[:].unsqueeze(1).unsqueeze(3).to_broadcast([P, groups, PACK, 4]),
+                ALU.mult,
+            )
 
-        def quantise_g(h):
+        def quantise_g(h, cols):
+            slots = slice(h * HALF + cols.start, h * HALF + cols.stop)
             nc.vector.quantize_mx(
-                out=g_codes[:, halves[h]].bitcast(E5M2), scales=g_plane[:, halves[h]], in_=g_grouped[h][:]
+                out=g_codes[:, slots].bitcast(E5M2),
+                scales=g_plane[:, slots],
+                in_=g_grouped[h][:, PACK * cols.start : PACK * cols.stop],
             )
 
         def cast_xm(first, last, tag, copy):
@@ -233,8 +252,11 @@ def tile_attend_glse_w_kernel(tc, xT, w_words, w_scales, y, lse, wt, xm, offs, o
             )
             return grad
 
-        def scatter(b, grad, slots, dense):
+        def leave_psum(grad, slots, dense):
             nc.scalar.copy(dense[:], grad[:, slots])
+            return dense
+
+        def scatter(b, slots, dense):
             entries = offsets[:, slots.start // 16 : slots.stop // 16]
             nc.vector.tensor_copy(windows[b % WINDOWS][:].indirect(entries), dense[:])
 
@@ -252,33 +274,40 @@ def tile_attend_glse_w_kernel(tc, xT, w_words, w_scales, y, lse, wt, xm, offs, o
 
         for t in range(2):
             nc.scalar.activation(y_wt[:, t, :], y_sb[0][:, t, :], ACT.Copy, scale=wt_sb[:, t : t + 1])
-        exponentiate(0, range(PACK))
+        for cols in pieces:
+            exponentiate(0, cols)
         for t in range(PACK):
             for o in range(PASSES):
                 score(1, o, t)
-        form_first_g()
-        interleave_g(0, slice(0, HALF), nc.vector.tensor_copy)
-        quantise_xm(0, 1, cast_xm(0, 1, "x_grouped1", nc.scalar.copy))
+        for t in range(2, PACK):
+            nc.vector.tensor_scalar(y_wt[:, t, :], y_sb[0][:, t, :], wt_sb[:, t : t + 1], None, ALU.mult)
+        form_first_g(pieces[0])
+        interleave_g(0, pieces[0], nc.vector.tensor_copy)
+        quantise_g(0, pieces[0])
+        form_first_g(pieces[1])
+        interleave_g(0, pieces[1], nc.vector.tensor_copy)
+        quantise_xm(0, 1, cast_xm(0, 1, "x_pair1", nc.scalar.copy))
         second_xm = cast_xm(1, 2, "x_grouped0", nc.scalar.copy)
-        quantise_g(0)
-        early = [multiply(0)]
-        exponentiate(1, range(PACK))
+        quantise_g(0, pieces[1])
+        early = [leave_psum(multiply(0), halves[0], dense_tile("dense_early0", HALF, "dense_early0"))]
+        exponentiate(1, slice(0, HALF))
         later_xm = cast_xm(2, EARLY, "g_rows0", nc.vector.tensor_copy)
         quantise_xm(1, 2, second_xm)
-        early.append(multiply(1))
+        early.append(leave_psum(multiply(1), halves[0], dense_tile("dense_early1", HALF, "dense_early1")))
         quantise_xm(2, EARLY, later_xm)
-        early.extend(multiply(b) for b in range(2, EARLY))
+        early.append(leave_psum(multiply(2), halves[0], dense_tile("dense_early2", HALF, "dense_early2")))
+        last_early = multiply(3)
         excess = keep.tile([P, PACK, HALF], F32, name="excess", tag="g_rows0", align_bytes=64)
         for b in range(EARLY - 1):
-            scatter(b, early[b], halves[0], dense_tile(f"dense_early{b}", HALF, f"dense_early{b}"))
+            scatter(b, halves[0], early[b])
         form_second_g(excess)
-        quantise_g(1)
-        scatter(3, early[3], halves[0], dense_tile("dense_early3", HALF, "g_rows1"))
+        quantise_g(1, slice(0, HALF))
+        scatter(3, halves[0], leave_psum(last_early, halves[0], dense_tile("dense_early3", HALF, "g_rows1")))
         for b, tag in enumerate(("dense_early0", "dense_early1", "scale_window", "dense_early2")):
             if b == EARLY - 2:
                 quantise_xm(EARLY, BLOCKS, cast_xm(EARLY, BLOCKS, "g_grouped1", nc.scalar.copy))
-            scatter(b, multiply(b), halves[1], dense_tile(f"dense_late{b}", HALF, tag))
+            scatter(b, halves[1], leave_psum(multiply(b), halves[1], dense_tile(f"dense_late{b}", HALF, tag)))
             store(b)
         for b in range(EARLY, BLOCKS):
-            scatter(b, multiply(b), slice(0, N), ring.tile([P, N], F32, name="dense"))
+            scatter(b, slice(0, N), leave_psum(multiply(b), slice(0, N), ring.tile([P, N], F32, name="dense")))
             store(b)

@@ -22,9 +22,9 @@ E2M1 = mybir.dt.float4_e2m1fn_x4
 ACT = mybir.ActivationFunctionType
 ALU = mybir.AluOpType
 
-VECTOR_SHARE = 84
 SCALE_FIRST = P - 16 * PASSES
 VECTOR_ZEROES = 384
+VECTOR_FIRST_SHARE = 96
 VECTOR_PAIR_SHARE = 24
 WINDOWS = 4
 EARLY = 4
@@ -84,8 +84,12 @@ def tile_attend_glse_w_kernel(tc, xT, w_words, w_scales, y, lse, wt, xm, offs, o
         x_raw.append(load_x(1, "scale_window"))
         w_pairs = keep.tile([P, N], U32, name="w_pairs", tag="w_pairs", align_bytes=64)
         nc.vector.tensor_copy(w_pairs[:], word_window[:].indirect(offsets[:]))
-        w_codes = keep.tile([P, PASSES, N], U16, name="w_codes", align_bytes=64)
-        nc.vector.tensor_copy(w_codes[:], w_pairs[:].bitcast(U16).rearrange("p (s o) -> p o s", o=PASSES))
+        w_codes = [keep.tile([P, PASSES, HALF], U16, name=f"w_codes{h}", align_bytes=64) for h in range(2)]
+
+        def part_words(h):
+            nc.vector.tensor_copy(
+                w_codes[h][:], w_pairs[:, halves[h]].bitcast(U16).rearrange("p (s o) -> p o s", o=PASSES)
+            )
 
         for cols in (slice(0, T // 2), slice(T // 2, T)):
             zero_in_odd_pieces(windows[0][:, cols].bitcast(I32))
@@ -109,8 +113,6 @@ def tile_attend_glse_w_kernel(tc, xT, w_words, w_scales, y, lse, wt, xm, offs, o
                 xm_raw[b] = raw[:, :, (b - first) * P : (b - first + 1) * P]
 
         load_y(0, "word_window", 2)
-        load_xm(0, 2, "w_pairs")
-        load_xm(2, 4, "scale_rows")
 
         x_codes = [keep.tile([P, R], U32, name=f"x_codes{o}", align_bytes=64) for o in range(PASSES)]
         x_planes = [keep.tile([P, R], U8, name=f"x_plane{o}", align_bytes=64) for o in range(PASSES)]
@@ -119,18 +121,24 @@ def tile_attend_glse_w_kernel(tc, xT, w_words, w_scales, y, lse, wt, xm, offs, o
             cols = slice(first * P, last * P)
             nc.vector.quantize_mx(out=x_codes[o][:, cols].bitcast(E4M3), scales=x_planes[o][:, cols], in_=grouped)
 
-        grouped = keep.tile([P, R * PACK], BF16, name="x_grouped0", tag="x_grouped0", align_bytes=64)
-        dst = grouped[:].rearrange("p (t m j) -> p m t j", t=PACK, j=PACK)
-        src = x_raw[0][:].rearrange("p j (m t) -> p m t j", t=PACK)
-        nc.vector.tensor_copy(dst[:, :VECTOR_SHARE], src[:, :VECTOR_SHARE])
-        nc.scalar.copy(dst[:, VECTOR_SHARE:], src[:, VECTOR_SHARE:])
-        quantise_x(0, 0, PACK, grouped[:])
+        def cast_views(o):
+            pairs = [
+                keep.tile([P, 2 * P * PACK], BF16, name=f"x_pair{o}{u}", tag=f"x_pair{o}{u}", align_bytes=64)
+                for u in range(2)
+            ]
+            dst = [pair[:].rearrange("p (t m j) -> p m j t", t=2, j=PACK) for pair in pairs]
+            return pairs, dst, x_raw[o][:].rearrange("p j (m u t) -> p u m j t", u=2, t=2)
 
-        pairs = [
-            keep.tile([P, 2 * P * PACK], BF16, name=f"x_pair{u}", tag=f"x_pair{u}", align_bytes=64) for u in range(2)
-        ]
-        dst = [pair[:].rearrange("p (t m j) -> p m j t", t=2, j=PACK) for pair in pairs]
-        src = x_raw[1][:].rearrange("p j (m u t) -> p u m j t", u=2, t=2)
+        pairs, dst, src = cast_views(0)
+        part_words(0)
+        nc.vector.tensor_copy(dst[0][:, :VECTOR_FIRST_SHARE], src[:, 0, :VECTOR_FIRST_SHARE])
+        nc.scalar.copy(dst[0][:, VECTOR_FIRST_SHARE:], src[:, 0, VECTOR_FIRST_SHARE:])
+        nc.scalar.copy(dst[1], src[:, 1])
+        part_words(1)
+        for u in range(2):
+            quantise_x(0, 2 * u, 2 * u + 2, pairs[u][:])
+
+        pairs, dst, src = cast_views(1)
         nc.vector.tensor_copy(dst[0], src[:, 0])
         nc.scalar.copy(dst[1][:, VECTOR_PAIR_SHARE:], src[:, 1, VECTOR_PAIR_SHARE:])
         nc.vector.tensor_copy(dst[1][:, :VECTOR_PAIR_SHARE], src[:, 1, :VECTOR_PAIR_SHARE])
@@ -149,7 +157,7 @@ def tile_attend_glse_w_kernel(tc, xT, w_words, w_scales, y, lse, wt, xm, offs, o
                     out=scores[h, t][:, c : c + P],
                     lhsT=x_codes[o][:, rows].bitcast(E4M3),
                     lhsT_scale=x_planes[o][:, rows],
-                    rhs=w_codes[:, o, slots].bitcast(E2M1),
+                    rhs=w_codes[h][:, o, c : c + P].bitcast(E2M1),
                     rhs_scale=w_planes[:, o, slots],
                     start=(o == 0 and c == 0),
                     stop=(o == PASSES - 1 and c == HALF - P),
@@ -159,6 +167,8 @@ def tile_attend_glse_w_kernel(tc, xT, w_words, w_scales, y, lse, wt, xm, offs, o
             for t in range(PACK):
                 score(0, o, t)
 
+        load_xm(0, 2, "w_pairs")
+        load_xm(2, 4, "scale_rows")
         load_y(1, "x_raw0", PACK)
         load_xm(4, BLOCKS, "scale_window")
 
@@ -265,8 +275,7 @@ def tile_attend_glse_w_kernel(tc, xT, w_words, w_scales, y, lse, wt, xm, offs, o
             if b < BLOCKS - 1:
                 nc.sync.dma_start(out[rows, :], windows[b % WINDOWS][:])
             else:
-                nc.sync.dma_start(out[rows, : T // 2], windows[b % WINDOWS][:, : T // 2])
-                nc.scalar.dma_start(out[rows, T // 2 :], windows[b % WINDOWS][:, T // 2 :])
+                nc.scalar.dma_start(out[rows, :], windows[b % WINDOWS][:])
 
 
         def dense_tile(name, width, tag):
@@ -286,8 +295,8 @@ def tile_attend_glse_w_kernel(tc, xT, w_words, w_scales, y, lse, wt, xm, offs, o
         quantise_g(0, pieces[0])
         form_first_g(pieces[1])
         interleave_g(0, pieces[1], nc.vector.tensor_copy)
-        quantise_xm(0, 1, cast_xm(0, 1, "x_pair1", nc.scalar.copy))
-        second_xm = cast_xm(1, 2, "x_grouped0", nc.scalar.copy)
+        quantise_xm(0, 1, cast_xm(0, 1, "x_pair11", nc.scalar.copy))
+        second_xm = cast_xm(1, 2, "x_pair00", nc.scalar.copy)
         quantise_g(0, pieces[1])
         early = [leave_psum(multiply(0), halves[0], dense_tile("dense_early0", HALF, "dense_early0"))]
         exponentiate(1, slice(0, HALF))

@@ -23,7 +23,7 @@ ACT = mybir.ActivationFunctionType
 ALU = mybir.AluOpType
 
 SCALE_FIRST = P - 16 * PASSES
-VECTOR_ZEROES = 384
+VECTOR_ZEROES = 640
 VECTOR_FIRST_SHARE = 96
 VECTOR_PAIR_SHARE = 24
 WINDOWS = 4
@@ -131,10 +131,10 @@ def tile_attend_glse_w_kernel(tc, xT, w_words, w_scales, y, lse, wt, xm, offs, o
 
         pairs, dst, src = cast_views(0)
         part_words(0)
-        nc.vector.tensor_copy(dst[0][:, :VECTOR_FIRST_SHARE], src[:, 0, :VECTOR_FIRST_SHARE])
-        nc.scalar.copy(dst[0][:, VECTOR_FIRST_SHARE:], src[:, 0, VECTOR_FIRST_SHARE:])
-        nc.scalar.copy(dst[1], src[:, 1])
         part_words(1)
+        nc.scalar.copy(dst[0], src[:, 0])
+        nc.vector.tensor_copy(dst[1][:, :VECTOR_FIRST_SHARE], src[:, 1, :VECTOR_FIRST_SHARE])
+        nc.scalar.copy(dst[1][:, VECTOR_FIRST_SHARE:], src[:, 1, VECTOR_FIRST_SHARE:])
         for u in range(2):
             quantise_x(0, 2 * u, 2 * u + 2, pairs[u][:])
 

@@ -23,9 +23,10 @@ ACT = mybir.ActivationFunctionType
 ALU = mybir.AluOpType
 
 SCALE_FIRST = P - 16 * PASSES
-VECTOR_ZEROES = 640
+VECTOR_ZEROES = 384
 VECTOR_FIRST_SHARE = 96
 VECTOR_PAIR_SHARE = 24
+SECOND_PIECES = (slice(0, 64), slice(64, 176), slice(176, HALF))
 WINDOWS = 4
 EARLY = 4
 
@@ -206,23 +207,29 @@ def tile_attend_glse_w_kernel(tc, xT, w_words, w_scales, y, lse, wt, xm, offs, o
             )
 
         def form_second_g(excess):
-            second_pieces = (slice(0, 64), slice(64, 192), slice(192, HALF))
-            for cols in second_pieces:
+            last = SECOND_PIECES[-1]
+            width = last.stop - last.start
+            weighted = []
+            for name, values in (("probs_wt", probs[1]), ("y_wt_last", y_sb[1])):
+                weighted.append(keep.tile([P, PACK, width], F32, name=name))
+                for t in range(PACK):
+                    nc.scalar.activation(
+                        weighted[-1][:, t, :], values[:, t, last], ACT.Copy, scale=wt_sb[:, t : t + 1]
+                    )
+            for cols in SECOND_PIECES[:-1]:
                 nc.gpsimd.tensor_tensor(excess[:, :, cols], probs[1][:, :, cols], y_sb[1][:, :, cols], ALU.subtract)
-            for cols in second_pieces[:-1]:
+            nc.gpsimd.tensor_tensor(
+                g_grouped[1][:, PACK * last.start : PACK * last.stop].rearrange("p (c i t) -> p c t i", i=4, t=PACK),
+                weighted[0][:].rearrange("p t (c i) -> p c t i", i=4),
+                weighted[1][:].rearrange("p t (c i) -> p c t i", i=4),
+                ALU.subtract,
+            )
+            for cols in SECOND_PIECES[:-1]:
                 for t in range(PACK):
                     nc.scalar.activation(
                         g_rows[1][:, t, cols], excess[:, t, cols], ACT.Copy, scale=wt_sb[:, t : t + 1]
                     )
                 interleave_g(1, cols, nc.scalar.copy)
-            cols = second_pieces[-1]
-            groups = (cols.stop - cols.start) // 4
-            nc.gpsimd.tensor_tensor(
-                g_grouped[1][:, PACK * cols.start : PACK * cols.stop].rearrange("p (c i t) -> p c t i", i=4, t=PACK),
-                excess[:, :, cols].rearrange("p t (c i) -> p c t i", i=4),
-                wt_sb[:].unsqueeze(1).unsqueeze(3).to_broadcast([P, groups, PACK, 4]),
-                ALU.mult,
-            )
 
         def quantise_g(h, cols):
             slots = slice(h * HALF + cols.start, h * HALF + cols.stop)
@@ -306,7 +313,7 @@ def tile_attend_glse_w_kernel(tc, xT, w_words, w_scales, y, lse, wt, xm, offs, o
         quantise_xm(2, EARLY, later_xm)
         early.append(leave_psum(multiply(2), halves[0], dense_tile("dense_early2", HALF, "dense_early2")))
         last_early = multiply(3)
-        excess = keep.tile([P, PACK, HALF], F32, name="excess", tag="g_rows0", align_bytes=64)
+        excess = keep.tile([P, PACK, SECOND_PIECES[-1].start], F32, name="excess", tag="g_rows0", align_bytes=64)
         for b in range(EARLY - 1):
             scatter(b, halves[0], early[b])
         form_second_g(excess)

@@ -6,7 +6,7 @@ N, T, D, R = 512, 2048, 1024, 512
 P = 128
 PACK = 4
 PASSES = D // (P * PACK)
-BLOCKS = D // P
+STRIPES = D // P
 HALF = N // 2
 FLOPS = 2 * 2 * R * D * N
 
@@ -23,21 +23,20 @@ ACT = mybir.ActivationFunctionType
 ALU = mybir.AluOpType
 
 SCALE_FIRST = P - 16 * PASSES
-VECTOR_ZEROES = 384
+VECTOR_ZEROES = 640
 VECTOR_FIRST_SHARE = 96
 VECTOR_PAIR_SHARE = 24
-SECOND_PIECES = (slice(0, 64), slice(64, 176), slice(176, HALF))
 WINDOWS = 4
-EARLY = 4
+BANKS = 8
 
 
 def tile_attend_glse_w_kernel(tc, xT, w_words, w_scales, y, lse, wt, xm, offs, out):
     nc = tc.nc
     with ExitStack() as ctx:
         keep = ctx.enter_context(tc.tile_pool(name="keep", bufs=1))
-        ring = ctx.enter_context(tc.tile_pool(name="ring", bufs=3))
         psum = ctx.enter_context(tc.psum_pool(name="psum", bufs=1))
         halves = [slice(h * HALF, (h + 1) * HALF) for h in range(2)]
+        whole = slice(0, N)
 
         offsets = keep.tile([P, N // 16], U16, name="offsets")
         nc.sync.dma_start(offsets[:], offs)
@@ -65,8 +64,6 @@ def tile_attend_glse_w_kernel(tc, xT, w_words, w_scales, y, lse, wt, xm, offs, o
             nc.vector.memset(words[:, middle:], 0)
 
         zero_in_odd_pieces(scale_window[:SCALE_FIRST, :].bitcast(I32))
-        g_codes = keep.tile([P, N], U32, name="g_codes", align_bytes=64)
-        g_plane = keep.tile([P, N], U8, name="g_plane", align_bytes=64)
         windows = [keep.tile([P, T], F32, name=f"out_window{i}") for i in range(WINDOWS)]
         for win in windows[1:-1]:
             nc.gpsimd.memset(win[:].bitcast(I32), 0)
@@ -95,25 +92,18 @@ def tile_attend_glse_w_kernel(tc, xT, w_words, w_scales, y, lse, wt, xm, offs, o
         for cols in (slice(0, T // 2), slice(T // 2, T)):
             zero_in_odd_pieces(windows[0][:, cols].bitcast(I32))
         zero_in_odd_pieces(windows[-1][:, :VECTOR_ZEROES].bitcast(I32))
-        zero_in_odd_pieces(g_codes[:, HALF:].bitcast(I32))
-        zero_in_odd_pieces(g_plane[:, HALF:].bitcast(I32))
 
         y_rows = y[0].rearrange("(p j) s -> p j s", j=PACK)
         xm_rows = xm[0].rearrange("(p j) d -> p j d", j=PACK)
-        y_sb, xm_raw = {}, {}
-
-        def load_y(h, tag, places):
-            y_sb[h] = keep.tile([P, PACK, HALF], F32, name=f"y_sb{h}", tag=tag, align_bytes=64)
-            for first in range(0, PACK, places):
-                nc.sync.dma_start(y_sb[h][:, first : first + places, :], y_rows[:, first : first + places, halves[h]])
+        y_sb = keep.tile([P, PACK, N], F32, name="y_sb", tag="word_window", align_bytes=64)
 
         def load_xm(first, last, tag):
             raw = keep.tile([P, PACK, (last - first) * P], F32, name=f"xm_raw{first}", tag=tag, align_bytes=64)
             nc.sync.dma_start(raw[:], xm_rows[:, :, first * P : last * P])
-            for b in range(first, last):
-                xm_raw[b] = raw[:, :, (b - first) * P : (b - first + 1) * P]
+            return raw
 
-        load_y(0, "word_window", 2)
+        for first in range(0, PACK, 2):
+            nc.sync.dma_start(y_sb[:, first : first + 2, :], y_rows[:, first : first + 2, :])
 
         x_codes = [keep.tile([P, R], U32, name=f"x_codes{o}", align_bytes=64) for o in range(PASSES)]
         x_planes = [keep.tile([P, R], U8, name=f"x_plane{o}", align_bytes=64) for o in range(PASSES)]
@@ -150,32 +140,33 @@ def tile_attend_glse_w_kernel(tc, xT, w_words, w_scales, y, lse, wt, xm, offs, o
 
         def score(h, o, t):
             if o == 0:
-                scores[h, t] = psum.tile([P, HALF], F32, name=f"scores{h}{t}", tag=f"score_bank{t}")
+                scores[h, t] = psum.tile([P, HALF], F32, name=f"scores{h}{t}", tag=f"bank{PACK * h + t}")
             rows = slice(t * P, (t + 1) * P)
-            for c in range(0, HALF, P):
-                slots = slice(h * HALF + c, h * HALF + c + P)
-                nc.tensor.matmul_mx(
-                    out=scores[h, t][:, c : c + P],
-                    lhsT=x_codes[o][:, rows].bitcast(E4M3),
-                    lhsT_scale=x_planes[o][:, rows],
-                    rhs=w_codes[h][:, o, c : c + P].bitcast(E2M1),
-                    rhs_scale=w_planes[:, o, slots],
-                    start=(o == 0 and c == 0),
-                    stop=(o == PASSES - 1 and c == HALF - P),
-                )
+            nc.tensor.matmul_mx(
+                out=scores[h, t][:],
+                lhsT=x_codes[o][:, rows].bitcast(E4M3),
+                lhsT_scale=x_planes[o][:, rows],
+                rhs=w_codes[h][:, o, :].bitcast(E2M1),
+                rhs_scale=w_planes[:, o, halves[h]],
+                start=(o == 0),
+                stop=(o == PASSES - 1),
+            )
 
-        for o in range(PASSES):
-            for t in range(PACK):
-                score(0, o, t)
+        for h in range(2):
+            for o in range(PASSES):
+                for t in range(PACK):
+                    score(h, o, t)
 
-        load_xm(0, 2, "w_pairs")
-        load_xm(2, 4, "scale_rows")
-        load_y(1, "x_raw0", PACK)
-        load_xm(4, BLOCKS, "scale_window")
+        xm_first = load_xm(0, 2, "w_pairs")
+        xm_second = load_xm(2, 4, "x_raw0")
+        xm_rest = load_xm(4, STRIPES, "scale_window")
 
         probs = [keep.tile([P, PACK, HALF], F32, name=f"probs{h}", tag=f"probs{h}", align_bytes=64) for h in range(2)]
+        y_wt = keep.tile([P, PACK, N], F32, name="y_wt", align_bytes=64)
         g_rows = [keep.tile([P, PACK, HALF], BF16, name=f"g_rows{h}", tag=f"g_rows{h}", align_bytes=64) for h in range(2)]
-        y_wt = keep.tile([P, PACK, HALF], F32, name="y_wt", tag="y_wt", align_bytes=64)
+        g_grouped = [keep.tile([P, HALF * PACK], BF16, name=f"g_grouped{h}", align_bytes=64) for h in range(2)]
+        g_codes = keep.tile([P, N], U32, name="g_codes", align_bytes=64)
+        g_plane = keep.tile([P, N], U8, name="g_plane", align_bytes=64)
         xm_codes = keep.tile([P, D], U32, name="xm_codes", align_bytes=64)
         xm_plane = keep.tile([P, D], U8, name="xm_plane", align_bytes=64)
 
@@ -185,51 +176,28 @@ def tile_attend_glse_w_kernel(tc, xT, w_words, w_scales, y, lse, wt, xm, offs, o
             for t in range(PACK):
                 nc.scalar.activation(probs[h][:, t, cols], scores[h, t][:, cols], ACT.Exp, bias=neg_lse[:, t : t + 1])
 
-        def form_first_g(cols):
+        def weigh_y_on_scalar(t):
+            nc.scalar.activation(y_wt[:, t, :], y_sb[:, t, :], ACT.Copy, scale=wt_sb[:, t : t + 1])
+
+        def weigh_y_on_vector(t):
+            nc.vector.tensor_scalar(y_wt[:, t, :], y_sb[:, t, :], wt_sb[:, t : t + 1], None, ALU.mult)
+
+        def form_g(h, cols):
             for t in range(PACK):
                 nc.vector.scalar_tensor_tensor(
-                    g_rows[0][:, t, cols],
-                    probs[0][:, t, cols],
+                    g_rows[h][:, t, cols],
+                    probs[h][:, t, cols],
                     wt_sb[:, t : t + 1],
-                    y_wt[:, t, cols],
+                    y_wt[:, t, h * HALF + cols.start : h * HALF + cols.stop],
                     ALU.mult,
                     ALU.subtract,
                 )
 
-        g_grouped = [
-            keep.tile([P, HALF * PACK], BF16, name=f"g_grouped{h}", tag=f"g_grouped{h}", align_bytes=64) for h in range(2)
-        ]
-
-        def interleave_g(h, cols, copy):
-            copy(
+        def interleave_g(h, cols):
+            nc.vector.tensor_copy(
                 g_grouped[h][:, PACK * cols.start : PACK * cols.stop].rearrange("p (c i t) -> p c t i", i=4, t=PACK),
                 g_rows[h][:, :, cols].rearrange("p t (c i) -> p c t i", i=4),
             )
-
-        def form_second_g(excess):
-            last = SECOND_PIECES[-1]
-            width = last.stop - last.start
-            weighted = []
-            for name, values in (("probs_wt", probs[1]), ("y_wt_last", y_sb[1])):
-                weighted.append(keep.tile([P, PACK, width], F32, name=name))
-                for t in range(PACK):
-                    nc.scalar.activation(
-                        weighted[-1][:, t, :], values[:, t, last], ACT.Copy, scale=wt_sb[:, t : t + 1]
-                    )
-            for cols in SECOND_PIECES[:-1]:
-                nc.gpsimd.tensor_tensor(excess[:, :, cols], probs[1][:, :, cols], y_sb[1][:, :, cols], ALU.subtract)
-            nc.gpsimd.tensor_tensor(
-                g_grouped[1][:, PACK * last.start : PACK * last.stop].rearrange("p (c i t) -> p c t i", i=4, t=PACK),
-                weighted[0][:].rearrange("p t (c i) -> p c t i", i=4),
-                weighted[1][:].rearrange("p t (c i) -> p c t i", i=4),
-                ALU.subtract,
-            )
-            for cols in SECOND_PIECES[:-1]:
-                for t in range(PACK):
-                    nc.scalar.activation(
-                        g_rows[1][:, t, cols], excess[:, t, cols], ACT.Copy, scale=wt_sb[:, t : t + 1]
-                    )
-                interleave_g(1, cols, nc.scalar.copy)
 
         def quantise_g(h, cols):
             slots = slice(h * HALF + cols.start, h * HALF + cols.stop)
@@ -239,14 +207,14 @@ def tile_attend_glse_w_kernel(tc, xT, w_words, w_scales, y, lse, wt, xm, offs, o
                 in_=g_grouped[h][:, PACK * cols.start : PACK * cols.stop],
             )
 
-        def cast_xm(first, last, tag, copy):
-            grouped = keep.tile([P, (last - first) * P * PACK], BF16, name=f"xm_grouped{first}", tag=tag, align_bytes=64)
-            for b in range(first, last):
-                copy(
-                    grouped[:, (b - first) * P * PACK : (b - first + 1) * P * PACK].rearrange("p (c i j) -> p c j i", i=4, j=PACK),
-                    xm_raw[b].rearrange("p j (c i) -> p c j i", i=4),
-                )
-            return grouped
+        def grouped_tile(first, last, tag):
+            return keep.tile([P, (last - first) * P * PACK], BF16, name=f"xm_grouped{first}", tag=tag, align_bytes=64)
+
+        def cast_xm(grouped, raw, copy):
+            copy(
+                grouped.rearrange("p (c i j) -> p c j i", i=4, j=PACK),
+                raw.rearrange("p j (c i) -> p c j i", i=4),
+            )
 
         def quantise_xm(first, last, grouped):
             nc.vector.quantize_mx(
@@ -255,75 +223,91 @@ def tile_attend_glse_w_kernel(tc, xT, w_words, w_scales, y, lse, wt, xm, offs, o
                 in_=grouped[:],
             )
 
-        def multiply(b):
+        def multiply(b, slots, bank):
             cols = slice(b * P, (b + 1) * P)
-            grad = psum.tile([P, N], F32, name="grad", bufs=4)
+            grad = psum.tile([P, slots.stop - slots.start], F32, name="grad", tag=f"bank{bank}")
             nc.tensor.matmul_mx(
                 out=grad[:],
                 lhsT=xm_codes[:, cols].bitcast(E4M3),
                 lhsT_scale=xm_plane[:, cols],
-                rhs=g_codes[:].bitcast(E5M2),
-                rhs_scale=g_plane[:],
+                rhs=g_codes[:, slots].bitcast(E5M2),
+                rhs_scale=g_plane[:, slots],
                 start=True,
                 stop=True,
             )
-            return grad
+            return grad[:]
 
-        def leave_psum(grad, slots, dense):
-            nc.scalar.copy(dense[:], grad[:, slots])
+        def leave_psum(grad, tag, copy):
+            dense = keep.tile([P, grad.shape[1]], F32, name="dense", tag=tag, align_bytes=64)
+            copy(dense[:], grad)
             return dense
 
-        def scatter(b, slots, dense):
-            entries = offsets[:, slots.start // 16 : slots.stop // 16]
-            nc.vector.tensor_copy(windows[b % WINDOWS][:].indirect(entries), dense[:])
+        def entries(slots):
+            return offsets[:, slots.start // 16 : slots.stop // 16]
+
+        def scatter_on_vector(b, slots, dense):
+            nc.vector.tensor_copy(windows[b % WINDOWS][:].indirect(entries(slots)), dense)
+
+        def scatter_on_scalar(b, slots, dense):
+            nc.scalar.activation(windows[b % WINDOWS][:].indirect(entries(slots)), dense, ACT.Copy)
 
         def store(b):
-            rows = slice(b * P, (b + 1) * P)
-            if b < BLOCKS - 1:
-                nc.sync.dma_start(out[rows, :], windows[b % WINDOWS][:])
-            else:
-                nc.scalar.dma_start(out[rows, :], windows[b % WINDOWS][:])
-
-
-        def dense_tile(name, width, tag):
-            return keep.tile([P, width], F32, name=name, tag=tag, align_bytes=64)
+            nc.sync.dma_start(out[b * P : (b + 1) * P, :], windows[b % WINDOWS][:])
 
         for t in range(2):
-            nc.scalar.activation(y_wt[:, t, :], y_sb[0][:, t, :], ACT.Copy, scale=wt_sb[:, t : t + 1])
+            weigh_y_on_scalar(t)
         for cols in pieces:
             exponentiate(0, cols)
-        for t in range(PACK):
-            for o in range(PASSES):
-                score(1, o, t)
         for t in range(2, PACK):
-            nc.vector.tensor_scalar(y_wt[:, t, :], y_sb[0][:, t, :], wt_sb[:, t : t + 1], None, ALU.mult)
-        form_first_g(pieces[0])
-        interleave_g(0, pieces[0], nc.vector.tensor_copy)
+            weigh_y_on_vector(t)
+        form_g(0, pieces[0])
+        interleave_g(0, pieces[0])
         quantise_g(0, pieces[0])
-        form_first_g(pieces[1])
-        interleave_g(0, pieces[1], nc.vector.tensor_copy)
-        quantise_xm(0, 1, cast_xm(0, 1, "x_pair11", nc.scalar.copy))
-        second_xm = cast_xm(1, 2, "x_pair00", nc.scalar.copy)
+        form_g(0, pieces[1])
+        interleave_g(0, pieces[1])
+        grouped = grouped_tile(0, 1, "x_pair11")
+        cast_xm(grouped[:], xm_first[:, :, :P], nc.scalar.copy)
+        quantise_xm(0, 1, grouped)
         quantise_g(0, pieces[1])
-        early = [leave_psum(multiply(0), halves[0], dense_tile("dense_early0", HALF, "dense_early0"))]
         exponentiate(1, slice(0, HALF))
-        later_xm = cast_xm(2, EARLY, "g_rows0", nc.vector.tensor_copy)
-        quantise_xm(1, 2, second_xm)
-        early.append(leave_psum(multiply(1), halves[0], dense_tile("dense_early1", HALF, "dense_early1")))
-        quantise_xm(2, EARLY, later_xm)
-        early.append(leave_psum(multiply(2), halves[0], dense_tile("dense_early2", HALF, "dense_early2")))
-        last_early = multiply(3)
-        excess = keep.tile([P, PACK, SECOND_PIECES[-1].start], F32, name="excess", tag="g_rows0", align_bytes=64)
-        for b in range(EARLY - 1):
-            scatter(b, halves[0], early[b])
-        form_second_g(excess)
+        grouped = grouped_tile(1, 2, "x_pair10")
+        cast_xm(grouped[:], xm_first[:, :, P:], nc.scalar.copy)
+        scatter_on_scalar(0, halves[0], leave_psum(multiply(0, halves[0], 0), "scalar_dense0", nc.scalar.copy)[:])
+
+        form_g(1, slice(0, HALF))
+        quantise_xm(1, 2, grouped)
+        interleave_g(1, slice(0, HALF))
+        grouped = grouped_tile(2, 4, "probs1")
+        cast_xm(grouped[:, : P * PACK], xm_second[:, :, :P], nc.vector.tensor_copy)
         quantise_g(1, slice(0, HALF))
-        scatter(3, halves[0], leave_psum(last_early, halves[0], dense_tile("dense_early3", HALF, "g_rows1")))
-        for b, tag in enumerate(("dense_early0", "dense_early1", "scale_window", "dense_early2")):
-            if b == EARLY - 2:
-                quantise_xm(EARLY, BLOCKS, cast_xm(EARLY, BLOCKS, "g_grouped1", nc.scalar.copy))
-            scatter(b, halves[1], leave_psum(multiply(b), halves[1], dense_tile(f"dense_late{b}", HALF, tag)))
-            store(b)
-        for b in range(EARLY, BLOCKS):
-            scatter(b, slice(0, N), leave_psum(multiply(b), slice(0, N), ring.tile([P, N], F32, name="dense")))
+        scatter_on_scalar(0, halves[1], leave_psum(multiply(0, halves[1], 2), "scalar_dense1", nc.scalar.copy)[:])
+        store(0)
+
+        cast_xm(grouped[:, P * PACK :], xm_second[:, :, P:], nc.vector.tensor_copy)
+        early = leave_psum(multiply(1, halves[0], 1), "g_rows1", nc.vector.tensor_copy)
+        quantise_xm(2, 4, grouped)
+        scatter_on_vector(1, halves[0], early[:])
+        scatter_on_vector(1, halves[1], leave_psum(multiply(1, halves[1], 3), "dense1b", nc.vector.tensor_copy)[:])
+        store(1)
+
+        grouped = grouped_tile(4, STRIPES, "probs1")
+        nc.gpsimd.tensor_scalar(
+            grouped[:].rearrange("p (d j) -> p d j", j=PACK),
+            xm_rest[:].rearrange("p j d -> p d j"),
+            1.0,
+            0.0,
+            ALU.mult,
+            ALU.add,
+        )
+        quantise_xm(4, STRIPES, grouped)
+        for b in range(2, STRIPES):
+            grad = multiply(b, whole, (b + 2) % BANKS)
+            if b % 2 == 0:
+                dense = [leave_psum(grad[:, halves[h]], f"scalar_dense{h}", nc.scalar.copy) for h in range(2)]
+                for h in range(2):
+                    scatter_on_scalar(b, halves[h], dense[h][:])
+            elif b == 5:
+                scatter_on_vector(b, whole, leave_psum(grad, "dense5", nc.scalar.copy)[:])
+            else:
+                scatter_on_vector(b, whole, leave_psum(grad, "probs1", nc.vector.tensor_copy)[:])
             store(b)

@@ -34,9 +34,13 @@ def tile_attend_glse_w_kernel(tc, xT, w_words, w_scales, y, lse, wt, xm, offs, o
     nc = tc.nc
     with ExitStack() as ctx:
         keep = ctx.enter_context(tc.tile_pool(name="keep", bufs=1))
+        reused = ctx.enter_context(tc.tile_pool(name="reused", bufs=1))
         psum = ctx.enter_context(tc.psum_pool(name="psum", bufs=1))
         halves = [slice(h * HALF, (h + 1) * HALF) for h in range(2)]
         whole = slice(0, N)
+
+        def reused_tile(name, shape, dtype, first_kib):
+            return reused.tile([P, *shape], dtype, name=name, offset=first_kib * 1024, align_bytes=64)
 
         offsets = keep.tile([P, N // 16], U16, name="offsets")
         nc.sync.dma_start(offsets[:], offs)
@@ -82,9 +86,10 @@ def tile_attend_glse_w_kernel(tc, xT, w_words, w_scales, y, lse, wt, xm, offs, o
         x_raw.append(load_x(1, "scale_window"))
         w_pairs = keep.tile([P, N], U32, name="w_pairs", tag="w_pairs", align_bytes=64)
         nc.vector.tensor_copy(w_pairs[:], word_window[:].indirect(offsets[:]))
-        w_codes = [keep.tile([P, PASSES, HALF], U16, name=f"w_codes{h}", align_bytes=64) for h in range(2)]
+        w_codes = {}
 
-        def part_words(h):
+        def part_words(h, codes):
+            w_codes[h] = codes
             nc.vector.tensor_copy(
                 w_codes[h][:], w_pairs[:, halves[h]].bitcast(U16).rearrange("p (s o) -> p o s", o=PASSES)
             )
@@ -114,15 +119,16 @@ def tile_attend_glse_w_kernel(tc, xT, w_words, w_scales, y, lse, wt, xm, offs, o
 
         def cast_views(o):
             pairs = [
-                keep.tile([P, 2 * P * PACK], BF16, name=f"x_pair{o}{u}", tag=f"x_pair{o}{u}", align_bytes=64)
+                reused_tile("last_pair", [2 * P * PACK], BF16, 6)
+                if (o, u) == (1, 1)
+                else keep.tile([P, 2 * P * PACK], BF16, name=f"x_pair{o}{u}", tag=f"x_pair{o}{u}", align_bytes=64)
                 for u in range(2)
             ]
             dst = [pair[:].rearrange("p (t m j) -> p m j t", t=2, j=PACK) for pair in pairs]
             return pairs, dst, x_raw[o][:].rearrange("p j (m u t) -> p u m j t", u=2, t=2)
 
         pairs, dst, src = cast_views(0)
-        part_words(0)
-        part_words(1)
+        part_words(0, keep.tile([P, PASSES, HALF], U16, name="w_codes0", align_bytes=64))
         nc.scalar.copy(dst[0], src[:, 0])
         nc.vector.tensor_copy(dst[1][:, :VECTOR_FIRST_SHARE], src[:, 1, :VECTOR_FIRST_SHARE])
         nc.scalar.copy(dst[1][:, VECTOR_FIRST_SHARE:], src[:, 1, VECTOR_FIRST_SHARE:])
@@ -135,6 +141,8 @@ def tile_attend_glse_w_kernel(tc, xT, w_words, w_scales, y, lse, wt, xm, offs, o
         nc.vector.tensor_copy(dst[1][:, :VECTOR_PAIR_SHARE], src[:, 1, :VECTOR_PAIR_SHARE])
         for t in range(PACK):
             quantise_x(1, t, t + 1, pairs[t // 2][:, (t % 2) * P * PACK : (t % 2 + 1) * P * PACK])
+
+        part_words(1, reused_tile("w_codes1", [PASSES, HALF], U16, 6))
 
         scores = {}
 
@@ -152,19 +160,24 @@ def tile_attend_glse_w_kernel(tc, xT, w_words, w_scales, y, lse, wt, xm, offs, o
                 stop=(o == PASSES - 1),
             )
 
-        for h in range(2):
+        for o in range(PASSES):
+            for t in range(PACK):
+                score(0, o, t)
+        for t in range(PACK):
             for o in range(PASSES):
-                for t in range(PACK):
-                    score(h, o, t)
+                score(1, o, t)
 
-        xm_first = load_xm(0, 2, "w_pairs")
-        xm_second = load_xm(2, 4, "x_raw0")
+        xm_first = load_xm(0, 1, "x_raw0")
+        xm_second = load_xm(1, 4, "x_pair01")
         xm_rest = load_xm(4, STRIPES, "scale_window")
 
-        probs = [keep.tile([P, PACK, HALF], F32, name=f"probs{h}", tag=f"probs{h}", align_bytes=64) for h in range(2)]
+        probs = [keep.tile([P, PACK, HALF], F32, name="probs0", align_bytes=64)]
         y_wt = keep.tile([P, PACK, N], F32, name="y_wt", align_bytes=64)
-        g_rows = [keep.tile([P, PACK, HALF], BF16, name=f"g_rows{h}", tag=f"g_rows{h}", align_bytes=64) for h in range(2)]
-        g_grouped = [keep.tile([P, HALF * PACK], BF16, name=f"g_grouped{h}", align_bytes=64) for h in range(2)]
+        g_rows = [keep.tile([P, PACK, HALF], BF16, name="g_rows0", align_bytes=64)]
+        g_grouped = [
+            reused_tile("g_grouped0", [HALF * PACK], BF16, 0),
+            keep.tile([P, HALF * PACK], BF16, name="g_grouped1", align_bytes=64),
+        ]
         g_codes = keep.tile([P, N], U32, name="g_codes", align_bytes=64)
         g_plane = keep.tile([P, N], U8, name="g_plane", align_bytes=64)
         xm_codes = keep.tile([P, D], U32, name="xm_codes", align_bytes=64)
@@ -265,32 +278,35 @@ def tile_attend_glse_w_kernel(tc, xT, w_words, w_scales, y, lse, wt, xm, offs, o
         quantise_g(0, pieces[0])
         form_g(0, pieces[1])
         interleave_g(0, pieces[1])
-        grouped = grouped_tile(0, 1, "x_pair11")
-        cast_xm(grouped[:], xm_first[:, :, :P], nc.scalar.copy)
+        grouped = reused_tile("xm_grouped0", [P * PACK], BF16, 2)
+        cast_xm(grouped[:], xm_first[:], nc.scalar.copy)
         quantise_xm(0, 1, grouped)
         quantise_g(0, pieces[1])
+        probs.append(keep.tile([P, PACK, HALF], F32, name="probs1", tag="x_raw0", align_bytes=64))
         exponentiate(1, slice(0, HALF))
-        grouped = grouped_tile(1, 2, "x_pair10")
-        cast_xm(grouped[:], xm_first[:, :, P:], nc.scalar.copy)
         scatter_on_scalar(0, halves[0], leave_psum(multiply(0, halves[0], 0), "scalar_dense0", nc.scalar.copy)[:])
+        grouped = grouped_tile(1, 2, "x_pair10")
+        cast_xm(grouped[:], xm_second[:, :, :P], nc.scalar.copy)
 
+        g_rows.append(reused_tile("g_rows1", [PACK, HALF], BF16, 3))
         form_g(1, slice(0, HALF))
         quantise_xm(1, 2, grouped)
         interleave_g(1, slice(0, HALF))
-        grouped = grouped_tile(2, 4, "probs1")
-        cast_xm(grouped[:, : P * PACK], xm_second[:, :, :P], nc.vector.tensor_copy)
+        grouped = grouped_tile(2, 4, "x_raw0")
+        cast_xm(grouped[:, : P * PACK], xm_second[:, :, P : 2 * P], nc.vector.tensor_copy)
         quantise_g(1, slice(0, HALF))
         scatter_on_scalar(0, halves[1], leave_psum(multiply(0, halves[1], 2), "scalar_dense1", nc.scalar.copy)[:])
         store(0)
 
-        cast_xm(grouped[:, P * PACK :], xm_second[:, :, P:], nc.vector.tensor_copy)
-        early = leave_psum(multiply(1, halves[0], 1), "g_rows1", nc.vector.tensor_copy)
+        cast_xm(grouped[:, P * PACK :], xm_second[:, :, 2 * P :], nc.vector.tensor_copy)
+        early = reused_tile("early_dense", [HALF], F32, 3)
+        nc.vector.tensor_copy(early[:], multiply(1, halves[0], 1))
         quantise_xm(2, 4, grouped)
         scatter_on_vector(1, halves[0], early[:])
         scatter_on_vector(1, halves[1], leave_psum(multiply(1, halves[1], 3), "dense1b", nc.vector.tensor_copy)[:])
         store(1)
 
-        grouped = grouped_tile(4, STRIPES, "probs1")
+        grouped = grouped_tile(4, STRIPES, "x_raw0")
         nc.gpsimd.tensor_scalar(
             grouped[:].rearrange("p (d j) -> p d j", j=PACK),
             xm_rest[:].rearrange("p j d -> p d j"),
@@ -309,5 +325,5 @@ def tile_attend_glse_w_kernel(tc, xT, w_words, w_scales, y, lse, wt, xm, offs, o
             elif b == 5:
                 scatter_on_vector(b, whole, leave_psum(grad, "dense5", nc.scalar.copy)[:])
             else:
-                scatter_on_vector(b, whole, leave_psum(grad, "probs1", nc.vector.tensor_copy)[:])
+                scatter_on_vector(b, whole, leave_psum(grad, "x_raw0", nc.vector.tensor_copy)[:])
             store(b)

@@ -35,12 +35,16 @@ def tile_attend_glse_w_kernel(tc, xT, w_words, w_scales, y, lse, wt, xm, offs, o
     with ExitStack() as ctx:
         keep = ctx.enter_context(tc.tile_pool(name="keep", bufs=1))
         reused = ctx.enter_context(tc.tile_pool(name="reused", bufs=1))
+        chain = ctx.enter_context(tc.tile_pool(name="chain", bufs=1))
         psum = ctx.enter_context(tc.psum_pool(name="psum", bufs=1))
         halves = [slice(h * HALF, (h + 1) * HALF) for h in range(2)]
         whole = slice(0, N)
 
         def reused_tile(name, shape, dtype, first_kib):
             return reused.tile([P, *shape], dtype, name=name, offset=first_kib * 1024, align_bytes=64)
+
+        def chain_tile(name, shape, dtype, first_byte):
+            return chain.tile([P, *shape], dtype, name=name, offset=first_byte, align_bytes=64)
 
         offsets = keep.tile([P, N // 16], U16, name="offsets")
         nc.sync.dma_start(offsets[:], offs)
@@ -55,12 +59,11 @@ def tile_attend_glse_w_kernel(tc, xT, w_words, w_scales, y, lse, wt, xm, offs, o
         nc.scalar.dma_start(lse_sb[:], lse[0].rearrange("(p j) o -> p (j o)", j=PACK))
         nc.scalar.dma_start(wt_sb[:], wt[0].rearrange("(p j) o -> p (j o)", j=PACK))
 
-        def load_x(o, tag):
-            raw = keep.tile([P, PACK, R], F32, name=f"x_raw{o}", tag=tag, align_bytes=64)
+        def load_x(o, raw):
             nc.sync.dma_start(raw[:], xT[0, o * 512 : (o + 1) * 512, :].rearrange("(p j) r -> p j r", j=PACK))
             return raw
 
-        x_raw = [load_x(0, "x_raw0")]
+        x_raw = [load_x(0, chain_tile("x_raw0", [PACK, R], F32, 0))]
 
         def zero_in_odd_pieces(words):
             middle = words.shape[1] // 2 - 1
@@ -83,7 +86,7 @@ def tile_attend_glse_w_kernel(tc, xT, w_words, w_scales, y, lse, wt, xm, offs, o
                 w_planes[32 * q : 32 * q + 4].rearrange("p o s -> p (o s)").bitcast(I32),
                 scale_rows[SCALE_FIRST + 8 * q : SCALE_FIRST + 8 * q + 8, :].bitcast(I32),
             )
-        x_raw.append(load_x(1, "scale_window"))
+        x_raw.append(load_x(1, keep.tile([P, PACK, R], F32, name="x_raw1", tag="scale_window", align_bytes=64)))
         w_pairs = keep.tile([P, N], U32, name="w_pairs", tag="w_pairs", align_bytes=64)
         nc.vector.tensor_copy(w_pairs[:], word_window[:].indirect(offsets[:]))
         w_codes = {}
@@ -102,8 +105,7 @@ def tile_attend_glse_w_kernel(tc, xT, w_words, w_scales, y, lse, wt, xm, offs, o
         xm_rows = xm[0].rearrange("(p j) d -> p j d", j=PACK)
         y_sb = keep.tile([P, PACK, N], F32, name="y_sb", tag="word_window", align_bytes=64)
 
-        def load_xm(first, last, tag):
-            raw = keep.tile([P, PACK, (last - first) * P], F32, name=f"xm_raw{first}", tag=tag, align_bytes=64)
+        def load_xm(first, last, raw):
             nc.sync.dma_start(raw[:], xm_rows[:, :, first * P : last * P])
             return raw
 
@@ -167,9 +169,11 @@ def tile_attend_glse_w_kernel(tc, xT, w_words, w_scales, y, lse, wt, xm, offs, o
             for o in range(PASSES):
                 score(1, o, t)
 
-        xm_first = load_xm(0, 1, "x_raw0")
-        xm_second = load_xm(1, 4, "x_pair01")
-        xm_rest = load_xm(4, STRIPES, "scale_window")
+        xm_first = load_xm(0, 1, chain_tile("xm_first", [PACK, P], F32, 6144))
+        xm_second = load_xm(1, 4, keep.tile([P, PACK, 3 * P], F32, name="xm_second", tag="x_pair01", align_bytes=64))
+        xm_rest = load_xm(
+            4, STRIPES, keep.tile([P, PACK, 4 * P], F32, name="xm_rest", tag="scale_window", align_bytes=64)
+        )
 
         probs = [keep.tile([P, PACK, HALF], F32, name="probs0", align_bytes=64)]
         y_wt = keep.tile([P, PACK, N], F32, name="y_wt", align_bytes=64)
@@ -250,10 +254,25 @@ def tile_attend_glse_w_kernel(tc, xT, w_words, w_scales, y, lse, wt, xm, offs, o
             )
             return grad[:]
 
-        def leave_psum(grad, tag, copy):
-            dense = keep.tile([P, grad.shape[1]], F32, name="dense", tag=tag, align_bytes=64)
-            copy(dense[:], grad)
-            return dense
+        def leave_psum_on_scalar(grad):
+            dense = keep.tile([P, HALF], F32, name="scalar_dense", bufs=2, align_bytes=64)
+            nc.scalar.copy(dense[:], grad)
+            return dense[:]
+
+        def leave_psum_on_vector(grad):
+            dense = keep.tile([P, N], F32, name="vector_dense", align_bytes=64)
+            nc.vector.tensor_copy(dense[:], grad)
+            return dense[:]
+
+        def cast_xm_on_gpsimd(first, last, grouped):
+            nc.gpsimd.tensor_scalar(
+                grouped[:].rearrange("p (d j) -> p d j", j=PACK),
+                xm_rest[:, :, (first - 4) * P : (last - 4) * P].rearrange("p j d -> p d j"),
+                1.0,
+                0.0,
+                ALU.mult,
+                ALU.add,
+            )
 
         def entries(slots):
             return offsets[:, slots.start // 16 : slots.stop // 16]
@@ -282,48 +301,62 @@ def tile_attend_glse_w_kernel(tc, xT, w_words, w_scales, y, lse, wt, xm, offs, o
         cast_xm(grouped[:], xm_first[:], nc.scalar.copy)
         quantise_xm(0, 1, grouped)
         quantise_g(0, pieces[1])
-        probs.append(keep.tile([P, PACK, HALF], F32, name="probs1", tag="x_raw0", align_bytes=64))
+        probs.append(chain_tile("probs1", [PACK, HALF], F32, 4096))
         exponentiate(1, slice(0, HALF))
-        scatter_on_scalar(0, halves[0], leave_psum(multiply(0, halves[0], 0), "scalar_dense0", nc.scalar.copy)[:])
+        dense = leave_psum_on_scalar(multiply(0, halves[0], 0))
         grouped = grouped_tile(1, 2, "x_pair10")
         cast_xm(grouped[:], xm_second[:, :, :P], nc.scalar.copy)
+        scatter_on_scalar(0, halves[0], dense)
 
         g_rows.append(reused_tile("g_rows1", [PACK, HALF], BF16, 3))
         form_g(1, slice(0, HALF))
         quantise_xm(1, 2, grouped)
+        scalar_halves = [leave_psum_on_scalar(multiply(1, halves[0], 1))]
         interleave_g(1, slice(0, HALF))
-        grouped = grouped_tile(2, 4, "x_raw0")
+        grouped = chain_tile("xm_grouped2", [2 * P * PACK], BF16, 6144)
         cast_xm(grouped[:, : P * PACK], xm_second[:, :, P : 2 * P], nc.vector.tensor_copy)
         quantise_g(1, slice(0, HALF))
-        scatter_on_scalar(0, halves[1], leave_psum(multiply(0, halves[1], 2), "scalar_dense1", nc.scalar.copy)[:])
-        store(0)
+        last_of_first = multiply(0, halves[1], 2)
+        scalar_halves.append(leave_psum_on_scalar(multiply(1, halves[1], 3)))
 
         cast_xm(grouped[:, P * PACK :], xm_second[:, :, 2 * P :], nc.vector.tensor_copy)
         early = reused_tile("early_dense", [HALF], F32, 3)
-        nc.vector.tensor_copy(early[:], multiply(1, halves[0], 1))
+        nc.vector.tensor_copy(early[:], last_of_first)
         quantise_xm(2, 4, grouped)
-        scatter_on_vector(1, halves[0], early[:])
-        scatter_on_vector(1, halves[1], leave_psum(multiply(1, halves[1], 3), "dense1b", nc.vector.tensor_copy)[:])
-        store(1)
+        scatter_on_vector(0, halves[1], early[:])
+        store(0)
 
-        grouped = grouped_tile(4, STRIPES, "x_raw0")
-        nc.gpsimd.tensor_scalar(
-            grouped[:].rearrange("p (d j) -> p d j", j=PACK),
-            xm_rest[:].rearrange("p j d -> p d j"),
-            1.0,
-            0.0,
-            ALU.mult,
-            ALU.add,
-        )
-        quantise_xm(4, STRIPES, grouped)
-        for b in range(2, STRIPES):
-            grad = multiply(b, whole, (b + 2) % BANKS)
-            if b % 2 == 0:
-                dense = [leave_psum(grad[:, halves[h]], f"scalar_dense{h}", nc.scalar.copy) for h in range(2)]
-                for h in range(2):
-                    scatter_on_scalar(b, halves[h], dense[h][:])
-            elif b == 5:
-                scatter_on_vector(b, whole, leave_psum(grad, "dense5", nc.scalar.copy)[:])
-            else:
-                scatter_on_vector(b, whole, leave_psum(grad, "x_raw0", nc.vector.tensor_copy)[:])
+        def product(b):
+            return multiply(b, whole, (b + 2) % BANKS)
+
+        def scalar_copies(b):
+            grad = product(b)
+            return [leave_psum_on_scalar(grad[:, halves[h]]) for h in range(2)]
+
+        def scalar_scatters(b, dense_halves):
+            for h in range(2):
+                scatter_on_scalar(b, halves[h], dense_halves[h])
             store(b)
+
+        grouped = chain_tile("xm_grouped4", [P * PACK], BF16, 7168)
+        cast_xm_on_gpsimd(4, 5, grouped)
+        dense = keep.tile([P, N], F32, name="dense2", align_bytes=64)[:]
+        nc.vector.tensor_copy(dense, product(2))
+        quantise_xm(4, 5, grouped)
+        scalar_scatters(1, scalar_halves)
+        scatter_on_vector(2, whole, dense)
+        store(2)
+
+        grouped = chain_tile("xm_grouped5", [3 * P * PACK], BF16, 7168)
+        cast_xm_on_gpsimd(5, STRIPES, grouped)
+        dense = leave_psum_on_vector(product(4))
+        quantise_xm(5, STRIPES, grouped)
+        scalar_scatters(3, scalar_copies(3))
+        scatter_on_vector(4, whole, dense)
+        store(4)
+
+        dense = leave_psum_on_vector(product(6))
+        scalar_scatters(5, scalar_copies(5))
+        scatter_on_vector(6, whole, dense)
+        store(6)
+        scalar_scatters(7, scalar_copies(7))

@@ -240,11 +240,13 @@ def tile_attend_glse_w_kernel(tc, xT, w_words, w_scales, y, lse, wt, xm, offs, o
                 in_=grouped[:],
             )
 
-        def multiply(b, slots, bank):
+        def bank_tile(bank, width):
+            return psum.tile([P, width], F32, name="grad", tag=f"bank{bank}")[:]
+
+        def multiply(b, slots, grad):
             cols = slice(b * P, (b + 1) * P)
-            grad = psum.tile([P, slots.stop - slots.start], F32, name="grad", tag=f"bank{bank}")
             nc.tensor.matmul_mx(
-                out=grad[:],
+                out=grad,
                 lhsT=xm_codes[:, cols].bitcast(E4M3),
                 lhsT_scale=xm_plane[:, cols],
                 rhs=g_codes[:, slots].bitcast(E5M2),
@@ -252,7 +254,7 @@ def tile_attend_glse_w_kernel(tc, xT, w_words, w_scales, y, lse, wt, xm, offs, o
                 start=True,
                 stop=True,
             )
-            return grad[:]
+            return grad
 
         def leave_psum_on_scalar(grad):
             dense = keep.tile([P, HALF], F32, name="scalar_dense", bufs=2, align_bytes=64)
@@ -303,7 +305,7 @@ def tile_attend_glse_w_kernel(tc, xT, w_words, w_scales, y, lse, wt, xm, offs, o
         quantise_g(0, pieces[1])
         probs.append(chain_tile("probs1", [PACK, HALF], F32, 4096))
         exponentiate(1, slice(0, HALF))
-        dense = leave_psum_on_scalar(multiply(0, halves[0], 0))
+        dense = leave_psum_on_scalar(multiply(0, halves[0], bank_tile(0, HALF)))
         grouped = grouped_tile(1, 2, "x_pair10")
         cast_xm(grouped[:], xm_second[:, :, :P], nc.scalar.copy)
         scatter_on_scalar(0, halves[0], dense)
@@ -311,13 +313,12 @@ def tile_attend_glse_w_kernel(tc, xT, w_words, w_scales, y, lse, wt, xm, offs, o
         g_rows.append(reused_tile("g_rows1", [PACK, HALF], BF16, 3))
         form_g(1, slice(0, HALF))
         quantise_xm(1, 2, grouped)
-        scalar_halves = [leave_psum_on_scalar(multiply(1, halves[0], 1))]
+        first_half = leave_psum_on_scalar(multiply(1, halves[0], bank_tile(1, HALF)))
         interleave_g(1, slice(0, HALF))
         grouped = chain_tile("xm_grouped2", [2 * P * PACK], BF16, 6144)
         cast_xm(grouped[:, : P * PACK], xm_second[:, :, P : 2 * P], nc.vector.tensor_copy)
         quantise_g(1, slice(0, HALF))
-        last_of_first = multiply(0, halves[1], 2)
-        scalar_halves.append(leave_psum_on_scalar(multiply(1, halves[1], 3)))
+        last_of_first = multiply(0, halves[1], bank_tile(2, HALF))
 
         cast_xm(grouped[:, P * PACK :], xm_second[:, :, 2 * P :], nc.vector.tensor_copy)
         early = reused_tile("early_dense", [HALF], F32, 3)
@@ -326,11 +327,17 @@ def tile_attend_glse_w_kernel(tc, xT, w_words, w_scales, y, lse, wt, xm, offs, o
         scatter_on_vector(0, halves[1], early[:])
         store(0)
 
-        def product(b):
-            return multiply(b, whole, (b + 2) % BANKS)
+        def shared_copies(b, bank):
+            dense = keep.tile([P, 3, HALF], F32, name=f"shared_dense{b}", align_bytes=64)
+            second_halves = bank_tile(bank, N)
+            multiply(b, halves[1], second_halves[:, HALF:])
+            multiply(b + 1, halves[1], second_halves[:, :HALF])
+            nc.vector.tensor_copy(dense[:, 0, :], multiply(b + 1, halves[0], bank_tile(bank + 1, HALF)))
+            nc.scalar.copy(dense[:, 1:, :].rearrange("p k s -> p (k s)"), second_halves)
+            return dense[:, 2, :], dense[:, :2, :].rearrange("p k s -> p (k s)")
 
-        def scalar_copies(b):
-            grad = product(b)
+        def scalar_copies(b, bank):
+            grad = multiply(b, whole, bank_tile(bank, N))
             return [leave_psum_on_scalar(grad[:, halves[h]]) for h in range(2)]
 
         def scalar_scatters(b, dense_halves):
@@ -340,23 +347,22 @@ def tile_attend_glse_w_kernel(tc, xT, w_words, w_scales, y, lse, wt, xm, offs, o
 
         grouped = chain_tile("xm_grouped4", [P * PACK], BF16, 7168)
         cast_xm_on_gpsimd(4, 5, grouped)
-        dense = keep.tile([P, N], F32, name="dense2", align_bytes=64)[:]
-        nc.vector.tensor_copy(dense, product(2))
+        second_half, dense = shared_copies(1, 3)
         quantise_xm(4, 5, grouped)
-        scalar_scatters(1, scalar_halves)
+        scalar_scatters(1, [first_half, second_half])
         scatter_on_vector(2, whole, dense)
         store(2)
 
         grouped = chain_tile("xm_grouped5", [3 * P * PACK], BF16, 7168)
         cast_xm_on_gpsimd(5, STRIPES, grouped)
-        dense = leave_psum_on_vector(product(4))
+        dense = leave_psum_on_vector(multiply(4, whole, bank_tile(6, N)))
         quantise_xm(5, STRIPES, grouped)
-        scalar_scatters(3, scalar_copies(3))
+        scalar_scatters(3, scalar_copies(3, 5))
         scatter_on_vector(4, whole, dense)
         store(4)
 
-        dense = leave_psum_on_vector(product(6))
-        scalar_scatters(5, scalar_copies(5))
+        dense = leave_psum_on_vector(multiply(6, whole, bank_tile(1, N)))
+        scalar_scatters(5, scalar_copies(5, 0))
         scatter_on_vector(6, whole, dense)
         store(6)
-        scalar_scatters(7, scalar_copies(7))
+        scalar_scatters(7, scalar_copies(7, 2))

from contextlib import ExitStack

import concourse.mybir as mybir

N, T, D, R = 512, 2048, 1024, 512
P = 128
PACK = 4
PASSES = D // (P * PACK)
STRIPES = D // P
HALF = N // 2
FLOPS = 2 * 2 * R * D * N

F32 = mybir.dt.float32
BF16 = mybir.dt.bfloat16
I32 = mybir.dt.int32
U32 = mybir.dt.uint32
U16 = mybir.dt.uint16
U8 = mybir.dt.uint8
E4M3 = mybir.dt.float8_e4m3fn_x4
E5M2 = mybir.dt.float8_e5m2_x4
E2M1 = mybir.dt.float4_e2m1fn_x4
ACT = mybir.ActivationFunctionType
ALU = mybir.AluOpType

SCALE_FIRST = P - 16 * PASSES
VECTOR_ZEROES = 640
VECTOR_FIRST_SHARE = 96
VECTOR_PAIR_SHARE = 24
WINDOWS = 4
BANKS = 8


def tile_attend_glse_w_kernel(tc, xT, w_words, w_scales, y, lse, wt, xm, offs, out):
    nc = tc.nc
    with ExitStack() as ctx:
        keep = ctx.enter_context(tc.tile_pool(name="keep", bufs=1))
        reused = ctx.enter_context(tc.tile_pool(name="reused", bufs=1))
        chain = ctx.enter_context(tc.tile_pool(name="chain", bufs=1))
        psum = ctx.enter_context(tc.psum_pool(name="psum", bufs=1))
        halves = [slice(h * HALF, (h + 1) * HALF) for h in range(2)]
        whole = slice(0, N)

        def reused_tile(name, shape, dtype, first_kib):
            return reused.tile([P, *shape], dtype, name=name, offset=first_kib * 1024, align_bytes=64)

        def chain_tile(name, shape, dtype, first_byte):
            return chain.tile([P, *shape], dtype, name=name, offset=first_byte, align_bytes=64)

        offsets = keep.tile([P, N // 16], U16, name="offsets")
        nc.sync.dma_start(offsets[:], offs)
        scale_window = keep.tile([P, T], U8, name="scale_window", tag="scale_window", align_bytes=64)
        nc.scalar.dma_start(
            scale_window[SCALE_FIRST:, :].bitcast(I32), w_scales.rearrange("o f t -> f o t").bitcast(I32)
        )
        word_window = keep.tile([P, T], U32, name="word_window", tag="word_window", align_bytes=64)
        nc.sync.dma_start(word_window[:].bitcast(I32), w_words[0].rearrange("p n b -> p (n b)").bitcast(I32))
        lse_sb = keep.tile([P, PACK], F32, name="lse_sb")
        wt_sb = keep.tile([P, PACK], F32, name="wt_sb")
        nc.scalar.dma_start(lse_sb[:], lse[0].rearrange("(p j) o -> p (j o)", j=PACK))
        nc.scalar.dma_start(wt_sb[:], wt[0].rearrange("(p j) o -> p (j o)", j=PACK))

        def load_x(o, raw):
            nc.sync.dma_start(raw[:], xT[0, o * 512 : (o + 1) * 512, :].rearrange("(p j) r -> p j r", j=PACK))
            return raw

        x_raw = [load_x(0, chain_tile("x_raw0", [PACK, R], F32, 0))]

        def zero_in_odd_pieces(words):
            middle = words.shape[1] // 2 - 1
            nc.vector.memset(words[:, :middle], 0)
            nc.vector.memset(words[:, middle:], 0)

        zero_in_odd_pieces(scale_window[:SCALE_FIRST, :].bitcast(I32))
        windows = [keep.tile([P, T], F32, name=f"out_window{i}") for i in range(WINDOWS)]
        for win in windows[1:-1]:
            nc.gpsimd.memset(win[:].bitcast(I32), 0)
        nc.gpsimd.memset(windows[-1][:, VECTOR_ZEROES:].bitcast(I32), 0)
        neg_lse = keep.tile([P, PACK], F32, name="neg_lse")
        nc.scalar.activation(neg_lse[:], lse_sb[:], ACT.Copy, scale=-1.0)

        scale_rows = keep.tile([P, N], U8, name="scale_rows", tag="scale_rows", align_bytes=64)
        nc.vector.tensor_copy(scale_rows[:], scale_window[:].indirect(offsets[:]))
        w_planes = keep.tile([P, PASSES, N], U8, name="w_planes", align_bytes=64)
        for q in range(4):
            nc.sync.dma_start(
                w_planes[32 * q : 32 * q + 4].rearrange("p o s -> p (o s)").bitcast(I32),
                scale_rows[SCALE_FIRST + 8 * q : SCALE_FIRST + 8 * q + 8, :].bitcast(I32),
            )
        x_raw.append(load_x(1, keep.tile([P, PACK, R], F32, name="x_raw1", tag="scale_window", align_bytes=64)))
        w_pairs = keep.tile([P, N], U32, name="w_pairs", tag="w_pairs", align_bytes=64)
        nc.vector.tensor_copy(w_pairs[:], word_window[:].indirect(offsets[:]))
        w_codes = {}

        def part_words(h, codes):
            w_codes[h] = codes
            nc.vector.tensor_copy(
                w_codes[h][:], w_pairs[:, halves[h]].bitcast(U16).rearrange("p (s o) -> p o s", o=PASSES)
            )

        for cols in (slice(0, T // 2), slice(T // 2, T)):
            zero_in_odd_pieces(windows[0][:, cols].bitcast(I32))
        zero_in_odd_pieces(windows[-1][:, :VECTOR_ZEROES].bitcast(I32))

        y_rows = y[0].rearrange("(p j) s -> p j s", j=PACK)
        xm_rows = xm[0].rearrange("(p j) d -> p j d", j=PACK)
        y_sb = keep.tile([P, PACK, N], F32, name="y_sb", tag="word_window", align_bytes=64)

        def load_xm(first, last, raw):
            nc.sync.dma_start(raw[:], xm_rows[:, :, first * P : last * P])
            return raw

        for first in range(0, PACK, 2):
            nc.sync.dma_start(y_sb[:, first : first + 2, :], y_rows[:, first : first + 2, :])

        x_codes = [keep.tile([P, R], U32, name=f"x_codes{o}", align_bytes=64) for o in range(PASSES)]
        x_planes = [keep.tile([P, R], U8, name=f"x_plane{o}", align_bytes=64) for o in range(PASSES)]

        def quantise_x(o, first, last, grouped):
            cols = slice(first * P, last * P)
            nc.vector.quantize_mx(out=x_codes[o][:, cols].bitcast(E4M3), scales=x_planes[o][:, cols], in_=grouped)

        def cast_views(o):
            pairs = [
                reused_tile("last_pair", [2 * P * PACK], BF16, 6)
                if (o, u) == (1, 1)
                else keep.tile([P, 2 * P * PACK], BF16, name=f"x_pair{o}{u}", tag=f"x_pair{o}{u}", align_bytes=64)
                for u in range(2)
            ]
            dst = [pair[:].rearrange("p (t m j) -> p m j t", t=2, j=PACK) for pair in pairs]
            return pairs, dst, x_raw[o][:].rearrange("p j (m u t) -> p u m j t", u=2, t=2)

        pairs, dst, src = cast_views(0)
        part_words(0, keep.tile([P, PASSES, HALF], U16, name="w_codes0", align_bytes=64))
        nc.scalar.copy(dst[0], src[:, 0])
        nc.vector.tensor_copy(dst[1][:, :VECTOR_FIRST_SHARE], src[:, 1, :VECTOR_FIRST_SHARE])
        nc.scalar.copy(dst[1][:, VECTOR_FIRST_SHARE:], src[:, 1, VECTOR_FIRST_SHARE:])
        for u in range(2):
            quantise_x(0, 2 * u, 2 * u + 2, pairs[u][:])

        pairs, dst, src = cast_views(1)
        nc.vector.tensor_copy(dst[0], src[:, 0])
        nc.scalar.copy(dst[1][:, VECTOR_PAIR_SHARE:], src[:, 1, VECTOR_PAIR_SHARE:])
        nc.vector.tensor_copy(dst[1][:, :VECTOR_PAIR_SHARE], src[:, 1, :VECTOR_PAIR_SHARE])
        for t in range(PACK):
            quantise_x(1, t, t + 1, pairs[t // 2][:, (t % 2) * P * PACK : (t % 2 + 1) * P * PACK])

        part_words(1, reused_tile("w_codes1", [PASSES, HALF], U16, 6))

        scores = {}

        def score(h, o, t):
            if o == 0:
                scores[h, t] = psum.tile([P, HALF], F32, name=f"scores{h}{t}", tag=f"bank{PACK * h + t}")
            rows = slice(t * P, (t + 1) * P)
            nc.tensor.matmul_mx(
                out=scores[h, t][:],
                lhsT=x_codes[o][:, rows].bitcast(E4M3),
                lhsT_scale=x_planes[o][:, rows],
                rhs=w_codes[h][:, o, :].bitcast(E2M1),
                rhs_scale=w_planes[:, o, halves[h]],
                start=(o == 0),
                stop=(o == PASSES - 1),
            )

        for o in range(PASSES):
            for t in range(PACK):
                score(0, o, t)
        for t in range(PACK):
            for o in range(PASSES):
                score(1, o, t)

        xm_first = load_xm(0, 1, chain_tile("xm_first", [PACK, P], F32, 6144))
        xm_second = load_xm(1, 4, keep.tile([P, PACK, 3 * P], F32, name="xm_second", tag="x_pair01", align_bytes=64))
        xm_rest = load_xm(
            4, STRIPES, keep.tile([P, PACK, 4 * P], F32, name="xm_rest", tag="scale_window", align_bytes=64)
        )

        probs = [keep.tile([P, PACK, HALF], F32, name="probs0", align_bytes=64)]
        y_wt = keep.tile([P, PACK, N], F32, name="y_wt", align_bytes=64)
        g_rows = [keep.tile([P, PACK, HALF], BF16, name="g_rows0", align_bytes=64)]
        g_grouped = [
            reused_tile("g_grouped0", [HALF * PACK], BF16, 0),
            keep.tile([P, HALF * PACK], BF16, name="g_grouped1", align_bytes=64),
        ]
        g_codes = keep.tile([P, N], U32, name="g_codes", align_bytes=64)
        g_plane = keep.tile([P, N], U8, name="g_plane", align_bytes=64)
        xm_codes = keep.tile([P, D], U32, name="xm_codes", align_bytes=64)
        xm_plane = keep.tile([P, D], U8, name="xm_plane", align_bytes=64)

        pieces = [slice(0, HALF // 2), slice(HALF // 2, HALF)]

        def exponentiate(h, cols):
            for t in range(PACK):
                nc.scalar.activation(probs[h][:, t, cols], scores[h, t][:, cols], ACT.Exp, bias=neg_lse[:, t : t + 1])

        def weigh_y_on_scalar(t):
            nc.scalar.activation(y_wt[:, t, :], y_sb[:, t, :], ACT.Copy, scale=wt_sb[:, t : t + 1])

        def weigh_y_on_vector(t):
            nc.vector.tensor_scalar(y_wt[:, t, :], y_sb[:, t, :], wt_sb[:, t : t + 1], None, ALU.mult)

        def form_g(h, cols):
            for t in range(PACK):
                nc.vector.scalar_tensor_tensor(
                    g_rows[h][:, t, cols],
                    probs[h][:, t, cols],
                    wt_sb[:, t : t + 1],
                    y_wt[:, t, h * HALF + cols.start : h * HALF + cols.stop],
                    ALU.mult,
                    ALU.subtract,
                )

        def interleave_g(h, cols):
            nc.vector.tensor_copy(
                g_grouped[h][:, PACK * cols.start : PACK * cols.stop].rearrange("p (c i t) -> p c t i", i=4, t=PACK),
                g_rows[h][:, :, cols].rearrange("p t (c i) -> p c t i", i=4),
            )

        def quantise_g(h, cols):
            slots = slice(h * HALF + cols.start, h * HALF + cols.stop)
            nc.vector.quantize_mx(
                out=g_codes[:, slots].bitcast(E5M2),
                scales=g_plane[:, slots],
                in_=g_grouped[h][:, PACK * cols.start : PACK * cols.stop],
            )

        def grouped_tile(first, last, tag):
            return keep.tile([P, (last - first) * P * PACK], BF16, name=f"xm_grouped{first}", tag=tag, align_bytes=64)

        def cast_xm(grouped, raw, copy):
            copy(
                grouped.rearrange("p (c i j) -> p c j i", i=4, j=PACK),
                raw.rearrange("p j (c i) -> p c j i", i=4),
            )

        def quantise_xm(first, last, grouped):
            nc.vector.quantize_mx(
                out=xm_codes[:, first * P : last * P].bitcast(E4M3),
                scales=xm_plane[:, first * P : last * P],
                in_=grouped[:],
            )

        def bank_tile(bank, width):
            return psum.tile([P, width], F32, name="grad", tag=f"bank{bank}")[:]

        def multiply(b, slots, grad):
            cols = slice(b * P, (b + 1) * P)
            nc.tensor.matmul_mx(
                out=grad,
                lhsT=xm_codes[:, cols].bitcast(E4M3),
                lhsT_scale=xm_plane[:, cols],
                rhs=g_codes[:, slots].bitcast(E5M2),
                rhs_scale=g_plane[:, slots],
                start=True,
                stop=True,
            )
            return grad

        def leave_psum_on_scalar(grad):
            dense = keep.tile([P, HALF], F32, name="scalar_dense", bufs=2, align_bytes=64)
            nc.scalar.copy(dense[:], grad)
            return dense[:]

        def leave_psum_on_vector(grad):
            dense = keep.tile([P, N], F32, name="vector_dense", align_bytes=64)
            nc.vector.tensor_copy(dense[:], grad)
            return dense[:]

        def cast_xm_on_gpsimd(first, last, grouped):
            nc.gpsimd.tensor_scalar(
                grouped[:].rearrange("p (d j) -> p d j", j=PACK),
                xm_rest[:, :, (first - 4) * P : (last - 4) * P].rearrange("p j d -> p d j"),
                1.0,
                0.0,
                ALU.mult,
                ALU.add,
            )

        def entries(slots):
            return offsets[:, slots.start // 16 : slots.stop // 16]

        def scatter_on_vector(b, slots, dense):
            nc.vector.tensor_copy(windows[b % WINDOWS][:].indirect(entries(slots)), dense)

        def scatter_on_scalar(b, slots, dense):
            nc.scalar.activation(windows[b % WINDOWS][:].indirect(entries(slots)), dense, ACT.Copy)

        def store(b):
            nc.sync.dma_start(out[b * P : (b + 1) * P, :], windows[b % WINDOWS][:])

        for t in range(2):
            weigh_y_on_scalar(t)
        for cols in pieces:
            exponentiate(0, cols)
        for t in range(2, PACK):
            weigh_y_on_vector(t)
        form_g(0, pieces[0])
        interleave_g(0, pieces[0])
        quantise_g(0, pieces[0])
        form_g(0, pieces[1])
        interleave_g(0, pieces[1])
        grouped = reused_tile("xm_grouped0", [P * PACK], BF16, 2)
        cast_xm(grouped[:], xm_first[:], nc.scalar.copy)
        quantise_xm(0, 1, grouped)
        quantise_g(0, pieces[1])
        probs.append(chain_tile("probs1", [PACK, HALF], F32, 4096))
        exponentiate(1, slice(0, HALF))
        dense = leave_psum_on_scalar(multiply(0, halves[0], bank_tile(0, HALF)))
        grouped = grouped_tile(1, 2, "x_pair10")
        cast_xm(grouped[:], xm_second[:, :, :P], nc.scalar.copy)
        scatter_on_scalar(0, halves[0], dense)

        g_rows.append(reused_tile("g_rows1", [PACK, HALF], BF16, 3))
        form_g(1, slice(0, HALF))
        quantise_xm(1, 2, grouped)
        first_half = leave_psum_on_scalar(multiply(1, halves[0], bank_tile(1, HALF)))
        interleave_g(1, slice(0, HALF))
        grouped = chain_tile("xm_grouped2", [2 * P * PACK], BF16, 6144)
        cast_xm(grouped[:, : P * PACK], xm_second[:, :, P : 2 * P], nc.vector.tensor_copy)
        quantise_g(1, slice(0, HALF))
        last_of_first = multiply(0, halves[1], bank_tile(2, HALF))

        cast_xm(grouped[:, P * PACK :], xm_second[:, :, 2 * P :], nc.vector.tensor_copy)
        early = reused_tile("early_dense", [HALF], F32, 3)
        nc.vector.tensor_copy(early[:], last_of_first)
        quantise_xm(2, 4, grouped)
        scatter_on_vector(0, halves[1], early[:])
        store(0)

        def shared_copies(b, bank):
            dense = keep.tile([P, 3, HALF], F32, name=f"shared_dense{b}", align_bytes=64)
            second_halves = bank_tile(bank, N)
            multiply(b, halves[1], second_halves[:, HALF:])
            multiply(b + 1, halves[1], second_halves[:, :HALF])
            nc.vector.tensor_copy(dense[:, 0, :], multiply(b + 1, halves[0], bank_tile(bank + 1, HALF)))
            nc.scalar.copy(dense[:, 1:, :].rearrange("p k s -> p (k s)"), second_halves)
            return dense[:, 2, :], dense[:, :2, :].rearrange("p k s -> p (k s)")

        def scalar_copies(b, bank):
            grad = multiply(b, whole, bank_tile(bank, N))
            return [leave_psum_on_scalar(grad[:, halves[h]]) for h in range(2)]

        def scalar_scatters(b, dense_halves):
            for h in range(2):
                scatter_on_scalar(b, halves[h], dense_halves[h])
            store(b)

        grouped = chain_tile("xm_grouped4", [P * PACK], BF16, 7168)
        cast_xm_on_gpsimd(4, 5, grouped)
        second_half, dense = shared_copies(1, 3)
        quantise_xm(4, 5, grouped)
        scalar_scatters(1, [first_half, second_half])
        scatter_on_vector(2, whole, dense)
        store(2)

        grouped = chain_tile("xm_grouped5", [3 * P * PACK], BF16, 7168)
        cast_xm_on_gpsimd(5, STRIPES, grouped)
        dense = leave_psum_on_vector(multiply(4, whole, bank_tile(6, N)))
        quantise_xm(5, STRIPES, grouped)
        scalar_scatters(3, scalar_copies(3, 5))
        scatter_on_vector(4, whole, dense)
        store(4)

        dense = leave_psum_on_vector(multiply(6, whole, bank_tile(1, N)))
        scalar_scatters(5, scalar_copies(5, 0))
        scatter_on_vector(6, whole, dense)
        store(6)
        scalar_scatters(7, scalar_copies(7, 2))
